import numpy as np
import ml_dtypes


def mxq(x, axis, fmt="e4m3"):
    dtype, down = {"e4m3": (ml_dtypes.float8_e4m3fn, 7), "e5m2": (ml_dtypes.float8_e5m2, 14)}[fmt]
    v = np.moveaxis(np.asarray(x, np.float32).astype(ml_dtypes.bfloat16).astype(np.float64), axis, -1)
    blocks = v.reshape(v.shape[:-1] + (-1, 32))
    amax = np.abs(blocks).max(-1, keepdims=True)
    byte = np.maximum(np.where(amax > 0, np.frexp(amax)[1] - 1 + 127, 0) - down, 1)
    scale = np.exp2(byte - 127.0)
    codes = (blocks / scale).astype(np.float32).astype(dtype).astype(np.float64)
    return np.moveaxis((codes * scale).reshape(v.shape), -1, axis)


WIDE = False


def mx_kscale(k):
    if not WIDE:
        return np.ones(k)
    levels = np.array([10, -10, 5, -5, 0])
    if k % 512:
        return np.exp2(np.random.permutation(np.resize(levels, k // 32))).repeat(32)
    a = np.empty((k // 512, 16))
    for p in range(k // 512):
        a[p, :8] = np.random.permutation(np.resize(levels, 8))
        for g in range(8):
            far = levels[np.abs(levels - a[p, g]) >= 10]
            a[p, g + 8] = far[np.random.randint(len(far))]
    return np.exp2(a.ravel()).repeat(32)


BF16 = ml_dtypes.bfloat16


def bf(x):
    return np.asarray(x, np.float32).astype(BF16)


def f64(x):
    return np.asarray(x).astype(np.float64)


E2M1 = np.array([0.0, 0.5, 1.0, 1.5, 2.0, 3.0, 4.0, 6.0, -0.0, -0.5, -1.0, -1.5, -2.0, -3.0, -4.0, -6.0])


def pack_weight(w, fmt):
    k, n = w.shape
    w = f64(bf(w)).reshape(k // 32, 32, n)
    amax = np.abs(w).max(1)
    if fmt == "e4m3":
        byte = np.frexp(amax)[1] - 1 + 127 - 7
    else:
        mant, ex = np.frexp(amax / 6.0)
        byte = np.where(mant > 0.5, ex, ex - 1) + 127
    byte = np.clip(np.where(amax > 0, byte, 1), 1, 254)
    scaled = (w * np.exp2(127.0 - byte)[:, None, :]).reshape(k, n).astype(np.float32)
    by_word = np.ascontiguousarray(scaled.reshape(k // 512, 128, 4, n).transpose(0, 1, 3, 2))
    if fmt == "e4m3":
        words = by_word.astype(ml_dtypes.float8_e4m3fn).view(np.uint8)
    else:
        c = by_word.astype(ml_dtypes.float4_e2m1fn).view(np.uint8) & 0xF
        words = c[..., 0::2] | (c[..., 1::2] << 4)
    return np.ascontiguousarray(words), np.ascontiguousarray(byte.astype(np.uint8).reshape(k // 512, 16, n))


def unpack_weight(words, scales, fmt):
    g, p, n, _ = words.shape
    if fmt == "e4m3":
        vals = np.ascontiguousarray(words).view(ml_dtypes.float8_e4m3fn).astype(np.float64)
    else:
        nib = np.empty((g, p, n, 4), np.uint8)
        nib[..., 0::2] = words & 0xF
        nib[..., 1::2] = words >> 4
        vals = E2M1[nib]
    vals = vals * np.repeat(np.exp2(scales.astype(np.float64) - 127.0), 8, axis=1)[..., None]
    return vals.transpose(0, 1, 3, 2).reshape(g * 512, n)
def pack4(w):
    words, scales = pack_weight(w, "e2m1")
    return words.reshape(words.shape[0], 128, -1), scales


def unpack4(words, scales):
    return unpack_weight(words.reshape(words.shape[0], 128, -1, 2), scales, "e2m1")


T, K, F1, F2, N, R = 1024, 1024, 1536, 1024, 512, 512


def draw0():
    s1, s2 = mx_kscale(K), mx_kscale(K)
    t1, t2 = mx_kscale(F1), mx_kscale(F2)
    u = mx_kscale(T)
    d1 = np.random.standard_normal((F1, N)) / np.sqrt(F1) / t1[:, None]
    d1_words, d1_scales = pack4(d1)
    return {"x1": bf(np.random.standard_normal((T, K)) * s1 * u[:, None]),
            "x2": bf(np.random.standard_normal((T, K)) * s2 * u[:, None]),
            "e1": bf(np.random.standard_normal((K, F1)) / np.sqrt(K) / s1[:, None] * t1),
            "e2": bf(np.random.standard_normal((K, F2)) / np.sqrt(K) / s2[:, None] * t2),
            "d1_words": d1_words,
            "d1_scales": d1_scales,
            "d2": bf(np.random.standard_normal((F2, N)) / np.sqrt(F2) / t2[:, None]),
            "labels": bf(np.random.standard_normal((T, R)) / np.sqrt(T) / u[:, None])}


def core(x1, x2, e1, e2, d1_words, d1_scales, d2, labels):
    a1 = np.maximum(mxq(f64(x1), 1, "e4m3") @ mxq(f64(e1), 0, "e4m3"), 0.0)
    a2 = np.maximum(mxq(f64(x2), 1, "e4m3") @ mxq(f64(e2), 0, "e4m3"), 0.0)
    d1 = unpack4(d1_words, d1_scales)
    y = (mxq(a1, 1, "e4m3") @ d1) + (mxq(a2, 1, "e4m3") @ mxq(f64(d2), 0, "e4m3"))
    lab = mxq(f64(labels), 0, "e4m3")
    c1 = mxq(a1, 0, "e4m3").T @ lab
    c2 = mxq(a2, 0, "e4m3").T @ lab
    return y, c1, c2


def e4m3fn_bytes(y):
    return np.clip(np.asarray(y, np.float64), -448.0, 448.0).astype(np.float32).astype(ml_dtypes.float8_e4m3fn).view(np.uint8)


def e4m3fn_values(b):
    return np.asarray(b, np.uint8).view(ml_dtypes.float8_e4m3fn).astype(np.float64)


def setup_inputs():
    d = draw0()
    x0 = np.asarray(d['labels']).astype(np.float64)
    s = (np.max(np.abs(x0), axis=(1,), keepdims=True) / 448.0).astype(np.float32)
    out = {}
    for k, v in d.items():
        if k == 'labels':
            out['labels_bytes'] = e4m3fn_bytes(x0 / s.astype(np.float64))
            out['labels_scale'] = s
        else:
            out[k] = v
    return out


def reference(x1, x2, e1, e2, d1_words, d1_scales, d2, labels_bytes, labels_scale):
    return core(x1, x2, e1, e2, d1_words, d1_scales, d2, e4m3fn_values(labels_bytes) * labels_scale.astype(np.float64))

@@ -1,0 +1,349 @@
+from contextlib import ExitStack
+
+import concourse.mybir as mybir
+from concourse.masks import make_identity
+
+F32 = mybir.dt.float32
+BF16 = mybir.dt.bfloat16
+U32 = mybir.dt.uint32
+I32 = mybir.dt.int32
+U8 = mybir.dt.uint8
+E4M3 = mybir.dt.float8_e4m3fn
+E4M3X4 = mybir.dt.float8_e4m3fn_x4
+E2M1X4 = mybir.dt.float4_e2m1fn_x4
+ACT = mybir.ActivationFunctionType
+ALU = mybir.AluOpType
+
+T, K, F1, F2, N, R = 1024, 1024, 1536, 1024, 512, 512
+P = 128
+FLOPS = 2 * (T * K * (F1 + F2) + T * (F1 + F2) * (N + R))
+NG = 5
+NU = 2 * NG
+SHARE = {}
+LABS = 2
+XR = 3
+ABUF = 5
+ACB = 6
+EB = 4
+ECB = 4
+MIXB = 3
+RV = 99
+WV = 99
+CV = 7
+PB = (3, 2, 3)
+YT = ['s1', 's1']
+LOADS = [('e0', 0), ('e0', 1), ('lab', 0), ('x', 0, 0, 0, 1), ('x', 0, 0, 3, 4), ('x', 0, 0, 1, 2), ('x', 0, 0, 2, 3), ('x', 0, 1, 0, 2), ('e', 1, 0), ('x', 0, 1, 2, 4), ('lab', 1), ('e', 1, 1), ('x', 1, 0, 0, 4), ('e', 3, 1), ('e', 3, 0), ('d2', 1), ('d2', 0), ('d',), ('x', 1, 1, 0, 4)]
+UNITS = [(0, 0), (0, 1), (1, 0), (1, 1), (2, 0), (2, 1), (3, 0), (4, 0), (3, 1), (4, 1)]
+PLAN = [('em', 0, 0), ('eq', 0, 0), ('em', 0, 1), ('eq', 0, 1), ('lw', 0), ('xt', 0, 0, 0), ('xq', 0, 0, 0), ('xt', 0, 0, 1), ('xq', 0, 0, 1), ('xt', 0, 0, 2), ('lm', 0), ('xq', 0, 0, 2), ('xt', 0, 0, 3), ('xq', 0, 0, 3), ('lq', 0), ('s1', 0, 0), ('em', 1, 0), ('s1', 0, 1), ('xt', 0, 1, 0), ('s1', 0, 2), ('xq', 0, 1, 0), ('xt', 0, 1, 1), ('s1', 0, 3), ('eq', 1, 0), ('xq', 0, 1, 1), ('am', 0), ('xt', 0, 1, 2), ('xq', 0, 1, 2), ('xt', 0, 1, 3), ('em', 1, 1), ('xq', 0, 1, 3), ('s1', 1, 0), ('eq', 1, 1), ('s1', 1, 1), ('tr', 0, 1), ('s1', 1, 2), ('tr', 0, 0), ('at', 0), ('em', 2, 0), ('lw', 1), ('s1', 1, 3), ('am', 1), ('ac', 0), ('eq', 2, 0), ('s1', 2, 0), ('em', 2, 1), ('lm', 1), ('s1', 2, 1), ('tr', 1, 1), ('s1', 2, 2), ('tr', 1, 0), ('at', 1), ('eq', 2, 1), ('xt', 1, 0, 0), ('s1', 2, 3), ('lq', 1), ('xq', 1, 0, 0), ('em', 3, 0), ('ac', 1), ('xt', 1, 0, 1), ('xq', 1, 0, 1), ('am', 2), ('xt', 1, 0, 2), ('s1', 3, 0), ('eq', 3, 0), ('xq', 1, 0, 2), ('s1', 3, 1), ('xt', 1, 0, 3), ('tr', 2, 1), ('em', 3, 1), ('s1', 3, 2), ('xq', 1, 0, 3), ('tr', 2, 0), ('at', 2), ('s1', 3, 3), ('eq', 3, 1), ('ac', 2), ('em', 4, 0), ('am', 3), ('s1', 4, 0), ('s1', 4, 1), ('eq', 4, 0), ('tr', 3, 1), ('s1', 4, 2), ('tr', 3, 0), ('at', 3), ('c', 0, 0), ('s1', 4, 3), ('em', 4, 1), ('c', 0, 1), ('ac', 3), ('eq', 4, 1), ('c', 0, 2), ('s1', 5, 0), ('am', 4), ('s1', 5, 1), ('c', 0, 3), ('tr', 4, 1), ('xt', 1, 1, 0), ('s1', 5, 2), ('tr', 4, 0), ('at', 4), ('xq', 1, 1, 0), ('s1', 5, 3), ('xt', 1, 1, 1), ('ac', 4), ('xq', 1, 1, 1), ('xt', 1, 1, 2), ('xq', 1, 1, 2), ('s1', 6, 0), ('xt', 1, 1, 3), ('s1', 6, 1), ('xq', 1, 1, 3), ('am', 5), ('s1', 6, 2), ('tr', 5, 1), ('tr', 5, 0), ('at', 5), ('s1', 6, 3), ('dm', 0), ('ac', 5), ('c', 1, 0), ('s1', 7, 0), ('c', 1, 1), ('dq', 0), ('dm', 1), ('s1', 7, 1), ('c', 1, 2), ('s1', 7, 2), ('tr', 6, 1), ('tr', 6, 0), ('at', 6), ('am', 6), ('s1', 7, 3), ('dq', 1), ('c', 1, 3), ('ac', 6), ('s1', 8, 0), ('s1', 8, 1), ('s1', 8, 2), ('tr', 7, 1), ('tr', 7, 0), ('at', 7), ('s1', 8, 3), ('am', 7), ('ac', 7), ('s1', 9, 0), ('s1', 9, 1), ('c', 2, 0), ('s1', 9, 2), ('tr', 8, 1), ('tr', 8, 0), ('at', 8), ('yp', 0, 0, 0, 4), ('c', 2, 1), ('s1', 9, 3), ('c', 2, 2), ('am', 8), ('ac', 8), ('yp', 0, 0, 4, 5), ('yo', 0, 0, 0), ('c', 2, 3), ('yp', 0, 1, 0, 4), ('tr', 9, 1), ('tr', 9, 0), ('at', 9), ('yp', 0, 1, 4, 5), ('yo', 0, 1, 1), ('yp', 0, 2, 0, 4), ('am', 9), ('ac', 9), ('yp', 0, 2, 4, 5), ('yo', 0, 2, 0), ('yp', 0, 3, 0, 4), ('c', 3, 0), ('yp', 0, 3, 4, 5), ('yo', 0, 3, 1), ('c', 3, 1), ('c', 3, 2), ('c', 3, 3), ('yp', 1, 0, 0, 4), ('yp', 1, 0, 4, 5), ('yo', 1, 0, 0), ('yp', 1, 1, 0, 4), ('c', 4, 0), ('yp', 1, 1, 4, 5), ('yo', 1, 1, 1), ('c', 4, 1), ('c', 4, 2), ('yp', 1, 2, 0, 4), ('c', 4, 3), ('yp', 1, 2, 4, 5), ('yo', 1, 2, 0), ('yp', 1, 3, 0, 4), ('yp', 1, 3, 4, 5), ('yo', 1, 3, 1)]
+
+
+def tile_cross_layer_transcoder_s8_kernel(
+    tc, x1, x2, e1, e2, d1_words, d1_scales, d2, labels_bytes, labels_scale, out_0, out_1, out_2
+):
+    nc = tc.nc
+    with ExitStack() as ctx:
+        keep = ctx.enter_context(tc.tile_pool(name="keep", bufs=1))
+        pool = ctx.enter_context(tc.tile_pool(name="work", bufs=1))
+        psum = ctx.enter_context(tc.psum_pool(name="psum", bufs=1))
+        ctx.enter_context(tc.manual_schedule())
+
+        def tile(shape, dtype, tag, bufs):
+            return pool.tile(shape, dtype, name=tag, tag=tag, bufs=bufs, align_bytes=64)
+
+        def bank(tag, bufs):
+            return psum.tile([P, 512], F32, name=tag, tag=tag, bufs=bufs)
+
+        ident = keep.tile([P, P], F32, name="ident", align_bytes=64)
+        make_identity(nc, ident[:])
+        warm = keep.tile([P, 1], F32, name="warm", align_bytes=64)
+        nc.gpsimd.memset(warm[:], 0.0)
+        nc.scalar.activation(out=warm[:], in_=warm[:], func=ACT.Relu)
+        d1_sc = keep.tile([P, 3, 512], U8, name="d1_sc", align_bytes=64)
+        nc.gpsimd.memset(d1_sc[:].rearrange("p g n -> p (g n)").bitcast(I32), 0)
+
+        x_raw = {}
+        e_raw = {}
+        xs = [x1, x2]
+
+        def load_x(s, g, parts):
+            t = tile([P, 4, K], BF16, "x_raw", XR)
+            view = xs[s].rearrange("(g p j) k -> g p j k", p=P, j=4)[g]
+            step = 4 // parts
+            for i in range(parts):
+                nc.sync.dma_start(out=t[:, i * step : (i + 1) * step, :], in_=view[:, i * step : (i + 1) * step, :])
+            x_raw[s, g] = t
+
+        def load_e(g0, q, width, tag, bufs, e, col):
+            t = tile([P, 4, width], BF16, tag, bufs)
+            nc.sync.dma_start(
+                out=t[:], in_=e.rearrange("(q p j) c -> q p j c", p=P, j=4)[q][:, :, col : col + width]
+            )
+            for i in range(width // 512):
+                e_raw[g0 + i, q] = t[:, :, i * 512 : (i + 1) * 512]
+
+        lab_sc = keep.tile([P, 2, 4], F32, name="lab_sc", align_bytes=64)
+        lab_raw = keep.tile([P, 2, 4, R], U8, name="lab_raw", align_bytes=64)
+        d1_w = keep.tile([P, 3, 1024], U8, name="d1_w", align_bytes=64)
+        d1_si = d1_scales.bitcast(I32)
+        d2_raw = {}
+        outs = {}
+
+        def ld_x(s, g, j0, j1):
+            if (s, g) not in x_raw:
+                x_raw[s, g] = tile([P, 4, K], BF16, "x_raw", XR)
+            view = xs[s].rearrange("(g p j) k -> g p j k", p=P, j=4)[g]
+            nc.sync.dma_start(out=x_raw[s, g][:, j0:j1, :], in_=view[:, j0:j1, :])
+
+        def ld_e0(q):
+            load_e(0, q, 512, "e_a", 2, e1, 0)
+
+        def ld_e(G, q):
+            if G == 1:
+                load_e(1, q, 1024, "e_b", EB, e1, 512)
+            else:
+                load_e(3, q, 1024, "e_b", EB, e2, 0)
+
+        def ld_lab(g):
+            if "sc" not in outs:
+                outs["sc"] = 1
+                nc.sync.dma_start(out=lab_sc[:], in_=labels_scale.rearrange("(g p j) o -> p g (j o)", p=P, j=4))
+            nc.sync.dma_start(
+                out=lab_raw[:, g, :, :], in_=labels_bytes.rearrange("(g p j) r -> g p j r", p=P, j=4)[g]
+            )
+
+        def ld_d():
+            nc.sync.dma_start(out=d1_w[:], in_=d1_words.rearrange("g p c -> p g c"))
+            for quad in range(4):
+                nc.sync.dma_start(
+                    out=d1_sc[32 * quad : 32 * quad + 4, :, :].rearrange("p g n -> p (g n)").bitcast(I32).rearrange(
+                        "p (g n) -> p g n", g=3
+                    ),
+                    in_=d1_si[:, 4 * quad : 4 * quad + 4, :].rearrange("g r n -> r g n"),
+                )
+
+        def ld_d2(g):
+            t = tile([P, 4, N], BF16, "e_a", 2)
+            nc.sync.dma_start(out=t[:], in_=d2.rearrange("(g p j) n -> g p j n", p=P, j=4)[g])
+            d2_raw[g] = t
+
+        LD = dict(x=ld_x, e0=ld_e0, e=ld_e, lab=ld_lab, d=ld_d, d2=ld_d2)
+        for op in LOADS:
+            LD[op[0]](*op[1:])
+
+        x_c, x_s, x_t = {}, {}, {}
+
+        def x_turn(s, g, j):
+            if (s, g) not in x_c:
+                x_c[s, g] = tile([P, 1024], U32, "x_c", 4)
+                x_s[s, g] = tile([P, 1024], U8, "x_s", 4)
+            tr = bank("tr", PB[1])
+            words = x_raw[s, g][:, j, :].bitcast(F32)
+            for q in range(2):
+                for u in range(2):
+                    i = 2 * q + u
+                    nc.tensor.transpose(
+                        tr[:, i * P : (i + 1) * P], words[:, 256 * q + u : 256 * (q + 1) : 2], ident[:]
+                    )
+            xt = tile([P, 1024], BF16, "x_t", 4)
+            nc.scalar.copy(
+                out=xt[:].bitcast(F32).rearrange("p (q t u) -> p q t u", q=2, u=2),
+                in_=tr[:].rearrange("p (q u t) -> p q t u", q=2, u=2),
+            )
+            x_t[s, g, j] = xt
+
+        def x_quant(s, g, j):
+            cols = slice(256 * j, 256 * (j + 1))
+            nc.vector.quantize_mx(
+                out=x_c[s, g][:, cols].bitcast(E4M3X4), scales=x_s[s, g][:, cols], in_=x_t[s, g, j][:]
+            )
+
+        def interleave(raw, share=0):
+            t = tile([P, 512, 4], BF16, "mix", MIXB)
+            src = raw.rearrange("p j c -> p c j")
+            cut = 512 - share
+            if share:
+                nc.scalar.copy(out=t[:, cut:, :], in_=src[:, cut:, :])
+            if cut:
+                nc.vector.tensor_copy(out=t[:, :cut, :], in_=src[:, :cut, :])
+            return t
+
+        def quant(codes, scales, src):
+            nc.vector.quantize_mx(out=codes.bitcast(E4M3X4), scales=scales, in_=src[:].rearrange("p c j -> p (c j)"))
+
+        e_c, e_s, e_m = {}, {}, {}
+
+        def e_mix(G, q):
+            if G not in e_c:
+                e_c[G] = tile([P, 2, 512], U32, "e_c", ECB)
+                e_s[G] = tile([P, 2, 512], U8, "e_s", ECB)
+            e_m[G, q] = interleave(e_raw[G, q], SHARE.get((G, q), 0))
+
+        def e_quant(G, q):
+            quant(e_c[G][:, q, :], e_s[G][:, q, :], e_m[G, q])
+
+        lab_c = keep.tile([P, 2, R], U32, name="lab_c", align_bytes=64)
+        lab_s = keep.tile([P, 2, R], U8, name="lab_s", align_bytes=64)
+        lab_b, lab_m = {}, {}
+
+        def lab_widen(g):
+            t = tile([P, 4, R], BF16, "mix", MIXB)
+            for j in range(4):
+                if j < LABS:
+                    nc.scalar.activation(
+                        out=t[:, j, :],
+                        in_=lab_raw[:, g, j, :].bitcast(E4M3),
+                        func=ACT.Copy,
+                        scale=lab_sc[:, g, j : j + 1],
+                    )
+                    continue
+                nc.vector.tensor_scalar(
+                    out=t[:, j, :],
+                    in0=lab_raw[:, g, j, :].bitcast(E4M3),
+                    scalar1=lab_sc[:, g, j : j + 1],
+                    scalar2=None,
+                    op0=ALU.mult,
+                )
+            lab_b[g] = t
+
+        def lab_mix(g):
+            lab_m[g] = interleave(lab_b[g][:])
+
+        def lab_quant(g):
+            quant(lab_c[:, g, :], lab_s[:, g, :], lab_m[g])
+
+        d2_c = keep.tile([P, 2, N], U32, name="d2_c", align_bytes=64)
+        d2_s = keep.tile([P, 2, N], U8, name="d2_s", align_bytes=64)
+        d2_m = {}
+
+        def d2_mix(g):
+            d2_m[g] = interleave(d2_raw[g][:])
+
+        def d2_quant(g):
+            quant(d2_c[:, g, :], d2_s[:, g, :], d2_m[g])
+
+        a_raw, a_m, a_t = {}, {}, {}
+        ac_c, ac_s, at_c, at_s = {}, {}, {}, {}
+
+        def stage1(n, j):
+            G, g = UNITS[n]
+            s = 0 if G < 3 else 1
+            if n not in a_raw:
+                a_raw[n] = tile([P, 4, 512], BF16, "a", ABUF)
+            a = a_raw[n]
+            acc = bank("s1", PB[0])
+            for q in range(2):
+                cols = slice(256 * j + 128 * q, 256 * j + 128 * (q + 1))
+                nc.tensor.matmul_mx(
+                    out=acc[:],
+                    lhsT=x_c[s, g][:, cols].bitcast(E4M3X4),
+                    lhsT_scale=x_s[s, g][:, cols],
+                    rhs=e_c[G][:, q, :].bitcast(E4M3X4),
+                    rhs_scale=e_s[G][:, q, :],
+                    start=(q == 0),
+                    stop=(q == 1),
+                )
+            out = a[:, j, :].rearrange("p (u m e) -> p u m e", u=2, e=2)
+            src = acc[:].rearrange("p (m u e) -> p u m e", u=2, e=2)
+            if n >= RV and j == 3:
+                nc.vector.tensor_scalar_max(out, src, 0.0)
+            else:
+                nc.scalar.activation(out=out, in_=src, func=ACT.Relu)
+
+        def a_turn(n, h):
+            if n not in a_t:
+                a_t[n] = tile([P, 512, 4], BF16, "a_t", 2)
+            words = a_raw[n][:].rearrange("p j f -> p (j f)").bitcast(F32)
+            out = a_t[n][:].rearrange("p t f -> p (t f)").bitcast(F32)
+            tr = bank("tr", PB[1])
+            for i in range(4):
+                col = 512 * h + 128 * i
+                nc.tensor.transpose(tr[:, i * P : (i + 1) * P], words[:, col : col + P], ident[:])
+            (nc.vector.tensor_copy if (n >= WV and h == 1) else nc.scalar.copy)(
+                out=out[:, 512 * h : 512 * (h + 1)].rearrange("p (j t u) -> p j t u", j=2, u=2),
+                in_=tr[:].rearrange("p (j u t) -> p j t u", j=2, u=2),
+            )
+
+        def a_mix(n):
+            t = tile([P, 512, 4], BF16, "a_m", 2)
+            src = a_raw[n][:].rearrange("p j (u m e) -> p u m e j", u=2, e=2)
+            dst = t[:].rearrange("p (m u e) j -> p u m e j", u=2, e=2)
+            for u in range(2):
+                nc.vector.tensor_copy(out=dst[:, u], in_=src[:, u])
+            a_m[n] = t
+
+        def ac_quant(n):
+            ac_c[n] = tile([P, 512], U32, "ac_c", ACB)
+            ac_s[n] = tile([P, 512], U8, "ac_s", ACB)
+            quant(ac_c[n][:], ac_s[n][:], a_m[n])
+
+        def at_quant(n):
+            at_c[n] = tile([P, 512], U32, "at_c", NU)
+            at_s[n] = tile([P, 512], U8, "at_s", NU)
+            quant(at_c[n][:], at_s[n][:], a_t[n])
+
+        def c_block(G, b):
+            half, i = divmod(b, 2)
+            if i == 0:
+                outs["c", G, half] = tile([P, 2, R], F32, "o", 4)
+            o = outs["c", G, half]
+            acc = bank("o", PB[2])
+            cols = slice(128 * b, 128 * (b + 1))
+            for g in range(2):
+                n = UNITS.index((G, g))
+                nc.tensor.matmul_mx(
+                    out=acc[:],
+                    lhsT=ac_c[n][:, cols].bitcast(E4M3X4),
+                    lhsT_scale=ac_s[n][:, cols],
+                    rhs=lab_c[:, g, :].bitcast(E4M3X4),
+                    rhs_scale=lab_s[:, g, :],
+                    start=(g == 0),
+                    stop=(g == 1),
+                )
+            if i == 1 and UNITS.index((G, 1)) >= CV:
+                nc.vector.tensor_copy(out=o[:, i, :], in_=acc[:])
+            else:
+                nc.scalar.copy(out=o[:, i, :], in_=acc[:])
+            if i == 1:
+                dst = out_1 if G < 3 else out_2
+                row = 512 * (G if G < 3 else G - 3) + 256 * half
+                nc.sync.dma_start(out=dst[row : row + 256, :].rearrange("(b p) r -> p b r", p=P), in_=o[:])
+
+        y_acc = {}
+
+        def y_pass(g, j, G0, G1):
+            if G0 == 0:
+                y_acc[g, j] = bank(YT[g], PB[0] if YT[g] == "s1" else PB[2])
+            cols = slice(128 * j, 128 * (j + 1))
+            for G in range(G0, G1):
+                n = UNITS.index((G, g))
+                if G < 3:
+                    rhs, rhs_scale = d1_w[:, G, :].bitcast(E2M1X4), d1_sc[:, G, :]
+                else:
+                    rhs, rhs_scale = d2_c[:, G - 3, :].bitcast(E4M3X4), d2_s[:, G - 3, :]
+                nc.tensor.matmul_mx(
+                    out=y_acc[g, j][:],
+                    lhsT=at_c[n][:, cols].bitcast(E4M3X4),
+                    lhsT_scale=at_s[n][:, cols],
+                    rhs=rhs,
+                    rhs_scale=rhs_scale,
+                    start=(G == 0),
+                    stop=(G == NG - 1),
+                )
+
+        def y_out(g, j, vec):
+            if j % 2 == 0:
+                outs[g] = tile([P, 2, N], F32, "o", 4)
+            o = outs[g]
+            (nc.vector.tensor_copy if vec else nc.scalar.copy)(out=o[:, j % 2, :], in_=y_acc[g, j][:])
+            if j % 2 == 1:
+                dst = out_0.rearrange("(g p j) n -> g p j n", p=P, j=4)[g]
+                nc.sync.dma_start(out=dst[:, j - 1 : j + 1, :], in_=o[:])
+
+        def do(op):
+            k, a = op[0], op[1:]
+            FN[k](*a)
+
+        FN = dict(xt=x_turn, xq=x_quant, em=e_mix, eq=e_quant, lw=lab_widen, lm=lab_mix, lq=lab_quant, dm=d2_mix, dq=d2_quant,
+                  s1=stage1, tr=a_turn, am=a_mix, ac=ac_quant, at=at_quant, c=c_block, yp=y_pass, yo=y_out)
+        for op in PLAN:
+            do(op)

@@ -1,3 +1,4 @@
+import math
 from contextlib import ExitStack
 
 import concourse.mybir as mybir
@@ -17,24 +18,13 @@ ALU = mybir.AluOpType
 T, K, F1, F2, N, R = 1024, 1024, 1536, 1024, 512, 512
 P = 128
 FLOPS = 2 * (T * K * (F1 + F2) + T * (F1 + F2) * (N + R))
-NG = 5
-NU = 2 * NG
-SHARE = {}
-LABS = 2
-XR = 3
-ABUF = 5
-ACB = 6
-EB = 4
-ECB = 4
-MIXB = 3
-RV = 99
-WV = 99
-CV = 7
-PB = (3, 2, 3)
-YT = ['s1', 's1']
-LOADS = [('e0', 0), ('e0', 1), ('lab', 0), ('x', 0, 0, 0, 1), ('x', 0, 0, 3, 4), ('x', 0, 0, 1, 2), ('x', 0, 0, 2, 3), ('x', 0, 1, 0, 2), ('e', 1, 0), ('x', 0, 1, 2, 4), ('lab', 1), ('e', 1, 1), ('x', 1, 0, 0, 4), ('e', 3, 1), ('e', 3, 0), ('d2', 1), ('d2', 0), ('d',), ('x', 1, 1, 0, 4)]
-UNITS = [(0, 0), (0, 1), (1, 0), (1, 1), (2, 0), (2, 1), (3, 0), (4, 0), (3, 1), (4, 1)]
-PLAN = [('em', 0, 0), ('eq', 0, 0), ('em', 0, 1), ('eq', 0, 1), ('lw', 0), ('xt', 0, 0, 0), ('xq', 0, 0, 0), ('xt', 0, 0, 1), ('xq', 0, 0, 1), ('xt', 0, 0, 2), ('lm', 0), ('xq', 0, 0, 2), ('xt', 0, 0, 3), ('xq', 0, 0, 3), ('lq', 0), ('s1', 0, 0), ('em', 1, 0), ('s1', 0, 1), ('xt', 0, 1, 0), ('s1', 0, 2), ('xq', 0, 1, 0), ('xt', 0, 1, 1), ('s1', 0, 3), ('eq', 1, 0), ('xq', 0, 1, 1), ('am', 0), ('xt', 0, 1, 2), ('xq', 0, 1, 2), ('xt', 0, 1, 3), ('em', 1, 1), ('xq', 0, 1, 3), ('s1', 1, 0), ('eq', 1, 1), ('s1', 1, 1), ('tr', 0, 1), ('s1', 1, 2), ('tr', 0, 0), ('at', 0), ('em', 2, 0), ('lw', 1), ('s1', 1, 3), ('am', 1), ('ac', 0), ('eq', 2, 0), ('s1', 2, 0), ('em', 2, 1), ('lm', 1), ('s1', 2, 1), ('tr', 1, 1), ('s1', 2, 2), ('tr', 1, 0), ('at', 1), ('eq', 2, 1), ('xt', 1, 0, 0), ('s1', 2, 3), ('lq', 1), ('xq', 1, 0, 0), ('em', 3, 0), ('ac', 1), ('xt', 1, 0, 1), ('xq', 1, 0, 1), ('am', 2), ('xt', 1, 0, 2), ('s1', 3, 0), ('eq', 3, 0), ('xq', 1, 0, 2), ('s1', 3, 1), ('xt', 1, 0, 3), ('tr', 2, 1), ('em', 3, 1), ('s1', 3, 2), ('xq', 1, 0, 3), ('tr', 2, 0), ('at', 2), ('s1', 3, 3), ('eq', 3, 1), ('ac', 2), ('em', 4, 0), ('am', 3), ('s1', 4, 0), ('s1', 4, 1), ('eq', 4, 0), ('tr', 3, 1), ('s1', 4, 2), ('tr', 3, 0), ('at', 3), ('c', 0, 0), ('s1', 4, 3), ('em', 4, 1), ('c', 0, 1), ('ac', 3), ('eq', 4, 1), ('c', 0, 2), ('s1', 5, 0), ('am', 4), ('s1', 5, 1), ('c', 0, 3), ('tr', 4, 1), ('xt', 1, 1, 0), ('s1', 5, 2), ('tr', 4, 0), ('at', 4), ('xq', 1, 1, 0), ('s1', 5, 3), ('xt', 1, 1, 1), ('ac', 4), ('xq', 1, 1, 1), ('xt', 1, 1, 2), ('xq', 1, 1, 2), ('s1', 6, 0), ('xt', 1, 1, 3), ('s1', 6, 1), ('xq', 1, 1, 3), ('am', 5), ('s1', 6, 2), ('tr', 5, 1), ('tr', 5, 0), ('at', 5), ('s1', 6, 3), ('dm', 0), ('ac', 5), ('c', 1, 0), ('s1', 7, 0), ('c', 1, 1), ('dq', 0), ('dm', 1), ('s1', 7, 1), ('c', 1, 2), ('s1', 7, 2), ('tr', 6, 1), ('tr', 6, 0), ('at', 6), ('am', 6), ('s1', 7, 3), ('dq', 1), ('c', 1, 3), ('ac', 6), ('s1', 8, 0), ('s1', 8, 1), ('s1', 8, 2), ('tr', 7, 1), ('tr', 7, 0), ('at', 7), ('s1', 8, 3), ('am', 7), ('ac', 7), ('s1', 9, 0), ('s1', 9, 1), ('c', 2, 0), ('s1', 9, 2), ('tr', 8, 1), ('tr', 8, 0), ('at', 8), ('yp', 0, 0, 0, 4), ('c', 2, 1), ('s1', 9, 3), ('c', 2, 2), ('am', 8), ('ac', 8), ('yp', 0, 0, 4, 5), ('yo', 0, 0, 0), ('c', 2, 3), ('yp', 0, 1, 0, 4), ('tr', 9, 1), ('tr', 9, 0), ('at', 9), ('yp', 0, 1, 4, 5), ('yo', 0, 1, 1), ('yp', 0, 2, 0, 4), ('am', 9), ('ac', 9), ('yp', 0, 2, 4, 5), ('yo', 0, 2, 0), ('yp', 0, 3, 0, 4), ('c', 3, 0), ('yp', 0, 3, 4, 5), ('yo', 0, 3, 1), ('c', 3, 1), ('c', 3, 2), ('c', 3, 3), ('yp', 1, 0, 0, 4), ('yp', 1, 0, 4, 5), ('yo', 1, 0, 0), ('yp', 1, 1, 0, 4), ('c', 4, 0), ('yp', 1, 1, 4, 5), ('yo', 1, 1, 1), ('c', 4, 1), ('c', 4, 2), ('yp', 1, 2, 0, 4), ('c', 4, 3), ('yp', 1, 2, 4, 5), ('yo', 1, 2, 0), ('yp', 1, 3, 0, 4), ('yp', 1, 3, 4, 5), ('yo', 1, 3, 1)]
+GROUPS = 5
+UNITS = [(G, g) for G in range(3) for g in range(2)] + [(G, g) for g in range(2) for G in (3, 4)]
+STEPS = 3
+HEAD_CUT = 336
+X2_FIRST = 2
+X2_DIV = 3
+V_OUT = 4
 
 
 def tile_cross_layer_transcoder_s8_kernel(
@@ -42,308 +32,283 @@ def tile_cross_layer_transcoder_s8_kernel(
 ):
     nc = tc.nc
     with ExitStack() as ctx:
-        keep = ctx.enter_context(tc.tile_pool(name="keep", bufs=1))
         pool = ctx.enter_context(tc.tile_pool(name="work", bufs=1))
         psum = ctx.enter_context(tc.psum_pool(name="psum", bufs=1))
         ctx.enter_context(tc.manual_schedule())
 
-        def tile(shape, dtype, tag, bufs):
+        def tile(shape, dtype, tag, bufs=1):
             return pool.tile(shape, dtype, name=tag, tag=tag, bufs=bufs, align_bytes=64)
 
-        def bank(tag, bufs):
-            return psum.tile([P, 512], F32, name=tag, tag=tag, bufs=bufs)
+        def bank():
+            return psum.tile([P, 512], F32, name="bank", tag="bank", bufs=8)
 
-        ident = keep.tile([P, P], F32, name="ident", align_bytes=64)
+        ident = tile([P, P], F32, "ident")
         make_identity(nc, ident[:])
-        warm = keep.tile([P, 1], F32, name="warm", align_bytes=64)
+        warm = tile([P, 1], F32, "warm")
         nc.gpsimd.memset(warm[:], 0.0)
         nc.scalar.activation(out=warm[:], in_=warm[:], func=ACT.Relu)
-        d1_sc = keep.tile([P, 3, 512], U8, name="d1_sc", align_bytes=64)
+        d1_sc = tile([P, 3, 512], U8, "d1_sc")
         nc.gpsimd.memset(d1_sc[:].rearrange("p g n -> p (g n)").bitcast(I32), 0)
 
-        x_raw = {}
-        e_raw = {}
-        xs = [x1, x2]
+        x_raw, rows, lab_raw = {}, {}, {}
 
-        def load_x(s, g, parts):
-            t = tile([P, 4, K], BF16, "x_raw", XR)
-            view = xs[s].rearrange("(g p j) k -> g p j k", p=P, j=4)[g]
-            step = 4 // parts
-            for i in range(parts):
-                nc.sync.dma_start(out=t[:, i * step : (i + 1) * step, :], in_=view[:, i * step : (i + 1) * step, :])
-            x_raw[s, g] = t
+        def load_x(s, g, j):
+            t = tile([P, K], BF16, "x_raw", 8)
+            nc.sync.dma_start(out=t[:], in_=(x1, x2)[s].rearrange("(g p j) k -> g p j k", p=P, j=4)[g][:, j, :])
+            x_raw[s, g, j] = t[:]
 
-        def load_e(g0, q, width, tag, bufs, e, col):
-            t = tile([P, 4, width], BF16, tag, bufs)
+        def load_labels(g):
+            lab_raw[g] = tile([P, 4 * R], U8, "lab_raw", 2)
+            nc.sync.dma_start(out=lab_raw[g][:], in_=labels_bytes.rearrange("(g p j) r -> g p (j r)", p=P, j=4)[g])
+
+        def load_rows(key, src, half, col):
+            t = tile([P, 4, 512], BF16, "rows", 6)
             nc.sync.dma_start(
-                out=t[:], in_=e.rearrange("(q p j) c -> q p j c", p=P, j=4)[q][:, :, col : col + width]
+                out=t[:], in_=src.rearrange("(h p j) c -> h p j c", p=P, j=4)[half][:, :, col : col + 512]
             )
-            for i in range(width // 512):
-                e_raw[g0 + i, q] = t[:, :, i * 512 : (i + 1) * 512]
+            rows[key, half] = t[:]
 
-        lab_sc = keep.tile([P, 2, 4], F32, name="lab_sc", align_bytes=64)
-        lab_raw = keep.tile([P, 2, 4, R], U8, name="lab_raw", align_bytes=64)
-        d1_w = keep.tile([P, 3, 1024], U8, name="d1_w", align_bytes=64)
-        d1_si = d1_scales.bitcast(I32)
-        d2_raw = {}
-        outs = {}
-
-        def ld_x(s, g, j0, j1):
-            if (s, g) not in x_raw:
-                x_raw[s, g] = tile([P, 4, K], BF16, "x_raw", XR)
-            view = xs[s].rearrange("(g p j) k -> g p j k", p=P, j=4)[g]
-            nc.sync.dma_start(out=x_raw[s, g][:, j0:j1, :], in_=view[:, j0:j1, :])
-
-        def ld_e0(q):
-            load_e(0, q, 512, "e_a", 2, e1, 0)
-
-        def ld_e(G, q):
-            if G == 1:
-                load_e(1, q, 1024, "e_b", EB, e1, 512)
+        def load_e(G, q):
+            if G < 3:
+                load_rows(G, e1, q, 512 * G)
             else:
-                load_e(3, q, 1024, "e_b", EB, e2, 0)
+                load_rows(G, e2, q, 512 * (G - 3))
 
-        def ld_lab(g):
-            if "sc" not in outs:
-                outs["sc"] = 1
-                nc.sync.dma_start(out=lab_sc[:], in_=labels_scale.rearrange("(g p j) o -> p g (j o)", p=P, j=4))
+        load_x(0, 0, 0)
+        load_e(0, 0)
+        load_e(0, 1)
+        for j in range(1, 4):
+            load_x(0, 0, j)
+        for j in range(4):
+            load_x(0, 1, j)
+        load_e(1, 0)
+        load_e(1, 1)
+        for g in range(2):
+            for j in range(4):
+                load_x(1, g, j)
+            load_e(2 + g, 0)
+            load_e(2 + g, 1)
+        load_e(4, 0)
+        load_e(4, 1)
+        load_rows("d2", d2, 0, 0)
+        load_rows("d2", d2, 1, 0)
+        lab_sc = tile([P, 2, 4], F32, "lab_sc")
+        nc.sync.dma_start(out=lab_sc[:], in_=labels_scale.rearrange("(g p j) o -> p g (j o)", p=P, j=4))
+        load_labels(0)
+        load_labels(1)
+        d1_w = tile([P, 3, 1024], U8, "d1_w")
+        nc.sync.dma_start(out=d1_w[:], in_=d1_words.rearrange("g p c -> p g c"))
+        d1_si = d1_scales.bitcast(I32)
+        d1_sv = d1_sc[:].rearrange("p g n -> p (g n)").bitcast(I32).rearrange("p (g n) -> p g n", g=3)
+        for quad in range(4):
             nc.sync.dma_start(
-                out=lab_raw[:, g, :, :], in_=labels_bytes.rearrange("(g p j) r -> g p j r", p=P, j=4)[g]
+                out=d1_sv[32 * quad : 32 * quad + 4, :, :],
+                in_=d1_si[:, 4 * quad : 4 * quad + 4, :].rearrange("g r n -> r g n"),
             )
 
-        def ld_d():
-            nc.sync.dma_start(out=d1_w[:], in_=d1_words.rearrange("g p c -> p g c"))
-            for quad in range(4):
-                nc.sync.dma_start(
-                    out=d1_sc[32 * quad : 32 * quad + 4, :, :].rearrange("p g n -> p (g n)").bitcast(I32).rearrange(
-                        "p (g n) -> p g n", g=3
-                    ),
-                    in_=d1_si[:, 4 * quad : 4 * quad + 4, :].rearrange("g r n -> r g n"),
-                )
-
-        def ld_d2(g):
-            t = tile([P, 4, N], BF16, "e_a", 2)
-            nc.sync.dma_start(out=t[:], in_=d2.rearrange("(g p j) n -> g p j n", p=P, j=4)[g])
-            d2_raw[g] = t
-
-        LD = dict(x=ld_x, e0=ld_e0, e=ld_e, lab=ld_lab, d=ld_d, d2=ld_d2)
-        for op in LOADS:
-            LD[op[0]](*op[1:])
-
-        x_c, x_s, x_t = {}, {}, {}
+        x_c, x_s, x_b, x_t = {}, {}, {}, {}
 
         def x_turn(s, g, j):
-            if (s, g) not in x_c:
-                x_c[s, g] = tile([P, 1024], U32, "x_c", 4)
-                x_s[s, g] = tile([P, 1024], U8, "x_s", 4)
-            tr = bank("tr", PB[1])
-            words = x_raw[s, g][:, j, :].bitcast(F32)
+            tr = bank()
+            words = x_raw[s, g, j].bitcast(F32)
             for q in range(2):
                 for u in range(2):
                     i = 2 * q + u
                     nc.tensor.transpose(
                         tr[:, i * P : (i + 1) * P], words[:, 256 * q + u : 256 * (q + 1) : 2], ident[:]
                     )
-            xt = tile([P, 1024], BF16, "x_t", 4)
-            nc.scalar.copy(
+            x_b[s, g, j] = tr
+
+        def x_out(s, g, j, copy):
+            xt = tile([P, 1024], BF16, "x_t", 6)
+            copy(
                 out=xt[:].bitcast(F32).rearrange("p (q t u) -> p q t u", q=2, u=2),
-                in_=tr[:].rearrange("p (q u t) -> p q t u", q=2, u=2),
+                in_=x_b[s, g, j][:].rearrange("p (q u t) -> p q t u", q=2, u=2),
             )
             x_t[s, g, j] = xt
 
         def x_quant(s, g, j):
-            cols = slice(256 * j, 256 * (j + 1))
+            x_c[s, g, j] = tile([P, 256], U32, "x_c", 16)
+            x_s[s, g, j] = tile([P, 256], U8, "x_s", 16)
+            nc.vector.quantize_mx(out=x_c[s, g, j][:].bitcast(E4M3X4), scales=x_s[s, g, j][:], in_=x_t[s, g, j][:])
+
+        mixed, codes, scales = {}, {}, {}
+
+        def mix(key, cut=512):
+            t = tile([P, 512, 4], BF16, "mix", 4)
+            dst = t[:].rearrange("p (c i) j -> p c j i", i=4)
+            src = rows[key].rearrange("p j (c i) -> p c j i", i=4)
+            nc.vector.tensor_copy(out=dst[:, : cut // 4], in_=src[:, : cut // 4])
+            if cut < 512:
+                nc.scalar.copy(out=dst[:, cut // 4 :], in_=src[:, cut // 4 :])
+            mixed[key] = t
+
+        def quant(key, tag, bufs):
+            codes[key] = tile([P, 512], U32, tag + "_c", bufs)
+            scales[key] = tile([P, 512], U8, tag + "_s", bufs)
             nc.vector.quantize_mx(
-                out=x_c[s, g][:, cols].bitcast(E4M3X4), scales=x_s[s, g][:, cols], in_=x_t[s, g, j][:]
+                out=codes[key][:].bitcast(E4M3X4), scales=scales[key][:], in_=mixed[key][:].rearrange("p c j -> p (c j)")
             )
 
-        def interleave(raw, share=0):
-            t = tile([P, 512, 4], BF16, "mix", MIXB)
-            src = raw.rearrange("p j c -> p c j")
-            cut = 512 - share
-            if share:
-                nc.scalar.copy(out=t[:, cut:, :], in_=src[:, cut:, :])
-            if cut:
-                nc.vector.tensor_copy(out=t[:, :cut, :], in_=src[:, :cut, :])
-            return t
-
-        def quant(codes, scales, src):
-            nc.vector.quantize_mx(out=codes.bitcast(E4M3X4), scales=scales, in_=src[:].rearrange("p c j -> p (c j)"))
-
-        e_c, e_s, e_m = {}, {}, {}
-
-        def e_mix(G, q):
-            if G not in e_c:
-                e_c[G] = tile([P, 2, 512], U32, "e_c", ECB)
-                e_s[G] = tile([P, 2, 512], U8, "e_s", ECB)
-            e_m[G, q] = interleave(e_raw[G, q], SHARE.get((G, q), 0))
-
-        def e_quant(G, q):
-            quant(e_c[G][:, q, :], e_s[G][:, q, :], e_m[G, q])
-
-        lab_c = keep.tile([P, 2, R], U32, name="lab_c", align_bytes=64)
-        lab_s = keep.tile([P, 2, R], U8, name="lab_s", align_bytes=64)
-        lab_b, lab_m = {}, {}
-
-        def lab_widen(g):
-            t = tile([P, 4, R], BF16, "mix", MIXB)
+        def widen(g):
+            t = tile([P, 4, R], BF16, "mix", 4)
             for j in range(4):
-                if j < LABS:
-                    nc.scalar.activation(
-                        out=t[:, j, :],
-                        in_=lab_raw[:, g, j, :].bitcast(E4M3),
-                        func=ACT.Copy,
-                        scale=lab_sc[:, g, j : j + 1],
-                    )
-                    continue
                 nc.vector.tensor_scalar(
                     out=t[:, j, :],
-                    in0=lab_raw[:, g, j, :].bitcast(E4M3),
+                    in0=lab_raw[g][:, j * R : (j + 1) * R].bitcast(E4M3),
                     scalar1=lab_sc[:, g, j : j + 1],
                     scalar2=None,
                     op0=ALU.mult,
                 )
-            lab_b[g] = t
+            rows["lab", g] = t[:]
 
-        def lab_mix(g):
-            lab_m[g] = interleave(lab_b[g][:])
-
-        def lab_quant(g):
-            quant(lab_c[:, g, :], lab_s[:, g, :], lab_m[g])
-
-        d2_c = keep.tile([P, 2, N], U32, name="d2_c", align_bytes=64)
-        d2_s = keep.tile([P, 2, N], U8, name="d2_s", align_bytes=64)
-        d2_m = {}
-
-        def d2_mix(g):
-            d2_m[g] = interleave(d2_raw[g][:])
-
-        def d2_quant(g):
-            quant(d2_c[:, g, :], d2_s[:, g, :], d2_m[g])
-
-        a_raw, a_m, a_t = {}, {}, {}
-        ac_c, ac_s, at_c, at_s = {}, {}, {}, {}
-
-        def stage1(n, j):
-            G, g = UNITS[n]
-            s = 0 if G < 3 else 1
-            if n not in a_raw:
-                a_raw[n] = tile([P, 4, 512], BF16, "a", ABUF)
-            a = a_raw[n]
-            acc = bank("s1", PB[0])
-            for q in range(2):
-                cols = slice(256 * j + 128 * q, 256 * j + 128 * (q + 1))
-                nc.tensor.matmul_mx(
-                    out=acc[:],
-                    lhsT=x_c[s, g][:, cols].bitcast(E4M3X4),
-                    lhsT_scale=x_s[s, g][:, cols],
-                    rhs=e_c[G][:, q, :].bitcast(E4M3X4),
-                    rhs_scale=e_s[G][:, q, :],
-                    start=(q == 0),
-                    stop=(q == 1),
-                )
-            out = a[:, j, :].rearrange("p (u m e) -> p u m e", u=2, e=2)
-            src = acc[:].rearrange("p (m u e) -> p u m e", u=2, e=2)
-            if n >= RV and j == 3:
-                nc.vector.tensor_scalar_max(out, src, 0.0)
-            else:
-                nc.scalar.activation(out=out, in_=src, func=ACT.Relu)
-
-        def a_turn(n, h):
-            if n not in a_t:
-                a_t[n] = tile([P, 512, 4], BF16, "a_t", 2)
-            words = a_raw[n][:].rearrange("p j f -> p (j f)").bitcast(F32)
-            out = a_t[n][:].rearrange("p t f -> p (t f)").bitcast(F32)
-            tr = bank("tr", PB[1])
-            for i in range(4):
-                col = 512 * h + 128 * i
-                nc.tensor.transpose(tr[:, i * P : (i + 1) * P], words[:, col : col + P], ident[:])
-            (nc.vector.tensor_copy if (n >= WV and h == 1) else nc.scalar.copy)(
-                out=out[:, 512 * h : 512 * (h + 1)].rearrange("p (j t u) -> p j t u", j=2, u=2),
-                in_=tr[:].rearrange("p (j u t) -> p j t u", j=2, u=2),
+        def mx(acc, lhs_c, lhs_s, rhs_c, rhs_s, first, last):
+            nc.tensor.matmul_mx(
+                out=acc, lhsT=lhs_c, lhsT_scale=lhs_s, rhs=rhs_c, rhs_scale=rhs_s, start=first, stop=last
             )
 
-        def a_mix(n):
-            t = tile([P, 512, 4], BF16, "a_m", 2)
-            src = a_raw[n][:].rearrange("p j (u m e) -> p u m e j", u=2, e=2)
-            dst = t[:].rearrange("p (m u e) j -> p u m e j", u=2, e=2)
-            for u in range(2):
-                nc.vector.tensor_copy(out=dst[:, u], in_=src[:, u])
-            a_m[n] = t
+        a_raw = {}
 
-        def ac_quant(n):
-            ac_c[n] = tile([P, 512], U32, "ac_c", ACB)
-            ac_s[n] = tile([P, 512], U8, "ac_s", ACB)
-            quant(ac_c[n][:], ac_s[n][:], a_m[n])
+        def stage1(unit, j):
+            G, g = unit
+            s = 0 if G < 3 else 1
+            if j == 0:
+                a_raw[unit] = tile([P, 4, 512], BF16, "a", 10)
+            acc = bank()
+            for q in range(2):
+                cols = slice(128 * q, 128 * (q + 1))
+                mx(acc[:], x_c[s, g, j][:, cols].bitcast(E4M3X4), x_s[s, g, j][:, cols],
+                   codes[G, q][:].bitcast(E4M3X4), scales[G, q][:], q == 0, q == 1)
+            nc.scalar.activation(
+                out=a_raw[unit][:, j, :].rearrange("p (u m e) -> p u m e", u=2, e=2),
+                in_=acc[:].rearrange("p (m u e) -> p u m e", u=2, e=2),
+                func=ACT.Relu,
+            )
 
-        def at_quant(n):
-            at_c[n] = tile([P, 512], U32, "at_c", NU)
-            at_s[n] = tile([P, 512], U8, "at_s", NU)
-            quant(at_c[n][:], at_s[n][:], a_t[n])
+        def a_turn(unit):
+            t = tile([P, 512, 4], BF16, "a_t", 4)
+            words = a_raw[unit][:].rearrange("p j f -> p (j f)").bitcast(F32)
+            dst = t[:].rearrange("p t f -> p (t f)").bitcast(F32)
+            for h in range(2):
+                tr = bank()
+                for i in range(4):
+                    col = 512 * h + 128 * i
+                    nc.tensor.transpose(tr[:, i * P : (i + 1) * P], words[:, col : col + P], ident[:])
+                nc.scalar.copy(
+                    out=dst[:, 512 * h : 512 * (h + 1)].rearrange("p (j t u) -> p j t u", j=2, u=2),
+                    in_=tr[:].rearrange("p (j u t) -> p j t u", j=2, u=2),
+                )
+            mixed["ay", unit] = t
 
-        def c_block(G, b):
-            half, i = divmod(b, 2)
-            if i == 0:
-                outs["c", G, half] = tile([P, 2, R], F32, "o", 4)
-            o = outs["c", G, half]
-            acc = bank("o", PB[2])
+        def a_mix(unit):
+            t = tile([P, 512, 4], BF16, "mix", 4)
+            nc.vector.tensor_copy(
+                out=t[:].rearrange("p (m u e) j -> p u m j e", u=2, e=2),
+                in_=a_raw[unit][:].rearrange("p j (u m e) -> p u m j e", u=2, e=2),
+            )
+            mixed["ac", unit] = t
+
+        def store(acc, dst, copy):
+            o = tile([P, 512], F32, "o", 6)
+            copy(out=o[:], in_=acc[:])
+            nc.sync.dma_start(out=dst, in_=o[:])
+
+        def c_block(G, b, copy):
+            acc = bank()
             cols = slice(128 * b, 128 * (b + 1))
             for g in range(2):
-                n = UNITS.index((G, g))
-                nc.tensor.matmul_mx(
-                    out=acc[:],
-                    lhsT=ac_c[n][:, cols].bitcast(E4M3X4),
-                    lhsT_scale=ac_s[n][:, cols],
-                    rhs=lab_c[:, g, :].bitcast(E4M3X4),
-                    rhs_scale=lab_s[:, g, :],
-                    start=(g == 0),
-                    stop=(g == 1),
-                )
-            if i == 1 and UNITS.index((G, 1)) >= CV:
-                nc.vector.tensor_copy(out=o[:, i, :], in_=acc[:])
-            else:
-                nc.scalar.copy(out=o[:, i, :], in_=acc[:])
-            if i == 1:
-                dst = out_1 if G < 3 else out_2
-                row = 512 * (G if G < 3 else G - 3) + 256 * half
-                nc.sync.dma_start(out=dst[row : row + 256, :].rearrange("(b p) r -> p b r", p=P), in_=o[:])
+                key = ("ac", (G, g))
+                mx(acc[:], codes[key][:, cols].bitcast(E4M3X4), scales[key][:, cols],
+                   codes["lab", g][:].bitcast(E4M3X4), scales["lab", g][:], g == 0, g == 1)
+            dst, row = (out_1, 512 * G + 128 * b) if G < 3 else (out_2, 512 * (G - 3) + 128 * b)
+            store(acc, dst[row : row + P, :], copy)
 
-        y_acc = {}
-
-        def y_pass(g, j, G0, G1):
-            if G0 == 0:
-                y_acc[g, j] = bank(YT[g], PB[0] if YT[g] == "s1" else PB[2])
+        def y_tile(g, j):
+            acc = bank()
             cols = slice(128 * j, 128 * (j + 1))
-            for G in range(G0, G1):
-                n = UNITS.index((G, g))
+            for G in range(GROUPS):
+                key = ("ay", (G, g))
                 if G < 3:
-                    rhs, rhs_scale = d1_w[:, G, :].bitcast(E2M1X4), d1_sc[:, G, :]
+                    rhs_c, rhs_s = d1_w[:, G, :].bitcast(E2M1X4), d1_sc[:, G, :]
                 else:
-                    rhs, rhs_scale = d2_c[:, G - 3, :].bitcast(E4M3X4), d2_s[:, G - 3, :]
-                nc.tensor.matmul_mx(
-                    out=y_acc[g, j][:],
-                    lhsT=at_c[n][:, cols].bitcast(E4M3X4),
-                    lhsT_scale=at_s[n][:, cols],
-                    rhs=rhs,
-                    rhs_scale=rhs_scale,
-                    start=(G == 0),
-                    stop=(G == NG - 1),
-                )
+                    rhs_c, rhs_s = codes["d2", G - 3][:].bitcast(E4M3X4), scales["d2", G - 3][:]
+                mx(acc[:], codes[key][:, cols].bitcast(E4M3X4), scales[key][:, cols], rhs_c, rhs_s,
+                   G == 0, G == GROUPS - 1)
+            store(acc, out_0.rearrange("(g p j) n -> g j p n", p=P, j=4)[g][j], nc.scalar.copy)
 
-        def y_out(g, j, vec):
-            if j % 2 == 0:
-                outs[g] = tile([P, 2, N], F32, "o", 4)
-            o = outs[g]
-            (nc.vector.tensor_copy if vec else nc.scalar.copy)(out=o[:, j % 2, :], in_=y_acc[g, j][:])
-            if j % 2 == 1:
-                dst = out_0.rearrange("(g p j) n -> g p j n", p=P, j=4)[g]
-                nc.sync.dma_start(out=dst[:, j - 1 : j + 1, :], in_=o[:])
+        def pair(keys, mixer, tag, bufs):
+            return [(mixer, (k,)) for k in keys] + [(quant, (k, tag, bufs)) for k in keys]
 
-        def do(op):
-            k, a = op[0], op[1:]
-            FN[k](*a)
+        background = []
+        for G in range(1, GROUPS):
+            background.extend(pair([(G, 0), (G, 1)], mix, "e", 6))
+        background.extend(pair([("d2", 0), ("d2", 1)], mix, "d2", 2))
+        background.extend([(widen, (0,)), (widen, (1,))] + pair([("lab", 0), ("lab", 1)], mix, "lab", 2))
+        for G in range(GROUPS):
+            background.extend([(a_mix, ((G, g),)) for g in range(2)])
+            background.extend([(quant, (("ac", (G, g)), "ac", 4)) for g in range(2)])
 
-        FN = dict(xt=x_turn, xq=x_quant, em=e_mix, eq=e_quant, lw=lab_widen, lm=lab_mix, lq=lab_quant, dm=d2_mix, dq=d2_quant,
-                  s1=stage1, tr=a_turn, am=a_mix, ac=ac_quant, at=at_quant, c=c_block, yp=y_pass, yo=y_out)
-        for op in PLAN:
-            do(op)
+        def steps(count):
+            for fn, args in background[:count]:
+                fn(*args)
+            background[:count] = []
+
+        def x_scalar(s, g, j):
+            x_turn(s, g, j)
+            x_out(s, g, j, nc.scalar.copy)
+
+        x_scalar(0, 0, 0)
+        mix((0, 0), HEAD_CUT)
+        x_quant(0, 0, 0)
+        quant((0, 0), "e", 6)
+        mix((0, 1), HEAD_CUT)
+        quant((0, 1), "e", 6)
+        for j in range(1, 4):
+            x_scalar(0, 0, j)
+            x_quant(0, 0, j)
+        for h in range(2):
+            stage1(UNITS[0], 2 * h)
+            stage1(UNITS[0], 2 * h + 1)
+            steps(1)
+            for j in (2 * h, 2 * h + 1):
+                x_scalar(0, 1, j)
+                x_quant(0, 1, j)
+
+        x2_tiles = [(1, g, j) for g in range(2) for j in range(4)]
+        last = len(UNITS) - 1
+        for n in range(1, len(UNITS)):
+            for j in range(4):
+                stage1(UNITS[n], j)
+            turned = [key for i, key in enumerate(x2_tiles) if X2_FIRST + (2 * i) // X2_DIV == n]
+            if n < last:
+                a_turn(UNITS[n - 1])
+            for key in turned:
+                x_turn(*key)
+                if key[2] % V_OUT != 0:
+                    x_out(*key, nc.scalar.copy)
+            steps(math.ceil(STEPS * n) - math.ceil(STEPS * (n - 1)))
+            for key in turned:
+                if key[2] % V_OUT == 0:
+                    x_out(*key, nc.vector.tensor_copy)
+            if n < last:
+                quant(("ay", UNITS[n - 1]), "ay", 10)
+            for key in turned:
+                x_quant(*key)
+
+        y_tile(0, 0)
+        y_tile(0, 1)
+        a_turn(UNITS[last - 1])
+        a_turn(UNITS[last])
+        y_tile(0, 2)
+        y_tile(0, 3)
+        left = len(background) % 4
+        steps(left)
+        quant(("ay", UNITS[last - 1]), "ay", 10)
+        quant(("ay", UNITS[last]), "ay", 10)
+        for G in range(GROUPS):
+            if len(background) > 4 * (GROUPS - 1 - G):
+                steps(4)
+            for b in range(4):
+                c_block(G, b, nc.vector.tensor_copy if G == GROUPS - 1 and b % 2 == 1 else nc.scalar.copy)
+            if G < GROUPS - 1:
+                y_tile(1, G)

@@ -44,9 +44,6 @@ def tile_cross_layer_transcoder_s8_kernel(
 
         ident = tile([P, P], F32, "ident")
         make_identity(nc, ident[:])
-        warm = tile([P, 1], F32, "warm")
-        nc.gpsimd.memset(warm[:], 0.0)
-        nc.scalar.activation(out=warm[:], in_=warm[:], func=ACT.Relu)
         d1_sc = tile([P, 3, 512], U8, "d1_sc")
         nc.gpsimd.memset(d1_sc[:].rearrange("p g n -> p (g n)").bitcast(I32), 0)
 

@@ -1,4 +1,3 @@
-import math
 from contextlib import ExitStack
 
 import concourse.mybir as mybir
@@ -20,17 +19,22 @@ P = 128
 FLOPS = 2 * (T * K * (F1 + F2) + T * (F1 + F2) * (N + R))
 GROUPS = 5
 UNITS = [(G, g) for G in range(3) for g in range(2)] + [(G, g) for g in range(2) for G in (3, 4)]
-STEPS = 3
-HEAD_CUT = 336
-X2_FIRST = 2
-X2_DIV = 3
-V_OUT = 4
+RUNS = (1, 3, 6, 8)
+X2_PER_UNIT = 2
+STEP_EVERY = 3
+OUT_DELAY = 2
+QUANT_DELAY = 4
+HEAD_CUT = (336, 384)
+SHARED = 7
+SHARE = 40
+WARM = (3, 1)
 
 
 def tile_cross_layer_transcoder_s8_kernel(
     tc, x1, x2, e1, e2, d1_words, d1_scales, d2, labels_bytes, labels_scale, out_0, out_1, out_2
 ):
     nc = tc.nc
+    scalar_copy, vector_copy = nc.scalar.copy, nc.vector.tensor_copy
     with ExitStack() as ctx:
         pool = ctx.enter_context(tc.tile_pool(name="work", bufs=1))
         psum = ctx.enter_context(tc.psum_pool(name="psum", bufs=1))
@@ -50,16 +54,12 @@ def tile_cross_layer_transcoder_s8_kernel(
         x_raw, rows, lab_raw = {}, {}, {}
 
         def load_x(s, g, j):
-            t = tile([P, K], BF16, "x_raw", 8)
+            t = tile([P, K], BF16, "x_raw", 7)
             nc.sync.dma_start(out=t[:], in_=(x1, x2)[s].rearrange("(g p j) k -> g p j k", p=P, j=4)[g][:, j, :])
             x_raw[s, g, j] = t[:]
 
-        def load_labels(g):
-            lab_raw[g] = tile([P, 4 * R], U8, "lab_raw", 2)
-            nc.sync.dma_start(out=lab_raw[g][:], in_=labels_bytes.rearrange("(g p j) r -> g p (j r)", p=P, j=4)[g])
-
         def load_rows(key, src, half, col):
-            t = tile([P, 4, 512], BF16, "rows", 6)
+            t = tile([P, 4, 512], BF16, "rows", 5)
             nc.sync.dma_start(
                 out=t[:], in_=src.rearrange("(h p j) c -> h p j c", p=P, j=4)[half][:, :, col : col + 512]
             )
@@ -71,28 +71,29 @@ def tile_cross_layer_transcoder_s8_kernel(
             else:
                 load_rows(G, e2, q, 512 * (G - 3))
 
-        load_x(0, 0, 0)
-        load_e(0, 0)
-        load_e(0, 1)
-        for j in range(1, 4):
-            load_x(0, 0, j)
-        for j in range(4):
-            load_x(0, 1, j)
+        for q in range(2):
+            load_x(0, 0, q)
+            load_e(0, q)
+        for g, j in [(0, 2), (0, 3), (1, 0), (1, 1), (1, 2), (1, 3)]:
+            load_x(0, g, j)
         load_e(1, 0)
         load_e(1, 1)
-        for g in range(2):
-            for j in range(4):
-                load_x(1, g, j)
-            load_e(2 + g, 0)
-            load_e(2 + g, 1)
+        for h in range(2):
+            load_x(1, 0, 2 * h)
+            load_x(1, 0, 2 * h + 1)
+            load_e(2 + h, 0)
+            load_e(2 + h, 1)
         load_e(4, 0)
         load_e(4, 1)
+        for j in range(4):
+            load_x(1, 1, j)
         load_rows("d2", d2, 0, 0)
         load_rows("d2", d2, 1, 0)
         lab_sc = tile([P, 2, 4], F32, "lab_sc")
         nc.sync.dma_start(out=lab_sc[:], in_=labels_scale.rearrange("(g p j) o -> p g (j o)", p=P, j=4))
-        load_labels(0)
-        load_labels(1)
+        for g in range(2):
+            lab_raw[g] = tile([P, 4 * R], U8, "lab_raw", 2)
+            nc.sync.dma_start(out=lab_raw[g][:], in_=labels_bytes.rearrange("(g p j) r -> g p (j r)", p=P, j=4)[g])
         d1_w = tile([P, 3, 1024], U8, "d1_w")
         nc.sync.dma_start(out=d1_w[:], in_=d1_words.rearrange("g p c -> p g c"))
         d1_si = d1_scales.bitcast(I32)
@@ -103,26 +104,34 @@ def tile_cross_layer_transcoder_s8_kernel(
                 in_=d1_si[:, 4 * quad : 4 * quad + 4, :].rearrange("g r n -> r g n"),
             )
 
-        x_c, x_s, x_b, x_t = {}, {}, {}, {}
+        x_c, x_s, x_b, x_t, x_w = {}, {}, {}, {}, {}
+
+        def x_sort(s, g, j):
+            t = tile([P, 512], F32, "x_t", 5)
+            vector_copy(
+                out=t[:].rearrange("p (q u m) -> p q u m", q=2, u=2),
+                in_=x_raw[s, g, j].bitcast(F32).rearrange("p (q m u) -> p q u m", q=2, u=2),
+            )
+            x_w[s, g, j] = t
 
         def x_turn(s, g, j):
-            tr = bank()
+            x_b[s, g, j] = bank()
             words = x_raw[s, g, j].bitcast(F32)
             for q in range(2):
                 for u in range(2):
                     i = 2 * q + u
-                    nc.tensor.transpose(
-                        tr[:, i * P : (i + 1) * P], words[:, 256 * q + u : 256 * (q + 1) : 2], ident[:]
-                    )
-            x_b[s, g, j] = tr
+                    if (s, g, j) in x_w:
+                        src = x_w[s, g, j][:, i * P : (i + 1) * P]
+                    else:
+                        src = words[:, 256 * q + u : 256 * (q + 1) : 2]
+                    nc.tensor.transpose(x_b[s, g, j][:, i * P : (i + 1) * P], src, ident[:])
 
         def x_out(s, g, j, copy):
-            xt = tile([P, 1024], BF16, "x_t", 6)
+            x_t[s, g, j] = tile([P, 1024], BF16, "x_t", 5)
             copy(
-                out=xt[:].bitcast(F32).rearrange("p (q t u) -> p q t u", q=2, u=2),
+                out=x_t[s, g, j][:].bitcast(F32).rearrange("p (q t u) -> p q t u", q=2, u=2),
                 in_=x_b[s, g, j][:].rearrange("p (q u t) -> p q t u", q=2, u=2),
             )
-            x_t[s, g, j] = xt
 
         def x_quant(s, g, j):
             x_c[s, g, j] = tile([P, 256], U32, "x_c", 16)
@@ -135,9 +144,9 @@ def tile_cross_layer_transcoder_s8_kernel(
             t = tile([P, 512, 4], BF16, "mix", 4)
             dst = t[:].rearrange("p (c i) j -> p c j i", i=4)
             src = rows[key].rearrange("p j (c i) -> p c j i", i=4)
-            nc.vector.tensor_copy(out=dst[:, : cut // 4], in_=src[:, : cut // 4])
+            vector_copy(out=dst[:, : cut // 4], in_=src[:, : cut // 4])
             if cut < 512:
-                nc.scalar.copy(out=dst[:, cut // 4 :], in_=src[:, cut // 4 :])
+                scalar_copy(out=dst[:, cut // 4 :], in_=src[:, cut // 4 :])
             mixed[key] = t
 
         def quant(key, tag, bufs):
@@ -146,6 +155,9 @@ def tile_cross_layer_transcoder_s8_kernel(
             nc.vector.quantize_mx(
                 out=codes[key][:].bitcast(E4M3X4), scales=scales[key][:], in_=mixed[key][:].rearrange("p c j -> p (c j)")
             )
+
+        def e_quant(G, q):
+            quant((G, q), "e", 6)
 
         def widen(g):
             t = tile([P, 4, R], BF16, "mix", 4)
@@ -159,51 +171,62 @@ def tile_cross_layer_transcoder_s8_kernel(
                 )
             rows["lab", g] = t[:]
 
-        def mx(acc, lhs_c, lhs_s, rhs_c, rhs_s, first, last):
+        def mx(acc, lhs_c, lhs_s, rhs_c, rhs_s, first, final):
             nc.tensor.matmul_mx(
-                out=acc, lhsT=lhs_c, lhsT_scale=lhs_s, rhs=rhs_c, rhs_scale=rhs_s, start=first, stop=last
+                out=acc, lhsT=lhs_c, lhsT_scale=lhs_s, rhs=rhs_c, rhs_scale=rhs_s, start=first, stop=final
             )
 
-        a_raw = {}
+        a_raw, a_acc, a_b = {}, {}, {}
+        shared = [(G, g) for G in range(GROUPS) for g in range(2)][:SHARED]
 
-        def stage1(unit, j):
+        def stage1(unit, j, passes=(0, 1)):
             G, g = unit
             s = 0 if G < 3 else 1
-            if j == 0:
+            if unit not in a_raw:
                 a_raw[unit] = tile([P, 4, 512], BF16, "a", 10)
-            acc = bank()
-            for q in range(2):
+            if 0 in passes:
+                a_acc[unit, j] = bank()
+            acc = a_acc[unit, j]
+            for q in passes:
                 cols = slice(128 * q, 128 * (q + 1))
                 mx(acc[:], x_c[s, g, j][:, cols].bitcast(E4M3X4), x_s[s, g, j][:, cols],
                    codes[G, q][:].bitcast(E4M3X4), scales[G, q][:], q == 0, q == 1)
-            nc.scalar.activation(
-                out=a_raw[unit][:, j, :].rearrange("p (u m e) -> p u m e", u=2, e=2),
-                in_=acc[:].rearrange("p (m u e) -> p u m e", u=2, e=2),
-                func=ACT.Relu,
+            if 1 in passes:
+                nc.scalar.activation(
+                    out=a_raw[unit][:, j, :].rearrange("p (u m e) -> p u m e", u=2, e=2),
+                    in_=acc[:].rearrange("p (m u e) -> p u m e", u=2, e=2),
+                    func=ACT.Relu,
+                )
+
+        def a_turn(unit, h):
+            if h == 0:
+                mixed["ay", unit] = tile([P, 512, 4], BF16, "a_t", 4)
+            words = a_raw[unit][:].rearrange("p j f -> p (j f)").bitcast(F32)
+            a_b[unit, h] = bank()
+            for i in range(4):
+                col = 512 * h + 128 * i
+                nc.tensor.transpose(a_b[unit, h][:, i * P : (i + 1) * P], words[:, col : col + P], ident[:])
+
+        def a_out(unit, h, copy):
+            dst = mixed["ay", unit][:].rearrange("p t f -> p (t f)").bitcast(F32)
+            copy(
+                out=dst[:, 512 * h : 512 * (h + 1)].rearrange("p (j t u) -> p j t u", j=2, u=2),
+                in_=a_b[unit, h][:].rearrange("p (j u t) -> p j t u", j=2, u=2),
             )
 
-        def a_turn(unit):
-            t = tile([P, 512, 4], BF16, "a_t", 4)
-            words = a_raw[unit][:].rearrange("p j f -> p (j f)").bitcast(F32)
-            dst = t[:].rearrange("p t f -> p (t f)").bitcast(F32)
-            for h in range(2):
-                tr = bank()
-                for i in range(4):
-                    col = 512 * h + 128 * i
-                    nc.tensor.transpose(tr[:, i * P : (i + 1) * P], words[:, col : col + P], ident[:])
-                nc.scalar.copy(
-                    out=dst[:, 512 * h : 512 * (h + 1)].rearrange("p (j t u) -> p j t u", j=2, u=2),
-                    in_=tr[:].rearrange("p (j u t) -> p j t u", j=2, u=2),
-                )
-            mixed["ay", unit] = t
+        def ay_quant(unit):
+            quant(("ay", unit), "ay", 10)
+
+        def a_part(unit, copy, quads):
+            if ("ac", unit) not in mixed:
+                mixed["ac", unit] = tile([P, 512, 4], BF16, "mix_shared" if unit in shared else "mix", 4)
+            copy(
+                out=mixed["ac", unit][:].rearrange("p (m u e) j -> p u m j e", u=2, e=2)[:, :, quads],
+                in_=a_raw[unit][:].rearrange("p j (u m e) -> p u m j e", u=2, e=2)[:, :, quads],
+            )
 
         def a_mix(unit):
-            t = tile([P, 512, 4], BF16, "mix", 4)
-            nc.vector.tensor_copy(
-                out=t[:].rearrange("p (m u e) j -> p u m j e", u=2, e=2),
-                in_=a_raw[unit][:].rearrange("p j (u m e) -> p u m j e", u=2, e=2),
-            )
-            mixed["ac", unit] = t
+            a_part(unit, vector_copy, slice(0, P - SHARE if unit in shared else P))
 
         def store(acc, dst, copy):
             o = tile([P, 512], F32, "o", 6)
@@ -221,6 +244,8 @@ def tile_cross_layer_transcoder_s8_kernel(
             store(acc, dst[row : row + P, :], copy)
 
         def y_tile(g, j):
+            if 4 * g + j < SHARED:
+                a_part(shared[4 * g + j], scalar_copy, slice(P - SHARE, P))
             acc = bank()
             cols = slice(128 * j, 128 * (j + 1))
             for G in range(GROUPS):
@@ -231,16 +256,16 @@ def tile_cross_layer_transcoder_s8_kernel(
                     rhs_c, rhs_s = codes["d2", G - 3][:].bitcast(E4M3X4), scales["d2", G - 3][:]
                 mx(acc[:], codes[key][:, cols].bitcast(E4M3X4), scales[key][:, cols], rhs_c, rhs_s,
                    G == 0, G == GROUPS - 1)
-            store(acc, out_0.rearrange("(g p j) n -> g j p n", p=P, j=4)[g][j], nc.scalar.copy)
+            store(acc, out_0.rearrange("(g p j) n -> g j p n", p=P, j=4)[g][j], scalar_copy)
 
-        def pair(keys, mixer, tag, bufs):
-            return [(mixer, (k,)) for k in keys] + [(quant, (k, tag, bufs)) for k in keys]
+        def pair(keys, tag, bufs):
+            return [(mix, (k,)) for k in keys] + [(quant, (k, tag, bufs)) for k in keys]
 
         background = []
-        for G in range(1, GROUPS):
-            background.extend(pair([(G, 0), (G, 1)], mix, "e", 6))
-        background.extend(pair([("d2", 0), ("d2", 1)], mix, "d2", 2))
-        background.extend([(widen, (0,)), (widen, (1,))] + pair([("lab", 0), ("lab", 1)], mix, "lab", 2))
+        for G in range(2, GROUPS):
+            background.extend(pair([(G, 0), (G, 1)], "e", 6))
+        background.extend(pair([("d2", 0), ("d2", 1)], "d2", 2))
+        background.extend([(widen, (0,)), (widen, (1,))] + pair([("lab", 0), ("lab", 1)], "lab", 2))
         for G in range(GROUPS):
             background.extend([(a_mix, ((G, g),)) for g in range(2)])
             background.extend([(quant, (("ac", (G, g)), "ac", 4)) for g in range(2)])
@@ -250,62 +275,116 @@ def tile_cross_layer_transcoder_s8_kernel(
                 fn(*args)
             background[:count] = []
 
-        def x_scalar(s, g, j):
-            x_turn(s, g, j)
-            x_out(s, g, j, nc.scalar.copy)
+        def warm_up(count):
+            for i in range(count):
+                unread = bank()
+                first = x_raw[0, 0, 0]
+                nc.tensor.matmul(unread[:], lhsT=first[:, :P], rhs=first[:, :512], start=True, stop=True)
 
-        x_scalar(0, 0, 0)
-        mix((0, 0), HEAD_CUT)
+        def x_turn_out(s, g, j):
+            x_turn(s, g, j)
+            x_out(s, g, j, scalar_copy)
+
+        x_turn(0, 0, 0)
+        warm_up(WARM[0])
+        mix((0, 0), HEAD_CUT[0])
+        x_out(0, 0, 0, scalar_copy)
+        e_quant(0, 0)
+        x_turn(0, 0, 1)
+        warm_up(WARM[1])
         x_quant(0, 0, 0)
-        quant((0, 0), "e", 6)
-        mix((0, 1), HEAD_CUT)
-        quant((0, 1), "e", 6)
-        for j in range(1, 4):
-            x_scalar(0, 0, j)
-            x_quant(0, 0, j)
+        mix((0, 1), HEAD_CUT[1])
+        x_out(0, 0, 1, scalar_copy)
+        e_quant(0, 1)
+        x_quant(0, 0, 1)
+        stage1(UNITS[0], 0, (0,))
+        x_turn_out(0, 0, 2)
+        x_turn_out(0, 0, 3)
+        stage1(UNITS[0], 0, (1,))
+        stage1(UNITS[0], 1)
         for h in range(2):
-            stage1(UNITS[0], 2 * h)
-            stage1(UNITS[0], 2 * h + 1)
-            steps(1)
-            for j in (2 * h, 2 * h + 1):
-                x_scalar(0, 1, j)
-                x_quant(0, 1, j)
+            x_sort(0, 1, 2 * h)
+            x_sort(0, 1, 2 * h + 1)
+            if h == 0:
+                x_quant(0, 0, 2)
+                x_quant(0, 0, 3)
+        x_turn_out(0, 1, 0)
+        x_turn_out(0, 1, 1)
+        mix((1, 0))
+        x_quant(0, 1, 0)
+        x_quant(0, 1, 1)
+        e_quant(1, 0)
+        stage1(UNITS[0], 2)
+        stage1(UNITS[0], 3)
+        x_turn_out(0, 1, 2)
+        x_turn_out(0, 1, 3)
+        x_quant(0, 1, 2)
+        x_quant(0, 1, 3)
+        mix((1, 1))
+        e_quant(1, 1)
+
+        due = []
+        filled = []
+
+        def later(delay, fn, *args):
+            due.append((len(filled) + delay, fn, args))
+
+        def flush(upto):
+            for item in [d for d in due if d[0] <= upto]:
+                due.remove(item)
+                item[1](*item[2])
+
+        def tick(step):
+            filled.append(1)
+            flush(len(filled))
+            if step and len(filled) % STEP_EVERY == 1:
+                steps(1)
 
         x2_tiles = [(1, g, j) for g in range(2) for j in range(4)]
         last = len(UNITS) - 1
+        turned = 0
         for n in range(1, len(UNITS)):
             for j in range(4):
                 stage1(UNITS[n], j)
-            turned = [key for i, key in enumerate(x2_tiles) if X2_FIRST + (2 * i) // X2_DIV == n]
-            if n < last:
-                a_turn(UNITS[n - 1])
-            for key in turned:
-                x_turn(*key)
-                if key[2] % V_OUT != 0:
-                    x_out(*key, nc.scalar.copy)
-            steps(math.ceil(STEPS * n) - math.ceil(STEPS * (n - 1)))
-            for key in turned:
-                if key[2] % V_OUT == 0:
-                    x_out(*key, nc.vector.tensor_copy)
-            if n < last:
-                quant(("ay", UNITS[n - 1]), "ay", 10)
-            for key in turned:
-                x_quant(*key)
+                tick(n < last)
+            if n in RUNS:
+                banks = []
+                for unit in UNITS[turned:n]:
+                    banks.append((a_turn, a_out, (unit, 0), None))
+                    banks.append((a_turn, a_out, (unit, 1), (ay_quant, unit)))
+                    banks.extend([(x_turn, x_out, key, (x_quant, *key)) for key in x2_tiles[:X2_PER_UNIT]])
+                    x2_tiles[:X2_PER_UNIT] = []
+                turned = n
+                for i, (turn, empty, args, then) in enumerate(banks):
+                    turn(*args)
+                    if i < len(banks) - 1:
+                        empty(*args, scalar_copy)
+                    else:
+                        later(OUT_DELAY, empty, *args, vector_copy)
+                    if then:
+                        later(QUANT_DELAY, *then)
+                    tick(n < last - 1)
+        flush(len(filled) + QUANT_DELAY)
+
+        def c_group(G):
+            steps(len(background) - 4 * (GROUPS - 1 - G))
+            for b in range(4):
+                c_block(G, b, vector_copy if G == GROUPS - 1 and b % 2 == 1 else scalar_copy)
 
         y_tile(0, 0)
         y_tile(0, 1)
-        a_turn(UNITS[last - 1])
-        a_turn(UNITS[last])
+        for unit in UNITS[last - 1 :]:
+            for h in range(2):
+                a_turn(unit, h)
+                a_out(unit, h, scalar_copy)
+        steps(len(background) - 4 * GROUPS + 2)
+        ay_quant(UNITS[last - 1])
+        ay_quant(UNITS[last])
         y_tile(0, 2)
         y_tile(0, 3)
-        left = len(background) % 4
-        steps(left)
-        quant(("ay", UNITS[last - 1]), "ay", 10)
-        quant(("ay", UNITS[last]), "ay", 10)
-        for G in range(GROUPS):
-            if len(background) > 4 * (GROUPS - 1 - G):
-                steps(4)
-            for b in range(4):
-                c_block(G, b, nc.vector.tensor_copy if G == GROUPS - 1 and b % 2 == 1 else nc.scalar.copy)
-            if G < GROUPS - 1:
-                y_tile(1, G)
+        for G in range(3):
+            y_tile(1, G)
+            c_group(G)
+        c_group(3)
+        y_tile(1, 3)
+        c_group(4)

@@ -20,13 +20,13 @@ FLOPS = 2 * (T * K * (F1 + F2) + T * (F1 + F2) * (N + R))
 GROUPS = 5
 UNITS = [(G, g) for G in range(3) for g in range(2)] + [(G, g) for g in range(2) for G in (3, 4)]
 RUNS = (1, 3, 6, 8)
-X2_PER_UNIT = 2
+X2_PER_RUN = 3
 STEP_EVERY = 3
-OUT_DELAY = 2
+OUT_DELAY = 1
 QUANT_DELAY = 4
-HEAD_CUT = (336, 384)
+HEAD_CUT = (336, 352)
 SHARED = 7
-SHARE = 40
+SHARE = 32
 WARM = (3, 1)
 
 
@@ -78,15 +78,12 @@ def tile_cross_layer_transcoder_s8_kernel(
             load_x(0, g, j)
         load_e(1, 0)
         load_e(1, 1)
-        for h in range(2):
-            load_x(1, 0, 2 * h)
-            load_x(1, 0, 2 * h + 1)
-            load_e(2 + h, 0)
-            load_e(2 + h, 1)
-        load_e(4, 0)
-        load_e(4, 1)
-        for j in range(4):
-            load_x(1, 1, j)
+        x2_tiles = [(1, g, j) for g in range(2) for j in range(4)]
+        for G in range(2, GROUPS):
+            for key in x2_tiles[X2_PER_RUN * (G - 2) : X2_PER_RUN * (G - 1)]:
+                load_x(*key)
+            load_e(G, 0)
+            load_e(G, 1)
         load_rows("d2", d2, 0, 0)
         load_rows("d2", d2, 1, 0)
         lab_sc = tile([P, 2, 4], F32, "lab_sc")
@@ -217,6 +214,17 @@ def tile_cross_layer_transcoder_s8_kernel(
         def ay_quant(unit):
             quant(("ay", unit), "ay", 10)
 
+        def ac_quant(unit, cols=slice(0, 512)):
+            key = ("ac", unit)
+            if key not in codes:
+                codes[key] = tile([P, 512], U32, "ac_c", 4)
+                scales[key] = tile([P, 512], U8, "ac_s", 4)
+            nc.vector.quantize_mx(
+                out=codes[key][:, cols].bitcast(E4M3X4),
+                scales=scales[key][:, cols],
+                in_=mixed[key][:, cols, :].rearrange("p c j -> p (c j)"),
+            )
+
         def a_part(unit, copy, quads):
             if ("ac", unit) not in mixed:
                 mixed["ac", unit] = tile([P, 512, 4], BF16, "mix_shared" if unit in shared else "mix", 4)
@@ -229,9 +237,9 @@ def tile_cross_layer_transcoder_s8_kernel(
             a_part(unit, vector_copy, slice(0, P - SHARE if unit in shared else P))
 
         def store(acc, dst, copy):
-            o = tile([P, 512], F32, "o", 6)
-            copy(out=o[:], in_=acc[:])
-            nc.sync.dma_start(out=dst, in_=o[:])
+            o = tile([P, 512], F32, "o", 6)[:, : acc.shape[1]]
+            copy(out=o, in_=acc)
+            nc.sync.dma_start(out=dst, in_=o)
 
         def c_block(G, b, copy):
             acc = bank()
@@ -241,22 +249,22 @@ def tile_cross_layer_transcoder_s8_kernel(
                 mx(acc[:], codes[key][:, cols].bitcast(E4M3X4), scales[key][:, cols],
                    codes["lab", g][:].bitcast(E4M3X4), scales["lab", g][:], g == 0, g == 1)
             dst, row = (out_1, 512 * G + 128 * b) if G < 3 else (out_2, 512 * (G - 3) + 128 * b)
-            store(acc, dst[row : row + P, :], copy)
+            store(acc[:], dst[row : row + P, :], copy)
 
-        def y_tile(g, j):
+        def y_tile(g, j, n=slice(0, N)):
             if 4 * g + j < SHARED:
                 a_part(shared[4 * g + j], scalar_copy, slice(P - SHARE, P))
-            acc = bank()
+            acc = bank()[:, : n.stop - n.start]
             cols = slice(128 * j, 128 * (j + 1))
             for G in range(GROUPS):
                 key = ("ay", (G, g))
                 if G < 3:
-                    rhs_c, rhs_s = d1_w[:, G, :].bitcast(E2M1X4), d1_sc[:, G, :]
+                    rhs_c, rhs_s = d1_w[:, G, 2 * n.start : 2 * n.stop].bitcast(E2M1X4), d1_sc[:, G, n]
                 else:
-                    rhs_c, rhs_s = codes["d2", G - 3][:].bitcast(E4M3X4), scales["d2", G - 3][:]
-                mx(acc[:], codes[key][:, cols].bitcast(E4M3X4), scales[key][:, cols], rhs_c, rhs_s,
+                    rhs_c, rhs_s = codes["d2", G - 3][:, n].bitcast(E4M3X4), scales["d2", G - 3][:, n]
+                mx(acc, codes[key][:, cols].bitcast(E4M3X4), scales[key][:, cols], rhs_c, rhs_s,
                    G == 0, G == GROUPS - 1)
-            store(acc, out_0.rearrange("(g p j) n -> g j p n", p=P, j=4)[g][j], scalar_copy)
+            store(acc, out_0.rearrange("(g p j) n -> g j p n", p=P, j=4)[g][j][:, n], scalar_copy)
 
         def pair(keys, tag, bufs):
             return [(mix, (k,)) for k in keys] + [(quant, (k, tag, bufs)) for k in keys]
@@ -266,9 +274,9 @@ def tile_cross_layer_transcoder_s8_kernel(
             background.extend(pair([(G, 0), (G, 1)], "e", 6))
         background.extend(pair([("d2", 0), ("d2", 1)], "d2", 2))
         background.extend([(widen, (0,)), (widen, (1,))] + pair([("lab", 0), ("lab", 1)], "lab", 2))
-        for G in range(GROUPS):
+        for G in range(GROUPS - 1):
             background.extend([(a_mix, ((G, g),)) for g in range(2)])
-            background.extend([(quant, (("ac", (G, g)), "ac", 4)) for g in range(2)])
+            background.extend([(ac_quant, ((G, g),)) for g in range(2)])
 
         def steps(count):
             for fn, args in background[:count]:
@@ -310,16 +318,16 @@ def tile_cross_layer_transcoder_s8_kernel(
                 x_quant(0, 0, 3)
         x_turn_out(0, 1, 0)
         x_turn_out(0, 1, 1)
-        mix((1, 0))
         x_quant(0, 1, 0)
         x_quant(0, 1, 1)
-        e_quant(1, 0)
+        mix((1, 0))
         stage1(UNITS[0], 2)
         stage1(UNITS[0], 3)
         x_turn_out(0, 1, 2)
         x_turn_out(0, 1, 3)
         x_quant(0, 1, 2)
         x_quant(0, 1, 3)
+        e_quant(1, 0)
         mix((1, 1))
         e_quant(1, 1)
 
@@ -340,7 +348,6 @@ def tile_cross_layer_transcoder_s8_kernel(
             if step and len(filled) % STEP_EVERY == 1:
                 steps(1)
 
-        x2_tiles = [(1, g, j) for g in range(2) for j in range(4)]
         last = len(UNITS) - 1
         turned = 0
         for n in range(1, len(UNITS)):
@@ -348,43 +355,55 @@ def tile_cross_layer_transcoder_s8_kernel(
                 stage1(UNITS[n], j)
                 tick(n < last)
             if n in RUNS:
-                banks = []
-                for unit in UNITS[turned:n]:
-                    banks.append((a_turn, a_out, (unit, 0), None))
-                    banks.append((a_turn, a_out, (unit, 1), (ay_quant, unit)))
-                    banks.extend([(x_turn, x_out, key, (x_quant, *key)) for key in x2_tiles[:X2_PER_UNIT]])
-                    x2_tiles[:X2_PER_UNIT] = []
+                x_now, a_now = x2_tiles[:X2_PER_RUN], UNITS[turned:n]
+                x2_tiles[:X2_PER_RUN] = []
                 turned = n
+                banks = []
+                for i in range(3):
+                    for key in x_now[i : i + 1]:
+                        banks.append((x_turn, x_out, key, (x_quant, *key)))
+                    for unit in a_now[i : i + 1]:
+                        banks.append((a_turn, a_out, (unit, 0), None))
+                        banks.append((a_turn, a_out, (unit, 1), (ay_quant, unit)))
+                on_vector = (0, 1) if n == RUNS[-1] else (len(banks) - 1,)
                 for i, (turn, empty, args, then) in enumerate(banks):
                     turn(*args)
-                    if i < len(banks) - 1:
-                        empty(*args, scalar_copy)
-                    else:
+                    if i in on_vector:
                         later(OUT_DELAY, empty, *args, vector_copy)
+                    else:
+                        empty(*args, scalar_copy)
                     if then:
                         later(QUANT_DELAY, *then)
-                    tick(n < last - 1)
+                    tick(n < RUNS[-1])
         flush(len(filled) + QUANT_DELAY)
 
         def c_group(G):
-            steps(len(background) - 4 * (GROUPS - 1 - G))
+            steps(len(background) - 4 * (GROUPS - 2 - G))
             for b in range(4):
-                c_block(G, b, vector_copy if G == GROUPS - 1 and b % 2 == 1 else scalar_copy)
+                c_block(G, b, scalar_copy)
 
         y_tile(0, 0)
         y_tile(0, 1)
-        for unit in UNITS[last - 1 :]:
+        for unit in UNITS[turned:]:
             for h in range(2):
                 a_turn(unit, h)
                 a_out(unit, h, scalar_copy)
-        steps(len(background) - 4 * GROUPS + 2)
-        ay_quant(UNITS[last - 1])
-        ay_quant(UNITS[last])
+        steps(len(background) - 4 * (GROUPS - 1) + 2)
+        for unit in UNITS[turned:]:
+            ay_quant(unit)
         y_tile(0, 2)
         y_tile(0, 3)
         for G in range(3):
             y_tile(1, G)
             c_group(G)
         c_group(3)
-        y_tile(1, 3)
-        c_group(4)
+        y_tile(1, 3, slice(0, N // 2))
+        G = GROUPS - 1
+        for h in range(2):
+            for g in range(2):
+                a_part((G, g), vector_copy, slice(64 * h, 64 * (h + 1)))
+            for g in range(2):
+                ac_quant((G, g), slice(256 * h, 256 * (h + 1)))
+            c_block(G, 2 * h, scalar_copy)
+            c_block(G, 2 * h + 1, vector_copy if h == 1 else scalar_copy)
+        y_tile(1, 3, slice(N // 2, N))

@@ -24,10 +24,10 @@ X2_PER_RUN = 3
 STEP_EVERY = 3
 OUT_DELAY = 1
 QUANT_DELAY = 4
-HEAD_CUT = (336, 352)
+HEAD_CUT = 352
 SHARED = 7
 SHARE = 32
-WARM = (3, 1)
+WARM = (2, 1)
 
 
 def tile_cross_layer_transcoder_s8_kernel(
@@ -236,8 +236,11 @@ def tile_cross_layer_transcoder_s8_kernel(
         def a_mix(unit):
             a_part(unit, vector_copy, slice(0, P - SHARE if unit in shared else P))
 
+        stored = []
+
         def store(acc, dst, copy):
-            o = tile([P, 512], F32, "o", 6)[:, : acc.shape[1]]
+            stored.append(dst)
+            o = tile([P, 512], F32, *[("x_raw", 7), ("x_t", 5)][len(stored) % 2])[:, : acc.shape[1]]
             copy(out=o, in_=acc)
             nc.sync.dma_start(out=dst, in_=o)
 
@@ -295,16 +298,16 @@ def tile_cross_layer_transcoder_s8_kernel(
 
         x_turn(0, 0, 0)
         warm_up(WARM[0])
-        mix((0, 0), HEAD_CUT[0])
         x_out(0, 0, 0, scalar_copy)
+        mix((0, 0), HEAD_CUT)
+        x_quant(0, 0, 0)
         e_quant(0, 0)
         x_turn(0, 0, 1)
         warm_up(WARM[1])
-        x_quant(0, 0, 0)
-        mix((0, 1), HEAD_CUT[1])
         x_out(0, 0, 1, scalar_copy)
-        e_quant(0, 1)
+        mix((0, 1), HEAD_CUT)
         x_quant(0, 0, 1)
+        e_quant(0, 1)
         stage1(UNITS[0], 0, (0,))
         x_turn_out(0, 0, 2)
         x_turn_out(0, 0, 3)
@@ -327,8 +330,8 @@ def tile_cross_layer_transcoder_s8_kernel(
         x_turn_out(0, 1, 3)
         x_quant(0, 1, 2)
         x_quant(0, 1, 3)
-        e_quant(1, 0)
         mix((1, 1))
+        e_quant(1, 0)
         e_quant(1, 1)
 
         due = []
@@ -365,7 +368,7 @@ def tile_cross_layer_transcoder_s8_kernel(
                     for unit in a_now[i : i + 1]:
                         banks.append((a_turn, a_out, (unit, 0), None))
                         banks.append((a_turn, a_out, (unit, 1), (ay_quant, unit)))
-                on_vector = (0, 1) if n == RUNS[-1] else (len(banks) - 1,)
+                on_vector = (0, 2) if n == RUNS[-1] else ()
                 for i, (turn, empty, args, then) in enumerate(banks):
                     turn(*args)
                     if i in on_vector:
@@ -399,11 +402,18 @@ def tile_cross_layer_transcoder_s8_kernel(
         c_group(3)
         y_tile(1, 3, slice(0, N // 2))
         G = GROUPS - 1
-        for h in range(2):
-            for g in range(2):
-                a_part((G, g), vector_copy, slice(64 * h, 64 * (h + 1)))
-            for g in range(2):
-                ac_quant((G, g), slice(256 * h, 256 * (h + 1)))
-            c_block(G, 2 * h, scalar_copy)
-            c_block(G, 2 * h + 1, vector_copy if h == 1 else scalar_copy)
+        quads = [slice(0, 64), slice(64, P)]
+        halves = [slice(0, 256), slice(256, 512)]
+        a_part((G, 0), vector_copy, quads[0])
+        a_part((G, 1), vector_copy, quads[0])
+        ac_quant((G, 0), halves[0])
+        a_part((G, 0), vector_copy, quads[1])
+        ac_quant((G, 1), halves[0])
+        c_block(G, 0, scalar_copy)
+        c_block(G, 1, scalar_copy)
+        a_part((G, 1), vector_copy, quads[1])
+        ac_quant((G, 0), halves[1])
+        ac_quant((G, 1), halves[1])
+        c_block(G, 2, scalar_copy)
+        c_block(G, 3, vector_copy)
         y_tile(1, 3, slice(N // 2, N))

@@ -19,15 +19,15 @@ P = 128
 FLOPS = 2 * (T * K * (F1 + F2) + T * (F1 + F2) * (N + R))
 GROUPS = 5
 UNITS = [(G, g) for G in range(3) for g in range(2)] + [(G, g) for g in range(2) for G in (3, 4)]
-RUNS = (1, 3, 6, 8)
-X2_PER_RUN = 3
-STEP_EVERY = 3
+RUNS = (1, 3, 4, 5, 8)
+X2_PER_RUN = 2
+STEP_AT = (1, 4)
 OUT_DELAY = 1
 QUANT_DELAY = 4
-HEAD_CUT = 352
-SHARED = 7
+HEAD_CUT = (336, 384)
+SHARED = 4
 SHARE = 32
-WARM = (2, 1)
+WARM = (3, 1)
 
 
 def tile_cross_layer_transcoder_s8_kernel(
@@ -79,11 +79,12 @@ def tile_cross_layer_transcoder_s8_kernel(
         load_e(1, 0)
         load_e(1, 1)
         x2_tiles = [(1, g, j) for g in range(2) for j in range(4)]
-        for G in range(2, GROUPS):
-            for key in x2_tiles[X2_PER_RUN * (G - 2) : X2_PER_RUN * (G - 1)]:
+        for i in range(4):
+            for key in x2_tiles[X2_PER_RUN * i : X2_PER_RUN * (i + 1)]:
                 load_x(*key)
-            load_e(G, 0)
-            load_e(G, 1)
+            if 2 + i < GROUPS:
+                load_e(2 + i, 0)
+                load_e(2 + i, 1)
         load_rows("d2", d2, 0, 0)
         load_rows("d2", d2, 1, 0)
         lab_sc = tile([P, 2, 4], F32, "lab_sc")
@@ -197,7 +198,7 @@ def tile_cross_layer_transcoder_s8_kernel(
 
         def a_turn(unit, h):
             if h == 0:
-                mixed["ay", unit] = tile([P, 512, 4], BF16, "a_t", 4)
+                mixed["ay", unit] = tile([P, 512, 4], BF16, "a_t", 5)
             words = a_raw[unit][:].rearrange("p j f -> p (j f)").bitcast(F32)
             a_b[unit, h] = bank()
             for i in range(4):
@@ -254,7 +255,7 @@ def tile_cross_layer_transcoder_s8_kernel(
             dst, row = (out_1, 512 * G + 128 * b) if G < 3 else (out_2, 512 * (G - 3) + 128 * b)
             store(acc[:], dst[row : row + P, :], copy)
 
-        def y_tile(g, j, n=slice(0, N)):
+        def y_tile(g, j, n=slice(0, N), copy=scalar_copy):
             if 4 * g + j < SHARED:
                 a_part(shared[4 * g + j], scalar_copy, slice(P - SHARE, P))
             acc = bank()[:, : n.stop - n.start]
@@ -267,7 +268,7 @@ def tile_cross_layer_transcoder_s8_kernel(
                     rhs_c, rhs_s = codes["d2", G - 3][:, n].bitcast(E4M3X4), scales["d2", G - 3][:, n]
                 mx(acc, codes[key][:, cols].bitcast(E4M3X4), scales[key][:, cols], rhs_c, rhs_s,
                    G == 0, G == GROUPS - 1)
-            store(acc, out_0.rearrange("(g p j) n -> g j p n", p=P, j=4)[g][j][:, n], scalar_copy)
+            store(acc, out_0.rearrange("(g p j) n -> g j p n", p=P, j=4)[g][j][:, n], copy)
 
         def pair(keys, tag, bufs):
             return [(mix, (k,)) for k in keys] + [(quant, (k, tag, bufs)) for k in keys]
@@ -298,16 +299,16 @@ def tile_cross_layer_transcoder_s8_kernel(
 
         x_turn(0, 0, 0)
         warm_up(WARM[0])
+        mix((0, 0), HEAD_CUT[0])
         x_out(0, 0, 0, scalar_copy)
-        mix((0, 0), HEAD_CUT)
-        x_quant(0, 0, 0)
         e_quant(0, 0)
         x_turn(0, 0, 1)
         warm_up(WARM[1])
+        x_quant(0, 0, 0)
+        mix((0, 1), HEAD_CUT[1])
         x_out(0, 0, 1, scalar_copy)
-        mix((0, 1), HEAD_CUT)
-        x_quant(0, 0, 1)
         e_quant(0, 1)
+        x_quant(0, 0, 1)
         stage1(UNITS[0], 0, (0,))
         x_turn_out(0, 0, 2)
         x_turn_out(0, 0, 3)
@@ -348,30 +349,26 @@ def tile_cross_layer_transcoder_s8_kernel(
         def tick(step):
             filled.append(1)
             flush(len(filled))
-            if step and len(filled) % STEP_EVERY == 1:
+            if step and len(filled) % 5 in STEP_AT:
                 steps(1)
 
         last = len(UNITS) - 1
-        turned = 0
+        turned = []
         for n in range(1, len(UNITS)):
             for j in range(4):
                 stage1(UNITS[n], j)
                 tick(n < last)
             if n in RUNS:
-                x_now, a_now = x2_tiles[:X2_PER_RUN], UNITS[turned:n]
-                x2_tiles[:X2_PER_RUN] = []
-                turned = n
                 banks = []
-                for i in range(3):
-                    for key in x_now[i : i + 1]:
-                        banks.append((x_turn, x_out, key, (x_quant, *key)))
-                    for unit in a_now[i : i + 1]:
-                        banks.append((a_turn, a_out, (unit, 0), None))
-                        banks.append((a_turn, a_out, (unit, 1), (ay_quant, unit)))
-                on_vector = (0, 2) if n == RUNS[-1] else ()
+                for unit in [u for u in UNITS[:n] if u[1] == 0 and u not in turned]:
+                    turned.append(unit)
+                    banks.append((a_turn, a_out, (unit, 0), None))
+                    banks.append((a_turn, a_out, (unit, 1), (ay_quant, unit)))
+                banks.extend([(x_turn, x_out, key, (x_quant, *key)) for key in x2_tiles[:X2_PER_RUN]])
+                x2_tiles[:X2_PER_RUN] = []
                 for i, (turn, empty, args, then) in enumerate(banks):
                     turn(*args)
-                    if i in on_vector:
+                    if n == RUNS[-1] and i % 2 == 0:
                         later(OUT_DELAY, empty, *args, vector_copy)
                     else:
                         empty(*args, scalar_copy)
@@ -380,27 +377,41 @@ def tile_cross_layer_transcoder_s8_kernel(
                     tick(n < RUNS[-1])
         flush(len(filled) + QUANT_DELAY)
 
+        late = [u for u in UNITS if u[1] == 1]
+
+        def turn_late(units):
+            for unit in units:
+                for h in range(2):
+                    a_turn(unit, h)
+                    a_out(unit, h, scalar_copy)
+
+        def prepare(groups, quantised=True):
+            steps(max(0, len(background) - 4 * (GROUPS - 1 - groups) - (0 if quantised else 2)))
+
         def c_group(G):
-            steps(len(background) - 4 * (GROUPS - 2 - G))
+            prepare(G + 1)
             for b in range(4):
                 c_block(G, b, scalar_copy)
 
         y_tile(0, 0)
         y_tile(0, 1)
-        for unit in UNITS[turned:]:
-            for h in range(2):
-                a_turn(unit, h)
-                a_out(unit, h, scalar_copy)
-        steps(len(background) - 4 * (GROUPS - 1) + 2)
-        for unit in UNITS[turned:]:
-            ay_quant(unit)
+        turn_late(late[:2])
         y_tile(0, 2)
         y_tile(0, 3)
-        for G in range(3):
-            y_tile(1, G)
-            c_group(G)
+        turn_late(late[2:])
+        prepare(2)
+        for unit in late[:2]:
+            ay_quant(unit)
+        c_group(0)
+        prepare(2 + 1, quantised=False)
+        for unit in late[2:]:
+            ay_quant(unit)
+        c_group(1)
+        y_tile(1, 0)
+        y_tile(1, 1)
+        c_group(2)
+        y_tile(1, 2)
         c_group(3)
-        y_tile(1, 3, slice(0, N // 2))
         G = GROUPS - 1
         quads = [slice(0, 64), slice(64, P)]
         halves = [slice(0, 256), slice(256, 512)]
@@ -416,4 +427,5 @@ def tile_cross_layer_transcoder_s8_kernel(
         ac_quant((G, 1), halves[1])
         c_block(G, 2, scalar_copy)
         c_block(G, 3, vector_copy)
+        y_tile(1, 3, slice(0, N // 2), vector_copy)
         y_tile(1, 3, slice(N // 2, N))

@@ -41,7 +41,7 @@ def tile_cross_layer_transcoder_s8_kernel(
         ctx.enter_context(tc.manual_schedule())
 
         def tile(shape, dtype, tag, bufs=1):
-            return pool.tile(shape, dtype, name=tag, tag=tag, bufs=bufs, align_bytes=64)
+            return pool.tile(shape, dtype, name=tag, tag=tag, bufs=bufs, align_bytes=256)
 
         def bank():
             return psum.tile([P, 512], F32, name="bank", tag="bank", bufs=8)
@@ -241,9 +241,9 @@ def tile_cross_layer_transcoder_s8_kernel(
 
         def store(acc, dst, copy):
             stored.append(dst)
-            o = tile([P, 512], F32, *[("x_raw", 7), ("x_t", 5)][len(stored) % 2])[:, : acc.shape[1]]
-            copy(out=o, in_=acc)
-            nc.sync.dma_start(out=dst, in_=o)
+            o = tile([P, 512], F32, *[("x_raw", 7), ("x_t", 5)][len(stored) % 2])
+            copy(out=o[:], in_=acc[:])
+            nc.sync.dma_start(out=dst, in_=o[:])
 
         def c_block(G, b, copy):
             acc = bank()
@@ -253,22 +253,22 @@ def tile_cross_layer_transcoder_s8_kernel(
                 mx(acc[:], codes[key][:, cols].bitcast(E4M3X4), scales[key][:, cols],
                    codes["lab", g][:].bitcast(E4M3X4), scales["lab", g][:], g == 0, g == 1)
             dst, row = (out_1, 512 * G + 128 * b) if G < 3 else (out_2, 512 * (G - 3) + 128 * b)
-            store(acc[:], dst[row : row + P, :], copy)
+            store(acc, dst[row : row + P, :], copy)
 
-        def y_tile(g, j, n=slice(0, N), copy=scalar_copy):
+        def y_tile(g, j):
             if 4 * g + j < SHARED:
                 a_part(shared[4 * g + j], scalar_copy, slice(P - SHARE, P))
-            acc = bank()[:, : n.stop - n.start]
+            acc = bank()
             cols = slice(128 * j, 128 * (j + 1))
             for G in range(GROUPS):
                 key = ("ay", (G, g))
                 if G < 3:
-                    rhs_c, rhs_s = d1_w[:, G, 2 * n.start : 2 * n.stop].bitcast(E2M1X4), d1_sc[:, G, n]
+                    rhs_c, rhs_s = d1_w[:, G, :].bitcast(E2M1X4), d1_sc[:, G, :]
                 else:
-                    rhs_c, rhs_s = codes["d2", G - 3][:, n].bitcast(E4M3X4), scales["d2", G - 3][:, n]
-                mx(acc, codes[key][:, cols].bitcast(E4M3X4), scales[key][:, cols], rhs_c, rhs_s,
+                    rhs_c, rhs_s = codes["d2", G - 3][:].bitcast(E4M3X4), scales["d2", G - 3][:]
+                mx(acc[:], codes[key][:, cols].bitcast(E4M3X4), scales[key][:, cols], rhs_c, rhs_s,
                    G == 0, G == GROUPS - 1)
-            store(acc, out_0.rearrange("(g p j) n -> g j p n", p=P, j=4)[g][j][:, n], copy)
+            store(acc, out_0.rearrange("(g p j) n -> g j p n", p=P, j=4)[g][j], scalar_copy)
 
         def pair(keys, tag, bufs):
             return [(mix, (k,)) for k in keys] + [(quant, (k, tag, bufs)) for k in keys]
@@ -427,5 +427,4 @@ def tile_cross_layer_transcoder_s8_kernel(
         ac_quant((G, 1), halves[1])
         c_block(G, 2, scalar_copy)
         c_block(G, 3, vector_copy)
-        y_tile(1, 3, slice(0, N // 2), vector_copy)
-        y_tile(1, 3, slice(N // 2, N))
+        y_tile(1, 3)

@@ -18,16 +18,8 @@ T, K, F1, F2, N, R = 1024, 1024, 1536, 1024, 512, 512
 P = 128
 FLOPS = 2 * (T * K * (F1 + F2) + T * (F1 + F2) * (N + R))
 GROUPS = 5
-UNITS = [(G, g) for G in range(3) for g in range(2)] + [(G, g) for g in range(2) for G in (3, 4)]
-RUNS = (1, 3, 4, 5, 8)
-X2_PER_RUN = 2
-STEP_AT = (1, 4)
-OUT_DELAY = 1
-QUANT_DELAY = 4
 HEAD_CUT = (336, 384)
-SHARED = 4
-SHARE = 32
-WARM = (3, 1)
+WARM = (2, 2)
 
 
 def tile_cross_layer_transcoder_s8_kernel(
@@ -54,7 +46,7 @@ def tile_cross_layer_transcoder_s8_kernel(
         x_raw, rows, lab_raw = {}, {}, {}
 
         def load_x(s, g, j):
-            t = tile([P, K], BF16, "x_raw", 7)
+            t = tile([P, K], BF16, "x_raw", 8)
             nc.sync.dma_start(out=t[:], in_=(x1, x2)[s].rearrange("(g p j) k -> g p j k", p=P, j=4)[g][:, j, :])
             x_raw[s, g, j] = t[:]
 
@@ -71,20 +63,27 @@ def tile_cross_layer_transcoder_s8_kernel(
             else:
                 load_rows(G, e2, q, 512 * (G - 3))
 
-        for q in range(2):
-            load_x(0, 0, q)
-            load_e(0, q)
-        for g, j in [(0, 2), (0, 3), (1, 0), (1, 1), (1, 2), (1, 3)]:
-            load_x(0, g, j)
+        def load_xs(s, g, js):
+            for j in js:
+                load_x(s, g, j)
+
+        load_x(0, 0, 0)
+        load_e(0, 0)
+        load_x(0, 0, 1)
+        load_e(0, 1)
+        load_xs(0, 0, (2, 3))
+        load_xs(0, 1, (0, 1))
         load_e(1, 0)
+        load_xs(0, 1, (2, 3))
         load_e(1, 1)
-        x2_tiles = [(1, g, j) for g in range(2) for j in range(4)]
-        for i in range(4):
-            for key in x2_tiles[X2_PER_RUN * i : X2_PER_RUN * (i + 1)]:
-                load_x(*key)
-            if 2 + i < GROUPS:
-                load_e(2 + i, 0)
-                load_e(2 + i, 1)
+        load_e(2, 0)
+        load_e(2, 1)
+        load_xs(1, 0, range(4))
+        load_e(3, 0)
+        load_e(3, 1)
+        load_e(4, 0)
+        load_e(4, 1)
+        load_xs(1, 1, range(4))
         load_rows("d2", d2, 0, 0)
         load_rows("d2", d2, 1, 0)
         lab_sc = tile([P, 2, 4], F32, "lab_sc")
@@ -103,49 +102,48 @@ def tile_cross_layer_transcoder_s8_kernel(
             )
 
         x_c, x_s, x_b, x_t, x_w = {}, {}, {}, {}, {}
+        mixed, codes, scales = {}, {}, {}
+        a_raw, acc, a_b = {}, {}, {}
+        copies = {"S": scalar_copy, "V": vector_copy}
 
-        def x_sort(s, g, j):
-            t = tile([P, 512], F32, "x_t", 5)
+        def x_sort(x):
+            t = tile([P, 512], F32, "x_w", 4)
             vector_copy(
                 out=t[:].rearrange("p (q u m) -> p q u m", q=2, u=2),
-                in_=x_raw[s, g, j].bitcast(F32).rearrange("p (q m u) -> p q u m", q=2, u=2),
+                in_=x_raw[x].bitcast(F32).rearrange("p (q m u) -> p q u m", q=2, u=2),
             )
-            x_w[s, g, j] = t
+            x_w[x] = t
 
-        def x_turn(s, g, j):
-            x_b[s, g, j] = bank()
-            words = x_raw[s, g, j].bitcast(F32)
+        def x_turn(x):
+            x_b[x] = bank()
+            words = x_raw[x].bitcast(F32)
             for q in range(2):
                 for u in range(2):
                     i = 2 * q + u
-                    if (s, g, j) in x_w:
-                        src = x_w[s, g, j][:, i * P : (i + 1) * P]
+                    if x in x_w:
+                        src = x_w[x][:, i * P : (i + 1) * P]
                     else:
                         src = words[:, 256 * q + u : 256 * (q + 1) : 2]
-                    nc.tensor.transpose(x_b[s, g, j][:, i * P : (i + 1) * P], src, ident[:])
+                    nc.tensor.transpose(x_b[x][:, i * P : (i + 1) * P], src, ident[:])
 
-        def x_out(s, g, j, copy):
-            x_t[s, g, j] = tile([P, 1024], BF16, "x_t", 5)
-            copy(
-                out=x_t[s, g, j][:].bitcast(F32).rearrange("p (q t u) -> p q t u", q=2, u=2),
-                in_=x_b[s, g, j][:].rearrange("p (q u t) -> p q t u", q=2, u=2),
+        def x_out(x, eng):
+            x_t[x] = tile([P, 1024], BF16, "x_t", 5)
+            copies[eng](
+                out=x_t[x][:].bitcast(F32).rearrange("p (q t u) -> p q t u", q=2, u=2),
+                in_=x_b[x][:].rearrange("p (q u t) -> p q t u", q=2, u=2),
             )
 
-        def x_quant(s, g, j):
-            x_c[s, g, j] = tile([P, 256], U32, "x_c", 16)
-            x_s[s, g, j] = tile([P, 256], U8, "x_s", 16)
-            nc.vector.quantize_mx(out=x_c[s, g, j][:].bitcast(E4M3X4), scales=x_s[s, g, j][:], in_=x_t[s, g, j][:])
+        def x_quant(x):
+            x_c[x] = tile([P, 256], U32, "x_c", 16)
+            x_s[x] = tile([P, 256], U8, "x_s", 16)
+            nc.vector.quantize_mx(out=x_c[x][:].bitcast(E4M3X4), scales=x_s[x][:], in_=x_t[x][:])
 
-        mixed, codes, scales = {}, {}, {}
-
-        def mix(key, cut=512):
-            t = tile([P, 512, 4], BF16, "mix", 4)
-            dst = t[:].rearrange("p (c i) j -> p c j i", i=4)
+        def mix(key, eng, lo, hi):
+            if key not in mixed:
+                mixed[key] = tile([P, 512, 4], BF16, "mix", 4)
+            dst = mixed[key][:].rearrange("p (c i) j -> p c j i", i=4)
             src = rows[key].rearrange("p j (c i) -> p c j i", i=4)
-            vector_copy(out=dst[:, : cut // 4], in_=src[:, : cut // 4])
-            if cut < 512:
-                scalar_copy(out=dst[:, cut // 4 :], in_=src[:, cut // 4 :])
-            mixed[key] = t
+            copies[eng](out=dst[:, lo // 4 : hi // 4], in_=src[:, lo // 4 : hi // 4])
 
         def quant(key, tag, bufs):
             codes[key] = tile([P, 512], U32, tag + "_c", bufs)
@@ -153,9 +151,6 @@ def tile_cross_layer_transcoder_s8_kernel(
             nc.vector.quantize_mx(
                 out=codes[key][:].bitcast(E4M3X4), scales=scales[key][:], in_=mixed[key][:].rearrange("p c j -> p (c j)")
             )
-
-        def e_quant(G, q):
-            quant((G, q), "e", 6)
 
         def widen(g):
             t = tile([P, 4, R], BF16, "mix", 4)
@@ -169,96 +164,92 @@ def tile_cross_layer_transcoder_s8_kernel(
                 )
             rows["lab", g] = t[:]
 
-        def mx(acc, lhs_c, lhs_s, rhs_c, rhs_s, first, final):
+        def mx(out, lhs_c, lhs_s, rhs_c, rhs_s, first, final):
             nc.tensor.matmul_mx(
-                out=acc, lhsT=lhs_c, lhsT_scale=lhs_s, rhs=rhs_c, rhs_scale=rhs_s, start=first, stop=final
+                out=out, lhsT=lhs_c, lhsT_scale=lhs_s, rhs=rhs_c, rhs_scale=rhs_s, start=first, stop=final
             )
 
-        a_raw, a_acc, a_b = {}, {}, {}
-        shared = [(G, g) for G in range(GROUPS) for g in range(2)][:SHARED]
-
-        def stage1(unit, j, passes=(0, 1)):
+        def stage1(unit, j, q):
             G, g = unit
-            s = 0 if G < 3 else 1
+            x = (0 if G < 3 else 1, g, j)
+            if q == 0:
+                acc[unit, j] = bank()
+            cols = slice(128 * q, 128 * (q + 1))
+            mx(acc[unit, j][:], x_c[x][:, cols].bitcast(E4M3X4), x_s[x][:, cols],
+               codes[G, q][:].bitcast(E4M3X4), scales[G, q][:], q == 0, q == 1)
+
+        def relu(unit, j, eng):
             if unit not in a_raw:
                 a_raw[unit] = tile([P, 4, 512], BF16, "a", 10)
-            if 0 in passes:
-                a_acc[unit, j] = bank()
-            acc = a_acc[unit, j]
-            for q in passes:
-                cols = slice(128 * q, 128 * (q + 1))
-                mx(acc[:], x_c[s, g, j][:, cols].bitcast(E4M3X4), x_s[s, g, j][:, cols],
-                   codes[G, q][:].bitcast(E4M3X4), scales[G, q][:], q == 0, q == 1)
-            if 1 in passes:
-                nc.scalar.activation(
-                    out=a_raw[unit][:, j, :].rearrange("p (u m e) -> p u m e", u=2, e=2),
-                    in_=acc[:].rearrange("p (m u e) -> p u m e", u=2, e=2),
-                    func=ACT.Relu,
-                )
+            dst = a_raw[unit][:, j, :].rearrange("p (u m e) -> p u m e", u=2, e=2)
+            src = acc[unit, j][:].rearrange("p (m u e) -> p u m e", u=2, e=2)
+            if eng == "S":
+                nc.scalar.activation(out=dst, in_=src, func=ACT.Relu)
+            else:
+                nc.vector.tensor_scalar(out=dst, in0=src, scalar1=0.0, scalar2=None, op0=ALU.max)
 
         def a_turn(unit, h):
-            if h == 0:
-                mixed["ay", unit] = tile([P, 512, 4], BF16, "a_t", 5)
             words = a_raw[unit][:].rearrange("p j f -> p (j f)").bitcast(F32)
             a_b[unit, h] = bank()
             for i in range(4):
                 col = 512 * h + 128 * i
                 nc.tensor.transpose(a_b[unit, h][:, i * P : (i + 1) * P], words[:, col : col + P], ident[:])
 
-        def a_out(unit, h, copy):
+        def a_out(unit, h, eng):
+            if ("ay", unit) not in mixed:
+                mixed["ay", unit] = tile([P, 512, 4], BF16, "a_t", 5)
             dst = mixed["ay", unit][:].rearrange("p t f -> p (t f)").bitcast(F32)
-            copy(
+            copies[eng](
                 out=dst[:, 512 * h : 512 * (h + 1)].rearrange("p (j t u) -> p j t u", j=2, u=2),
                 in_=a_b[unit, h][:].rearrange("p (j u t) -> p j t u", j=2, u=2),
             )
 
-        def ay_quant(unit):
-            quant(("ay", unit), "ay", 10)
+        def a_mix(unit, eng, es, half=None):
+            if ("ac", unit) not in mixed:
+                mixed["ac", unit] = tile([P, 512, 4], BF16, "mix", 4)
+            dst = mixed["ac", unit][:].rearrange("p (e w l) j -> p w j l e", e=2, l=2)
+            src = a_raw[unit][:].rearrange("p j (w l e) -> p w j l e", l=2, e=2)
+            if half is None:
+                copies[eng](out=dst[:, es], in_=src[:, es])
+            else:
+                dst = mixed["ac", unit][:].rearrange("p (u e w l) j -> p u w j l e", u=2, e=2, l=2)
+                src = a_raw[unit][:].rearrange("p j (u w l e) -> p u w j l e", u=2, l=2, e=2)
+                copies[eng](out=dst[:, half], in_=src[:, half])
 
-        def ac_quant(unit, cols=slice(0, 512)):
+        def ac_quant(unit, cols):
             key = ("ac", unit)
             if key not in codes:
-                codes[key] = tile([P, 512], U32, "ac_c", 4)
-                scales[key] = tile([P, 512], U8, "ac_s", 4)
+                codes[key] = tile([P, 512], U32, "ac_c", 6)
+                scales[key] = tile([P, 512], U8, "ac_s", 6)
             nc.vector.quantize_mx(
                 out=codes[key][:, cols].bitcast(E4M3X4),
                 scales=scales[key][:, cols],
                 in_=mixed[key][:, cols, :].rearrange("p c j -> p (c j)"),
             )
 
-        def a_part(unit, copy, quads):
-            if ("ac", unit) not in mixed:
-                mixed["ac", unit] = tile([P, 512, 4], BF16, "mix_shared" if unit in shared else "mix", 4)
-            copy(
-                out=mixed["ac", unit][:].rearrange("p (m u e) j -> p u m j e", u=2, e=2)[:, :, quads],
-                in_=a_raw[unit][:].rearrange("p j (u m e) -> p u m j e", u=2, e=2)[:, :, quads],
-            )
-
-        def a_mix(unit):
-            a_part(unit, vector_copy, slice(0, P - SHARE if unit in shared else P))
-
         stored = []
 
-        def store(acc, dst, copy):
+        def store(key, dst, eng):
             stored.append(dst)
-            o = tile([P, 512], F32, *[("x_raw", 7), ("x_t", 5)][len(stored) % 2])
-            copy(out=o[:], in_=acc[:])
+            o = tile([P, 512], F32, *[("x_raw", 8), ("x_t", 5)][len(stored) % 2])
+            copies[eng](out=o[:], in_=acc[key][:])
             nc.sync.dma_start(out=dst, in_=o[:])
 
-        def c_block(G, b, copy):
-            acc = bank()
+        def c_block(G, b):
+            acc["c", G, b] = bank()
             cols = slice(128 * b, 128 * (b + 1))
             for g in range(2):
                 key = ("ac", (G, g))
-                mx(acc[:], codes[key][:, cols].bitcast(E4M3X4), scales[key][:, cols],
+                mx(acc["c", G, b][:], codes[key][:, cols].bitcast(E4M3X4), scales[key][:, cols],
                    codes["lab", g][:].bitcast(E4M3X4), scales["lab", g][:], g == 0, g == 1)
-            dst, row = (out_1, 512 * G + 128 * b) if G < 3 else (out_2, 512 * (G - 3) + 128 * b)
-            store(acc, dst[row : row + P, :], copy)
+
+        def c_out(G, b, eng):
+            dst = out_1[512 * G : 512 * (G + 1), :] if G < 3 else out_2[512 * (G - 3) : 512 * (G - 2), :]
+            order = "(m u e) r -> e u m r" if G < GROUPS - 1 else "(m u e) r -> u e m r"
+            store(("c", G, b), dst.rearrange(order, u=2, e=2)[b // 2][b % 2], eng)
 
         def y_tile(g, j):
-            if 4 * g + j < SHARED:
-                a_part(shared[4 * g + j], scalar_copy, slice(P - SHARE, P))
-            acc = bank()
+            acc["y", g, j] = bank()
             cols = slice(128 * j, 128 * (j + 1))
             for G in range(GROUPS):
                 key = ("ay", (G, g))
@@ -266,26 +257,11 @@ def tile_cross_layer_transcoder_s8_kernel(
                     rhs_c, rhs_s = d1_w[:, G, :].bitcast(E2M1X4), d1_sc[:, G, :]
                 else:
                     rhs_c, rhs_s = codes["d2", G - 3][:].bitcast(E4M3X4), scales["d2", G - 3][:]
-                mx(acc[:], codes[key][:, cols].bitcast(E4M3X4), scales[key][:, cols], rhs_c, rhs_s,
+                mx(acc["y", g, j][:], codes[key][:, cols].bitcast(E4M3X4), scales[key][:, cols], rhs_c, rhs_s,
                    G == 0, G == GROUPS - 1)
-            store(acc, out_0.rearrange("(g p j) n -> g j p n", p=P, j=4)[g][j], scalar_copy)
 
-        def pair(keys, tag, bufs):
-            return [(mix, (k,)) for k in keys] + [(quant, (k, tag, bufs)) for k in keys]
-
-        background = []
-        for G in range(2, GROUPS):
-            background.extend(pair([(G, 0), (G, 1)], "e", 6))
-        background.extend(pair([("d2", 0), ("d2", 1)], "d2", 2))
-        background.extend([(widen, (0,)), (widen, (1,))] + pair([("lab", 0), ("lab", 1)], "lab", 2))
-        for G in range(GROUPS - 1):
-            background.extend([(a_mix, ((G, g),)) for g in range(2)])
-            background.extend([(ac_quant, ((G, g),)) for g in range(2)])
-
-        def steps(count):
-            for fn, args in background[:count]:
-                fn(*args)
-            background[:count] = []
+        def y_out(g, j, eng):
+            store(("y", g, j), out_0.rearrange("(g p j) n -> g j p n", p=P, j=4)[g][j], eng)
 
         def warm_up(count):
             for i in range(count):
@@ -293,138 +269,192 @@ def tile_cross_layer_transcoder_s8_kernel(
                 first = x_raw[0, 0, 0]
                 nc.tensor.matmul(unread[:], lhsT=first[:, :P], rhs=first[:, :512], start=True, stop=True)
 
-        def x_turn_out(s, g, j):
-            x_turn(s, g, j)
-            x_out(s, g, j, scalar_copy)
+        tensor_p, scalar_p, vector_p = [], [], []
+        prog = {"S": scalar_p, "V": vector_p}
+        parts = {}
 
-        x_turn(0, 0, 0)
-        warm_up(WARM[0])
-        mix((0, 0), HEAD_CUT[0])
-        x_out(0, 0, 0, scalar_copy)
-        e_quant(0, 0)
-        x_turn(0, 0, 1)
-        warm_up(WARM[1])
-        x_quant(0, 0, 0)
-        mix((0, 1), HEAD_CUT[1])
-        x_out(0, 0, 1, scalar_copy)
-        e_quant(0, 1)
-        x_quant(0, 0, 1)
-        stage1(UNITS[0], 0, (0,))
-        x_turn_out(0, 0, 2)
-        x_turn_out(0, 0, 3)
-        stage1(UNITS[0], 0, (1,))
-        stage1(UNITS[0], 1)
-        for h in range(2):
-            x_sort(0, 1, 2 * h)
-            x_sort(0, 1, 2 * h + 1)
-            if h == 0:
-                x_quant(0, 0, 2)
-                x_quant(0, 0, 3)
-        x_turn_out(0, 1, 0)
-        x_turn_out(0, 1, 1)
-        x_quant(0, 1, 0)
-        x_quant(0, 1, 1)
-        mix((1, 0))
-        stage1(UNITS[0], 2)
-        stage1(UNITS[0], 3)
-        x_turn_out(0, 1, 2)
-        x_turn_out(0, 1, 3)
-        x_quant(0, 1, 2)
-        x_quant(0, 1, 3)
-        mix((1, 1))
-        e_quant(1, 0)
-        e_quant(1, 1)
+        def p_sort(x):
+            vector_p.append((("xw", x), [], x_sort, (x,)))
 
-        due = []
-        filled = []
+        def p_turn_x(x, sort=False):
+            tensor_p.append((("xb", x), [("xw", x)] if sort else [], x_turn, (x,)))
 
-        def later(delay, fn, *args):
-            due.append((len(filled) + delay, fn, args))
+        def p_x_out(x, eng):
+            prog[eng].append((("xt", x), [("xb", x)], x_out, (x, eng)))
 
-        def flush(upto):
-            for item in [d for d in due if d[0] <= upto]:
-                due.remove(item)
-                item[1](*item[2])
+        def p_xq(x):
+            vector_p.append((("xc", x), [("xt", x)], x_quant, (x,)))
 
-        def tick(step):
-            filled.append(1)
-            flush(len(filled))
-            if step and len(filled) % 5 in STEP_AT:
-                steps(1)
+        def p_mix(key, eng="V", lo=0, hi=512):
+            parts.setdefault(key, []).append(("mix", key, lo))
+            prog[eng].append((("mix", key, lo), [("wide", key[1])] if key[0] == "lab" else [], mix, (key, eng, lo, hi)))
 
-        last = len(UNITS) - 1
-        turned = []
-        for n in range(1, len(UNITS)):
+        def p_quant(key, tag, bufs):
+            vector_p.append((("q", key), parts[key], quant, (key, tag, bufs)))
+
+        def p_widen(g):
+            vector_p.append((("wide", g), [], widen, (g,)))
+
+        def p_s1(unit, j, q):
+            tensor_p.append((("s1", unit, j, q), [("xc", (unit[0] // 3, unit[1], j)), ("q", (unit[0], q))], stage1, (unit, j, q)))
+
+        def p_relu(unit, j, eng):
+            prog[eng].append((("a", unit, j), [("s1", unit, j, 1)], relu, (unit, j, eng)))
+
+        def p_turn_a(unit, h):
+            tensor_p.append((("ab", unit, h), [("a", unit, 2 * h), ("a", unit, 2 * h + 1)], a_turn, (unit, h)))
+
+        def p_a_out(unit, h, eng):
+            parts.setdefault(("ay", unit), []).append(("at", unit, h))
+            prog[eng].append((("at", unit, h), [("ab", unit, h)], a_out, (unit, h, eng)))
+
+        def p_amix(unit, eng="V", lo=0, hi=P):
+            parts.setdefault(("ac", unit), []).append(("amix", unit, lo))
+            prog[eng].append((("amix", unit, lo), [("a", unit, j) for j in range(4)], a_mix, (unit, eng, slice(lo, hi))))
+
+        def p_ahalf(unit, e):
+            parts["ac", unit, e] = [("amix", unit, e)]
+            vector_p.append((("amix", unit, e), [("a", unit, j) for j in range(4)], a_mix, (unit, "V", None, e)))
+
+        def p_acq(unit, lo=0, hi=512):
+            vector_p.append((("acq", unit, lo), parts["ac", unit] if hi - lo == 512 else parts["ac", unit, lo // 256], ac_quant, (unit, slice(lo, hi))))
+            for b in range(lo // P, hi // P):
+                parts["acb", unit, b] = ("acq", unit, lo)
+
+        def p_c(G, b):
+            tensor_p.append((("c", G, b), [("acb", (G, g), b) for g in range(2)] + [("q", ("lab", g)) for g in range(2)], c_block, (G, b)))
+
+        def p_c_out(G, b, eng):
+            prog[eng].append((("co", G, b), [("c", G, b)], c_out, (G, b, eng)))
+
+        def p_y(g, j):
+            needs = [("q", ("ay", (G, g))) for G in range(GROUPS)] + [("q", ("d2", q)) for q in range(2)]
+            tensor_p.append((("y", g, j), needs, y_tile, (g, j)))
+
+        def p_y_out(g, j, eng):
+            prog[eng].append((("yo", g, j), [("y", g, j)], y_out, (g, j, eng)))
+
+        def p_warm(n):
+            tensor_p.append((("warm", len(tensor_p)), [], warm_up, (n,)))
+
+        def unit_s(unit, on_v=()):
             for j in range(4):
-                stage1(UNITS[n], j)
-                tick(n < last)
-            if n in RUNS:
-                banks = []
-                for unit in [u for u in UNITS[:n] if u[1] == 0 and u not in turned]:
-                    turned.append(unit)
-                    banks.append((a_turn, a_out, (unit, 0), None))
-                    banks.append((a_turn, a_out, (unit, 1), (ay_quant, unit)))
-                banks.extend([(x_turn, x_out, key, (x_quant, *key)) for key in x2_tiles[:X2_PER_RUN]])
-                x2_tiles[:X2_PER_RUN] = []
-                for i, (turn, empty, args, then) in enumerate(banks):
-                    turn(*args)
-                    if n == RUNS[-1] and i % 2 == 0:
-                        later(OUT_DELAY, empty, *args, vector_copy)
-                    else:
-                        empty(*args, scalar_copy)
-                    if then:
-                        later(QUANT_DELAY, *then)
-                    tick(n < RUNS[-1])
-        flush(len(filled) + QUANT_DELAY)
+                p_s1(unit, j, 0)
+                p_s1(unit, j, 1)
+                if j not in on_v:
+                    p_relu(unit, j, "S")
 
-        late = [u for u in UNITS if u[1] == 1]
+        def e_group(G, tag="e", bufs=6):
+            for q in range(2):
+                p_mix((G, q))
+            for q in range(2):
+                p_quant((G, q), tag, bufs)
 
-        def turn_late(units):
-            for unit in units:
-                for h in range(2):
-                    a_turn(unit, h)
-                    a_out(unit, h, scalar_copy)
+        def ac_group(G):
+            for g in range(2):
+                p_amix((G, g))
+            for g in range(2):
+                p_acq((G, g))
 
-        def prepare(groups, quantised=True):
-            steps(max(0, len(background) - 4 * (GROUPS - 1 - groups) - (0 if quantised else 2)))
+        def c_group(G, bs=range(4)):
+            for b in bs:
+                p_c(G, b)
+                p_c_out(G, b, "S")
 
-        def c_group(G):
-            prepare(G + 1)
-            for b in range(4):
-                c_block(G, b, scalar_copy)
+        def y_s(g, j):
+            p_y(g, j)
+            p_y_out(g, j, "S")
 
-        y_tile(0, 0)
-        y_tile(0, 1)
-        turn_late(late[:2])
-        y_tile(0, 2)
-        y_tile(0, 3)
-        turn_late(late[2:])
-        prepare(2)
-        for unit in late[:2]:
-            ay_quant(unit)
+        X = lambda s, g, js=range(4): [(s, g, j) for j in js]
+        U0 = (0, 0)
+        p_turn_x((0, 0, 0)); p_warm(WARM[0]); p_mix((0, 0), "V", 0, HEAD_CUT[0]); p_mix((0, 0), "S", HEAD_CUT[0], 512)
+        p_x_out((0, 0, 0), "S"); p_quant((0, 0), "e", 6)
+        p_turn_x((0, 0, 1)); p_warm(WARM[1]); p_xq((0, 0, 0))
+        p_x_out((0, 0, 1), "S")
+        p_mix((0, 1), "V", 0, HEAD_CUT[1]); p_mix((0, 1), "S", HEAD_CUT[1], 512)
+        p_xq((0, 0, 1)); p_quant((0, 1), "e", 6)
+        p_s1(U0, 0, 0)
+        for j in (2, 3):
+            p_turn_x((0, 0, j)); p_x_out((0, 0, j), "S")
+        p_s1(U0, 1, 0); p_s1(U0, 0, 1); p_s1(U0, 1, 1)
+        p_sort((0, 1, 0)); p_sort((0, 1, 1)); p_xq((0, 0, 2)); p_xq((0, 0, 3)); p_mix((1, 0)); p_sort((0, 1, 2));  p_sort((0, 1, 3))
+        p_relu(U0, 0, "S")
+        for x in X(0, 1, (0, 1)):
+            p_turn_x(x, True); p_x_out(x, "S")
+        p_relu(U0, 1, "S")
+        for j in (2, 3):
+            p_s1(U0, j, 0); p_s1(U0, j, 1)
+        p_relu(U0, 2, "S")
+        for x in X(0, 1, (2, 3)):
+            p_turn_x(x, True); p_x_out(x, "S")
+        p_relu(U0, 3, "S")
+        p_xq((0, 1, 0)); p_xq((0, 1, 1)); p_quant((1, 0), "e", 6); p_mix((1, 1)); p_xq((0, 1, 2)); p_xq((0, 1, 3)); p_quant((1, 1), "e", 6)
+        for j in (0, 1):
+            p_s1((0, 1), j, 0); p_s1((0, 1), j, 1); p_relu((0, 1), j, "S")
+        for j in range(4):
+            p_s1((1, 0), j, 0)
+        for j in (2, 3):
+            p_s1((0, 1), j, 0); p_s1((0, 1), j, 1); p_relu((0, 1), j, "S")
+        for j in range(4):
+            p_s1((1, 0), j, 1); p_relu((1, 0), j, "S")
+
+        p_mix((2, 0)); p_mix((2, 1)); p_quant((2, 0), "e", 6); p_quant((2, 1), "e", 6)
+        unit_s((1, 1))
+        for x in X(1, 0):
+            p_turn_x(x); p_x_out(x, "S")
+        p_mix((3, 0)); p_mix((3, 1)); p_quant((3, 0), "e", 6); p_quant((3, 1), "e", 6)
+        unit_s((2, 0))
+        p_mix((4, 0)); p_mix((4, 1))
+        for x in X(1, 0):
+            p_xq(x)
+        unit_s((2, 1))
+        p_quant((4, 0), "e", 6); p_quant((4, 1), "e", 6)
+        for x in X(1, 1):
+            p_sort(x)
+        unit_s((3, 0))
+        unit_s((4, 0))
+        p_mix(("d2", 0)); p_mix(("d2", 1)); p_quant(("d2", 0), "d2", 2); p_quant(("d2", 1), "d2", 2)
+        p_widen(0)
+        for x in X(1, 1):
+            p_turn_x(x, True); p_x_out(x, "VVVS"[x[2]])
+        for x in X(1, 1):
+            p_xq(x)
+        p_widen(1)
+        for G in range(GROUPS):
+            for h in range(2):
+                p_turn_a((G, 0), h); p_a_out((G, 0), h, "S")
+        unit_s((3, 1)); unit_s((4, 1))
+        p_mix(("lab", 0))
+        for G in range(GROUPS):
+            p_quant(("ay", (G, 0)), "ay", 10)
+        p_mix(("lab", 1)); p_quant(("lab", 0), "lab", 2)
+        p_amix((0, 0)); p_quant(("lab", 1), "lab", 2); p_amix((0, 1)); p_acq((0, 0)); p_amix((1, 0)); p_acq((0, 1))
+        y_s(0, 0); y_s(0, 1)
+        p_amix((1, 1)); p_acq((1, 0))
+        for G in range(GROUPS):
+            for h in range(2):
+                p_turn_a((G, 1), h); p_a_out((G, 1), h, "S")
+        y_s(0, 2); y_s(0, 3)
+        p_amix((2, 0)); p_acq((1, 1))
         c_group(0)
-        prepare(2 + 1, quantised=False)
-        for unit in late[2:]:
-            ay_quant(unit)
+        for G in range(GROUPS):
+            p_quant(("ay", (G, 1)), "ay", 10)
+        p_amix((2, 1)); p_acq((2, 0))
         c_group(1)
-        y_tile(1, 0)
-        y_tile(1, 1)
+        p_amix((3, 0)); p_acq((2, 1)); p_amix((3, 1)); p_acq((3, 0))
+        y_s(1, 0); y_s(1, 1)
         c_group(2)
-        y_tile(1, 2)
+        y_s(1, 2)
+        p_ahalf((4, 0), 0); p_acq((3, 1)); p_ahalf((4, 1), 0); p_acq((4, 0), 0, 256); p_ahalf((4, 0), 1); p_acq((4, 1), 0, 256)
+        p_ahalf((4, 1), 1); p_acq((4, 0), 256, 512); p_acq((4, 1), 256, 512)
         c_group(3)
-        G = GROUPS - 1
-        quads = [slice(0, 64), slice(64, P)]
-        halves = [slice(0, 256), slice(256, 512)]
-        a_part((G, 0), vector_copy, quads[0])
-        a_part((G, 1), vector_copy, quads[0])
-        ac_quant((G, 0), halves[0])
-        a_part((G, 0), vector_copy, quads[1])
-        ac_quant((G, 1), halves[0])
-        c_block(G, 0, scalar_copy)
-        c_block(G, 1, scalar_copy)
-        a_part((G, 1), vector_copy, quads[1])
-        ac_quant((G, 0), halves[1])
-        ac_quant((G, 1), halves[1])
-        c_block(G, 2, scalar_copy)
-        c_block(G, 3, vector_copy)
-        y_tile(1, 3)
+        c_group(4)
+        y_s(1, 3)
+
+        made = set()
+        queues = [scalar_p, vector_p, tensor_p]
+        while any(queues):
+            ready = [q for q in queues if q and all(parts.get(n, n) in made if n[0] == "acb" else n in made for n in q[0][1])]
+            key, needs, fn, args = ready[0].pop(0)
+            fn(*args)
+            made.add(key)

@@ -141,9 +141,9 @@ def tile_cross_layer_transcoder_s8_kernel(
         def mix(key, eng, lo, hi):
             if key not in mixed:
                 mixed[key] = tile([P, 512, 4], BF16, "mix", 4)
-            dst = mixed[key][:].rearrange("p (c i) j -> p c j i", i=4)
-            src = rows[key].rearrange("p j (c i) -> p c j i", i=4)
-            copies[eng](out=dst[:, lo // 4 : hi // 4], in_=src[:, lo // 4 : hi // 4])
+            dst = mixed[key][:].rearrange("p (c i) j -> p c j i", i=2)
+            src = rows[key].rearrange("p j (c i) -> p c j i", i=2)
+            copies[eng](out=dst[:, lo // 2 : hi // 2], in_=src[:, lo // 2 : hi // 2])
 
         def quant(key, tag, bufs):
             codes[key] = tile([P, 512], U32, tag + "_c", bufs)
@@ -204,17 +204,13 @@ def tile_cross_layer_transcoder_s8_kernel(
                 in_=a_b[unit, h][:].rearrange("p (j u t) -> p j t u", j=2, u=2),
             )
 
-        def a_mix(unit, eng, es, half=None):
+        def a_mix(unit, eng, quads):
             if ("ac", unit) not in mixed:
                 mixed["ac", unit] = tile([P, 512, 4], BF16, "mix", 4)
-            dst = mixed["ac", unit][:].rearrange("p (e w l) j -> p w j l e", e=2, l=2)
-            src = a_raw[unit][:].rearrange("p j (w l e) -> p w j l e", l=2, e=2)
-            if half is None:
-                copies[eng](out=dst[:, es], in_=src[:, es])
-            else:
-                dst = mixed["ac", unit][:].rearrange("p (u e w l) j -> p u w j l e", u=2, e=2, l=2)
-                src = a_raw[unit][:].rearrange("p j (u w l e) -> p u w j l e", u=2, l=2, e=2)
-                copies[eng](out=dst[:, half], in_=src[:, half])
+            copies[eng](
+                out=mixed["ac", unit][:].rearrange("p (m u e) j -> p u m j e", u=2, e=2)[:, :, quads],
+                in_=a_raw[unit][:].rearrange("p j (u m e) -> p u m j e", u=2, e=2)[:, :, quads],
+            )
 
         def ac_quant(unit, cols):
             key = ("ac", unit)
@@ -245,8 +241,7 @@ def tile_cross_layer_transcoder_s8_kernel(
 
         def c_out(G, b, eng):
             dst = out_1[512 * G : 512 * (G + 1), :] if G < 3 else out_2[512 * (G - 3) : 512 * (G - 2), :]
-            order = "(m u e) r -> e u m r" if G < GROUPS - 1 else "(m u e) r -> u e m r"
-            store(("c", G, b), dst.rearrange(order, u=2, e=2)[b // 2][b % 2], eng)
+            store(("c", G, b), dst[128 * b : 128 * (b + 1), :], eng)
 
         def y_tile(g, j):
             acc["y", g, j] = bank()
@@ -314,7 +309,7 @@ def tile_cross_layer_transcoder_s8_kernel(
 
         def p_ahalf(unit, e):
             parts["ac", unit, e] = [("amix", unit, e)]
-            vector_p.append((("amix", unit, e), [("a", unit, j) for j in range(4)], a_mix, (unit, "V", None, e)))
+            vector_p.append((("amix", unit, e), [("a", unit, j) for j in range(4)], a_mix, (unit, "V", slice(64 * e, 64 * (e + 1)))))
 
         def p_acq(unit, lo=0, hi=512):
             vector_p.append((("acq", unit, lo), parts["ac", unit] if hi - lo == 512 else parts["ac", unit, lo // 256], ac_quant, (unit, slice(lo, hi))))

@@ -20,6 +20,8 @@ FLOPS = 2 * (T * K * (F1 + F2) + T * (F1 + F2) * (N + R))
 GROUPS = 5
 HEAD_CUT = (336, 384)
 WARM = (2, 2)
+SH = 96
+VH = [(0, 1), (1, 1)]
 
 
 def tile_cross_layer_transcoder_s8_kernel(
@@ -399,49 +401,49 @@ def tile_cross_layer_transcoder_s8_kernel(
             p_turn_x(x); p_x_out(x, "S")
         p_mix((3, 0)); p_mix((3, 1)); p_quant((3, 0), "e", 6); p_quant((3, 1), "e", 6)
         unit_s((2, 0))
-        p_mix((4, 0)); p_mix((4, 1))
+        p_mix((4, 0))
         for x in X(1, 0):
             p_xq(x)
+        p_mix((4, 1)); p_quant((4, 0), "e", 6); p_mix(("d2", 0)); p_quant((4, 1), "e", 6)
         unit_s((2, 1))
-        p_quant((4, 0), "e", 6); p_quant((4, 1), "e", 6)
-        for x in X(1, 1):
-            p_sort(x)
         unit_s((3, 0))
+        for x in X(1, 1):
+            p_turn_x(x); p_x_out(x, "S")
         unit_s((4, 0))
-        p_mix(("d2", 0)); p_mix(("d2", 1)); p_quant(("d2", 0), "d2", 2); p_quant(("d2", 1), "d2", 2)
-        p_widen(0)
-        for x in X(1, 1):
-            p_turn_x(x, True); p_x_out(x, "VVVS"[x[2]])
-        for x in X(1, 1):
-            p_xq(x)
-        p_widen(1)
+        p_mix(("d2", 1)); p_quant(("d2", 0), "d2", 2); p_widen(0); p_quant(("d2", 1), "d2", 2); p_widen(1)
         for G in range(GROUPS):
             for h in range(2):
-                p_turn_a((G, 0), h); p_a_out((G, 0), h, "S")
+                p_turn_a((G, 0), h); p_a_out((G, 0), h, "V" if (G, h) in VH else "S")
+            if G == 1:
+                for x in X(1, 1):
+                    p_xq(x)
         unit_s((3, 1)); unit_s((4, 1))
         p_mix(("lab", 0))
         for G in range(GROUPS):
             p_quant(("ay", (G, 0)), "ay", 10)
         p_mix(("lab", 1)); p_quant(("lab", 0), "lab", 2)
-        p_amix((0, 0)); p_quant(("lab", 1), "lab", 2); p_amix((0, 1)); p_acq((0, 0)); p_amix((1, 0)); p_acq((0, 1))
+        p_amix((0, 0)); p_quant(("lab", 1), "lab", 2); p_amix((0, 1)); p_acq((0, 0)); p_acq((0, 1)); p_amix((1, 0))
         y_s(0, 0); y_s(0, 1)
-        p_amix((1, 1)); p_acq((1, 0))
-        for G in range(GROUPS):
+        for G in range(3):
             for h in range(2):
                 p_turn_a((G, 1), h); p_a_out((G, 1), h, "S")
-        y_s(0, 2); y_s(0, 3)
-        p_amix((2, 0)); p_acq((1, 1))
+        y_s(0, 2)
         c_group(0)
-        for G in range(GROUPS):
+        for G in range(3, 5):
+            for h in range(2):
+                p_turn_a((G, 1), h); p_a_out((G, 1), h, "S")
+        y_s(0, 3)
+        p_amix((1, 1)); p_acq((1, 0)); p_acq((1, 1))
+        for G in range(3):
             p_quant(("ay", (G, 1)), "ay", 10)
-        p_amix((2, 1)); p_acq((2, 0))
+        p_amix((2, 0)); p_quant(("ay", (3, 1)), "ay", 10); p_quant(("ay", (4, 1)), "ay", 10)
+        p_amix((2, 1)); p_acq((2, 0)); p_acq((2, 1)); p_amix((3, 0), "V", 0, SH); p_amix((3, 1), "V", 0, SH); p_acq((3, 0))
         c_group(1)
-        p_amix((3, 0)); p_acq((2, 1)); p_amix((3, 1)); p_acq((3, 0))
-        y_s(1, 0); y_s(1, 1)
+        p_amix((3, 0), "S", SH, P); y_s(1, 0); p_amix((3, 1), "S", SH, P); y_s(1, 1)
         c_group(2)
-        y_s(1, 2)
-        p_ahalf((4, 0), 0); p_acq((3, 1)); p_ahalf((4, 1), 0); p_acq((4, 0), 0, 256); p_ahalf((4, 0), 1); p_acq((4, 1), 0, 256)
+        p_acq((3, 1)); p_ahalf((4, 0), 0); p_ahalf((4, 1), 0); p_acq((4, 0), 0, 256); p_ahalf((4, 0), 1); p_acq((4, 1), 0, 256)
         p_ahalf((4, 1), 1); p_acq((4, 0), 256, 512); p_acq((4, 1), 256, 512)
+        y_s(1, 2)
         c_group(3)
         c_group(4)
         y_s(1, 3)

@@ -21,7 +21,7 @@ GROUPS = 5
 HEAD_CUT = (336, 384)
 WARM = (2, 2)
 SH = 96
-VH = [(0, 1), (1, 1)]
+VH = (0, 1)
 
 
 def tile_cross_layer_transcoder_s8_kernel(
@@ -374,7 +374,7 @@ def tile_cross_layer_transcoder_s8_kernel(
         for j in (2, 3):
             p_turn_x((0, 0, j)); p_x_out((0, 0, j), "S")
         p_s1(U0, 1, 0); p_s1(U0, 0, 1); p_s1(U0, 1, 1)
-        p_sort((0, 1, 0)); p_sort((0, 1, 1)); p_xq((0, 0, 2)); p_xq((0, 0, 3)); p_mix((1, 0)); p_sort((0, 1, 2));  p_sort((0, 1, 3))
+        p_sort((0, 1, 0)); p_sort((0, 1, 1)); p_xq((0, 0, 2)); p_xq((0, 0, 3)); p_mix((1, 0))
         p_relu(U0, 0, "S")
         for x in X(0, 1, (0, 1)):
             p_turn_x(x, True); p_x_out(x, "S")
@@ -383,7 +383,7 @@ def tile_cross_layer_transcoder_s8_kernel(
             p_s1(U0, j, 0); p_s1(U0, j, 1)
         p_relu(U0, 2, "S")
         for x in X(0, 1, (2, 3)):
-            p_turn_x(x, True); p_x_out(x, "S")
+            p_turn_x(x); p_x_out(x, "S")
         p_relu(U0, 3, "S")
         p_xq((0, 1, 0)); p_xq((0, 1, 1)); p_quant((1, 0), "e", 6); p_mix((1, 1)); p_xq((0, 1, 2)); p_xq((0, 1, 3)); p_quant((1, 1), "e", 6)
         for j in (0, 1):
@@ -407,16 +407,19 @@ def tile_cross_layer_transcoder_s8_kernel(
         p_mix((4, 1)); p_quant((4, 0), "e", 6); p_mix(("d2", 0)); p_quant((4, 1), "e", 6)
         unit_s((2, 1))
         unit_s((3, 0))
-        for x in X(1, 1):
-            p_turn_x(x); p_x_out(x, "S")
         unit_s((4, 0))
-        p_mix(("d2", 1)); p_quant(("d2", 0), "d2", 2); p_widen(0); p_quant(("d2", 1), "d2", 2); p_widen(1)
+        for x in X(1, 1):
+            p_sort(x)
+        p_mix(("d2", 1)); p_quant(("d2", 0), "d2", 2); p_quant(("d2", 1), "d2", 2)
+        for x in X(1, 1):
+            p_turn_x(x, True); p_x_out(x, "V" if x[2] in VH else "S")
+        p_widen(0)
+        for x in X(1, 1):
+            p_xq(x)
+        p_widen(1)
         for G in range(GROUPS):
             for h in range(2):
-                p_turn_a((G, 0), h); p_a_out((G, 0), h, "V" if (G, h) in VH else "S")
-            if G == 1:
-                for x in X(1, 1):
-                    p_xq(x)
+                p_turn_a((G, 0), h); p_a_out((G, 0), h, "S")
         unit_s((3, 1)); unit_s((4, 1))
         p_mix(("lab", 0))
         for G in range(GROUPS):

@@ -47,52 +47,45 @@ def tile_cross_layer_transcoder_s8_kernel(
 
         x_raw, rows, lab_raw = {}, {}, {}
 
-        def load_x(s, g, j):
-            t = tile([P, K], BF16, "x_raw", 8)
-            nc.sync.dma_start(out=t[:], in_=(x1, x2)[s].rearrange("(g p j) k -> g p j k", p=P, j=4)[g][:, j, :])
-            x_raw[s, g, j] = t[:]
+        def load_x(s, g, j, n):
+            t = tile([P, n, K], BF16, *(("x_t", 5) if n == 1 else ("x_raw", 4)))
+            nc.sync.dma_start(out=t[:], in_=(x1, x2)[s].rearrange("(g p j) k -> g p j k", p=P, j=4)[g][:, j : j + n, :])
+            for i in range(n):
+                x_raw[s, g, j + i] = t[:, i, :]
 
-        def load_rows(key, src, half, col):
-            t = tile([P, 4, 512], BF16, "rows", 5)
+        def load_rows(keys, src, half, col):
+            width = 512 * len(keys)
+            t = tile([P, 4, width], BF16, "rows", 4)
             nc.sync.dma_start(
-                out=t[:], in_=src.rearrange("(h p j) c -> h p j c", p=P, j=4)[half][:, :, col : col + 512]
+                out=t[:], in_=src.rearrange("(h p j) c -> h p j c", p=P, j=4)[half][:, :, col : col + width]
             )
-            rows[key, half] = t[:]
+            for i, key in enumerate(keys):
+                rows[key, half] = t[:, :, 512 * i : 512 * (i + 1)]
 
-        def load_e(G, q):
-            if G < 3:
-                load_rows(G, e1, q, 512 * G)
-            else:
-                load_rows(G, e2, q, 512 * (G - 3))
-
-        def load_xs(s, g, js):
-            for j in js:
-                load_x(s, g, j)
-
-        load_x(0, 0, 0)
-        load_e(0, 0)
-        load_x(0, 0, 1)
-        load_e(0, 1)
-        load_xs(0, 0, (2, 3))
-        load_xs(0, 1, (0, 1))
-        load_e(1, 0)
-        load_xs(0, 1, (2, 3))
-        load_e(1, 1)
-        load_e(2, 0)
-        load_e(2, 1)
-        load_xs(1, 0, range(4))
-        load_e(3, 0)
-        load_e(3, 1)
-        load_e(4, 0)
-        load_e(4, 1)
-        load_xs(1, 1, range(4))
-        load_rows("d2", d2, 0, 0)
-        load_rows("d2", d2, 1, 0)
+        load_x(0, 0, 0, 1)
+        load_rows([0], e1, 0, 0)
+        load_x(0, 0, 1, 1)
+        load_rows([0], e1, 1, 0)
+        load_x(0, 0, 2, 2)
+        load_x(0, 1, 0, 2)
+        load_rows([1], e1, 0, 512)
+        load_x(0, 1, 2, 2)
+        load_rows([1], e1, 1, 512)
+        load_rows([2], e1, 0, 1024)
+        load_rows([2], e1, 1, 1024)
+        load_rows([3, 4], e2, 0, 0)
+        load_x(1, 0, 0, 2)
+        load_x(1, 0, 2, 2)
+        load_rows([3, 4], e2, 1, 0)
         lab_sc = tile([P, 2, 4], F32, "lab_sc")
         nc.sync.dma_start(out=lab_sc[:], in_=labels_scale.rearrange("(g p j) o -> p g (j o)", p=P, j=4))
         for g in range(2):
             lab_raw[g] = tile([P, 4 * R], U8, "lab_raw", 2)
             nc.sync.dma_start(out=lab_raw[g][:], in_=labels_bytes.rearrange("(g p j) r -> g p (j r)", p=P, j=4)[g])
+        load_x(1, 1, 0, 2)
+        load_x(1, 1, 2, 2)
+        load_rows(["d2"], d2, 0, 0)
+        load_rows(["d2"], d2, 1, 0)
         d1_w = tile([P, 3, 1024], U8, "d1_w")
         nc.sync.dma_start(out=d1_w[:], in_=d1_words.rearrange("g p c -> p g c"))
         d1_si = d1_scales.bitcast(I32)
@@ -109,7 +102,7 @@ def tile_cross_layer_transcoder_s8_kernel(
         copies = {"S": scalar_copy, "V": vector_copy}
 
         def x_sort(x):
-            t = tile([P, 512], F32, "x_w", 4)
+            t = tile([P, 512], F32, "x_w", 2)
             vector_copy(
                 out=t[:].rearrange("p (q u m) -> p q u m", q=2, u=2),
                 in_=x_raw[x].bitcast(F32).rearrange("p (q m u) -> p q u m", q=2, u=2),
@@ -154,9 +147,12 @@ def tile_cross_layer_transcoder_s8_kernel(
                 out=codes[key][:].bitcast(E4M3X4), scales=scales[key][:], in_=mixed[key][:].rearrange("p c j -> p (c j)")
             )
 
-        def widen(g):
-            t = tile([P, 4, R], BF16, "mix", 4)
-            for j in range(4):
+        def widen(g, js):
+            if ("lab", g) not in rows:
+                wide = tile([P, 4, R], BF16, "rows", 4)
+                rows["lab", g] = wide[:]
+            t = rows["lab", g]
+            for j in js:
                 nc.vector.tensor_scalar(
                     out=t[:, j, :],
                     in0=lab_raw[g][:, j * R : (j + 1) * R].bitcast(E4M3),
@@ -164,7 +160,6 @@ def tile_cross_layer_transcoder_s8_kernel(
                     scalar2=None,
                     op0=ALU.mult,
                 )
-            rows["lab", g] = t[:]
 
         def mx(out, lhs_c, lhs_s, rhs_c, rhs_s, first, final):
             nc.tensor.matmul_mx(
@@ -199,8 +194,8 @@ def tile_cross_layer_transcoder_s8_kernel(
 
         def a_out(unit, h, eng):
             if ("ay", unit) not in mixed:
-                mixed["ay", unit] = tile([P, 512, 4], BF16, "a_t", 5)
-            dst = mixed["ay", unit][:].rearrange("p t f -> p (t f)").bitcast(F32)
+                mixed["ay", unit] = tile([P, 1024], F32, "a_t", 5)
+            dst = mixed["ay", unit][:]
             copies[eng](
                 out=dst[:, 512 * h : 512 * (h + 1)].rearrange("p (j t u) -> p j t u", j=2, u=2),
                 in_=a_b[unit, h][:].rearrange("p (j u t) -> p j t u", j=2, u=2),
@@ -225,13 +220,30 @@ def tile_cross_layer_transcoder_s8_kernel(
                 in_=mixed[key][:, cols, :].rearrange("p c j -> p (c j)"),
             )
 
-        stored = []
+        def ay_quant(unit, cols):
+            key = ("ay", unit)
+            if key not in codes:
+                codes[key] = tile([P, 512], U32, "ay_c", 10)
+                scales[key] = tile([P, 512], U8, "ay_s", 10)
+            nc.vector.quantize_mx(
+                out=codes[key][:, cols].bitcast(E4M3X4),
+                scales=scales[key][:, cols],
+                in_=mixed[key][:, 2 * cols.start : 2 * cols.stop].bitcast(BF16),
+            )
 
-        def store(key, dst, eng):
+        stored, staging = [], {}
+
+        def store(key, dst, eng, width=512):
             stored.append(dst)
-            o = tile([P, 512], F32, *[("x_raw", 8), ("x_t", 5)][len(stored) % 2])
-            copies[eng](out=o[:], in_=acc[key][:])
-            nc.sync.dma_start(out=dst, in_=o[:])
+            n = len(stored)
+            if n % 2:
+                o = tile([P, 512], F32, "x_t", 5)[:]
+            else:
+                if n % 4 == 2:
+                    staging["pair"] = tile([P, 2, 512], F32, "x_raw", 4)
+                o = staging["pair"][:, n // 2 % 2, :]
+            copies[eng](out=o[:, :width], in_=acc[key][:, :width])
+            nc.sync.dma_start(out=dst, in_=o[:, :width])
 
         def c_block(G, b):
             acc["c", G, b] = bank()
@@ -245,20 +257,20 @@ def tile_cross_layer_transcoder_s8_kernel(
             dst = out_1[512 * G : 512 * (G + 1), :] if G < 3 else out_2[512 * (G - 3) : 512 * (G - 2), :]
             store(("c", G, b), dst[128 * b : 128 * (b + 1), :], eng)
 
-        def y_tile(g, j):
-            acc["y", g, j] = bank()
+        def y_tile(g, j, lo=0, hi=512):
+            acc["y", g, j, lo] = bank()
             cols = slice(128 * j, 128 * (j + 1))
             for G in range(GROUPS):
                 key = ("ay", (G, g))
                 if G < 3:
-                    rhs_c, rhs_s = d1_w[:, G, :].bitcast(E2M1X4), d1_sc[:, G, :]
+                    rhs_c, rhs_s = d1_w[:, G, 2 * lo : 2 * hi].bitcast(E2M1X4), d1_sc[:, G, lo:hi]
                 else:
-                    rhs_c, rhs_s = codes["d2", G - 3][:].bitcast(E4M3X4), scales["d2", G - 3][:]
-                mx(acc["y", g, j][:], codes[key][:, cols].bitcast(E4M3X4), scales[key][:, cols], rhs_c, rhs_s,
+                    rhs_c, rhs_s = codes["d2", G - 3][:, lo:hi].bitcast(E4M3X4), scales["d2", G - 3][:, lo:hi]
+                mx(acc["y", g, j, lo][:, : hi - lo], codes[key][:, cols].bitcast(E4M3X4), scales[key][:, cols], rhs_c, rhs_s,
                    G == 0, G == GROUPS - 1)
 
-        def y_out(g, j, eng):
-            store(("y", g, j), out_0.rearrange("(g p j) n -> g j p n", p=P, j=4)[g][j], eng)
+        def y_out(g, j, eng, lo=0, hi=512):
+            store(("y", g, j, lo), out_0.rearrange("(g p j) n -> g j p n", p=P, j=4)[g][j][:, lo:hi], eng, hi - lo)
 
         def warm_up(count):
             for i in range(count):
@@ -289,8 +301,8 @@ def tile_cross_layer_transcoder_s8_kernel(
         def p_quant(key, tag, bufs):
             vector_p.append((("q", key), parts[key], quant, (key, tag, bufs)))
 
-        def p_widen(g):
-            vector_p.append((("wide", g), [], widen, (g,)))
+        def p_widen(g, js):
+            vector_p.append((("wide", g) if 3 in js else ("wide", g, 0), [], widen, (g, js)))
 
         def p_s1(unit, j, q):
             tensor_p.append((("s1", unit, j, q), [("xc", (unit[0] // 3, unit[1], j)), ("q", (unit[0], q))], stage1, (unit, j, q)))
@@ -318,18 +330,24 @@ def tile_cross_layer_transcoder_s8_kernel(
             for b in range(lo // P, hi // P):
                 parts["acb", unit, b] = ("acq", unit, lo)
 
+        def p_ayq(unit, js=range(4)):
+            needs = [("at", unit, h) for h in sorted({j // 2 for j in js})]
+            vector_p.append((("ayq", unit, js[0]), needs, ay_quant, (unit, slice(P * js[0], P * (js[-1] + 1)))))
+            for j in js:
+                parts["acb", ("y", unit), j] = ("ayq", unit, js[0])
+
         def p_c(G, b):
             tensor_p.append((("c", G, b), [("acb", (G, g), b) for g in range(2)] + [("q", ("lab", g)) for g in range(2)], c_block, (G, b)))
 
         def p_c_out(G, b, eng):
             prog[eng].append((("co", G, b), [("c", G, b)], c_out, (G, b, eng)))
 
-        def p_y(g, j):
-            needs = [("q", ("ay", (G, g))) for G in range(GROUPS)] + [("q", ("d2", q)) for q in range(2)]
-            tensor_p.append((("y", g, j), needs, y_tile, (g, j)))
+        def p_y(g, j, lo=0, hi=512):
+            needs = [("acb", ("y", (G, g)), j) for G in range(GROUPS)] + [("q", ("d2", q)) for q in range(2)]
+            tensor_p.append((("y", g, j, lo), needs, y_tile, (g, j, lo, hi)))
 
-        def p_y_out(g, j, eng):
-            prog[eng].append((("yo", g, j), [("y", g, j)], y_out, (g, j, eng)))
+        def p_y_out(g, j, eng, lo=0, hi=512):
+            prog[eng].append((("yo", g, j, lo), [("y", g, j, lo)], y_out, (g, j, eng, lo, hi)))
 
         def p_warm(n):
             tensor_p.append((("warm", len(tensor_p)), [], warm_up, (n,)))
@@ -353,14 +371,16 @@ def tile_cross_layer_transcoder_s8_kernel(
             for g in range(2):
                 p_acq((G, g))
 
-        def c_group(G, bs=range(4)):
+        def c_group(G, bs=range(4), eng="S"):
             for b in bs:
                 p_c(G, b)
-                p_c_out(G, b, "S")
+                if eng:
+                    p_c_out(G, b, eng)
 
-        def y_s(g, j):
-            p_y(g, j)
-            p_y_out(g, j, "S")
+        def y_s(g, j, eng="S", lo=0, hi=512):
+            p_y(g, j, lo, hi)
+            if eng:
+                p_y_out(g, j, eng, lo, hi)
 
         X = lambda s, g, js=range(4): [(s, g, j) for j in js]
         U0 = (0, 0)
@@ -395,61 +415,86 @@ def tile_cross_layer_transcoder_s8_kernel(
         for j in range(4):
             p_s1((1, 0), j, 1); p_relu((1, 0), j, "S")
 
+
+        def turn_x(xs, sort=(), on_v=()):
+            for x in xs:
+                p_turn_x(x, x[2] in sort)
+                if x[2] not in on_v:
+                    p_x_out(x, "S")
+
+        def turn_a(g, banks, on_v=()):
+            for G, h in banks:
+                p_turn_a((G, g), h)
+                if (G, h) not in on_v:
+                    p_a_out((G, g), h, "S")
+
+        def both(Gs):
+            return [(G, h) for G in Gs for h in range(2)]
+
+        SORT, XV, RV, AV = (0,), (), (2, 3), ()
         p_mix((2, 0)); p_mix((2, 1)); p_quant((2, 0), "e", 6); p_quant((2, 1), "e", 6)
         unit_s((1, 1))
-        for x in X(1, 0):
-            p_turn_x(x); p_x_out(x, "S")
-        p_mix((3, 0)); p_mix((3, 1)); p_quant((3, 0), "e", 6); p_quant((3, 1), "e", 6)
         unit_s((2, 0))
-        p_mix((4, 0))
-        for x in X(1, 0):
-            p_xq(x)
-        p_mix((4, 1)); p_quant((4, 0), "e", 6); p_mix(("d2", 0)); p_quant((4, 1), "e", 6)
+        SA = (0,)
+        turn_x(X(1, 0), SA)
+        p_mix((3, 0)); p_mix((4, 0))
+        for j in SA:
+            p_sort((1, 0, j))
+        p_quant((3, 0), "e", 6); p_quant((4, 0), "e", 6)
+        p_mix((3, 1)); p_mix((4, 1)); p_quant((3, 1), "e", 6)
+        p_xq((1, 0, 0)); p_xq((1, 0, 1)); p_quant((4, 1), "e", 6); p_xq((1, 0, 2)); p_widen(0, (0,)); p_xq((1, 0, 3))
+        for j in SORT:
+            p_sort((1, 1, j))
+        p_widen(0, (1, 2, 3))
         unit_s((2, 1))
-        unit_s((3, 0))
+        unit_s((3, 0), on_v=RV)
+        turn_x(X(1, 1), SORT, XV)
         unit_s((4, 0))
-        for x in X(1, 1):
-            p_sort(x)
-        p_mix(("d2", 1)); p_quant(("d2", 0), "d2", 2); p_quant(("d2", 1), "d2", 2)
-        for x in X(1, 1):
-            p_turn_x(x, True); p_x_out(x, "V" if x[2] in VH else "S")
-        p_widen(0)
+        for j in RV:
+            p_relu((3, 0), j, "V")
+        p_mix(("d2", 0)); p_widen(1, range(4))
+
+        for j in XV:
+            p_x_out((1, 1, j), "V")
+        turn_a(0, both(range(5)), AV)
+        p_mix(("d2", 1))
+        for G, h in AV:
+            p_a_out((G, 0), h, "V")
+        p_quant(("d2", 0), "d2", 2)
         for x in X(1, 1):
             p_xq(x)
-        p_widen(1)
-        for G in range(GROUPS):
-            for h in range(2):
-                p_turn_a((G, 0), h); p_a_out((G, 0), h, "S")
+        p_quant(("d2", 1), "d2", 2)
         unit_s((3, 1)); unit_s((4, 1))
-        p_mix(("lab", 0))
-        for G in range(GROUPS):
-            p_quant(("ay", (G, 0)), "ay", 10)
-        p_mix(("lab", 1)); p_quant(("lab", 0), "lab", 2)
-        p_amix((0, 0)); p_quant(("lab", 1), "lab", 2); p_amix((0, 1)); p_acq((0, 0)); p_acq((0, 1)); p_amix((1, 0))
+        p_mix(("lab", 0)); p_mix(("lab", 1)); p_ayq((0, 0)); p_ayq((1, 0)); p_ayq((2, 0)); p_quant(("lab", 0), "lab", 2); p_ayq((3, 0)); p_ayq((4, 0))
+        p_amix((0, 0)); p_quant(("lab", 1), "lab", 2); p_amix((0, 1)); p_acq((0, 0)); p_amix((1, 0)); p_acq((0, 1))
         y_s(0, 0); y_s(0, 1)
-        for G in range(3):
-            for h in range(2):
-                p_turn_a((G, 1), h); p_a_out((G, 1), h, "S")
+        turn_a(1, both(range(3)))
         y_s(0, 2)
         c_group(0)
-        for G in range(3, 5):
-            for h in range(2):
-                p_turn_a((G, 1), h); p_a_out((G, 1), h, "S")
         y_s(0, 3)
-        p_amix((1, 1)); p_acq((1, 0)); p_acq((1, 1))
-        for G in range(3):
-            p_quant(("ay", (G, 1)), "ay", 10)
-        p_amix((2, 0)); p_quant(("ay", (3, 1)), "ay", 10); p_quant(("ay", (4, 1)), "ay", 10)
-        p_amix((2, 1)); p_acq((2, 0)); p_acq((2, 1)); p_amix((3, 0), "V", 0, SH); p_amix((3, 1), "V", 0, SH); p_acq((3, 0))
+        p_amix((1, 1)); p_acq((1, 0)); p_amix((2, 0)); p_acq((1, 1))
         c_group(1)
-        p_amix((3, 0), "S", SH, P); y_s(1, 0); p_amix((3, 1), "S", SH, P); y_s(1, 1)
+        turn_a(1, [(G, h) for h in range(2) for G in (3, 4)], ((3, 0),))
+        p_amix((2, 1)); p_acq((2, 0)); p_ayq((0, 1), range(2)); p_acq((2, 1))
         c_group(2)
-        p_acq((3, 1)); p_ahalf((4, 0), 0); p_ahalf((4, 1), 0); p_acq((4, 0), 0, 256); p_ahalf((4, 0), 1); p_acq((4, 1), 0, 256)
-        p_ahalf((4, 1), 1); p_acq((4, 0), 256, 512); p_acq((4, 1), 256, 512)
-        y_s(1, 2)
+        for G in range(1, 3):
+            p_ayq((G, 1), range(0, 2))
+        p_amix((3, 0))
+        for G, h in ((3, 0),):
+            p_a_out((G, 1), h, "V")
+        p_amix((3, 1))
+        for G in range(3, 5):
+            p_ayq((G, 1), range(0, 2))
+        y_s(1, 0); y_s(1, 1)
+        p_acq((3, 0)); p_ahalf((4, 0), 0); p_acq((3, 1))
         c_group(3)
+        p_ahalf((4, 1), 0); p_acq((4, 0), 0, 256); p_ahalf((4, 0), 1); p_acq((4, 1), 0, 256)
+        p_ahalf((4, 1), 1); p_acq((4, 0), 256, 512); p_ayq((0, 1), range(2, 4)); p_acq((4, 1), 256, 512)
         c_group(4)
-        y_s(1, 3)
+        for G in range(1, 5):
+            p_ayq((G, 1), range(2, 4))
+        y_s(1, 2)
+        y_s(1, 3, "S", 0, 256); y_s(1, 3, "V", 256, 384); y_s(1, 3, "S", 384, 512)
 
         made = set()
         queues = [scalar_p, vector_p, tensor_p]

@@ -431,15 +431,16 @@ def tile_cross_layer_transcoder_s8_kernel(
         def both(Gs):
             return [(G, h) for G in Gs for h in range(2)]
 
-        SORT, XV, RV, AV = (0,), (), (2, 3), ()
+        SORT, XV, RV, AV = (0,), (), (3,), ()
         p_mix((2, 0)); p_mix((2, 1)); p_quant((2, 0), "e", 6); p_quant((2, 1), "e", 6)
         unit_s((1, 1))
         unit_s((2, 0))
-        SA = (0,)
+        SA = ()
         turn_x(X(1, 0), SA)
-        p_mix((3, 0)); p_mix((4, 0))
+        p_mix((3, 0))
         for j in SA:
             p_sort((1, 0, j))
+        p_mix((4, 0))
         p_quant((3, 0), "e", 6); p_quant((4, 0), "e", 6)
         p_mix((3, 1)); p_mix((4, 1)); p_quant((3, 1), "e", 6)
         p_xq((1, 0, 0)); p_xq((1, 0, 1)); p_quant((4, 1), "e", 6); p_xq((1, 0, 2)); p_widen(0, (0,)); p_xq((1, 0, 3))
@@ -465,7 +466,7 @@ def tile_cross_layer_transcoder_s8_kernel(
             p_xq(x)
         p_quant(("d2", 1), "d2", 2)
         unit_s((3, 1)); unit_s((4, 1))
-        p_mix(("lab", 0)); p_mix(("lab", 1)); p_ayq((0, 0)); p_ayq((1, 0)); p_ayq((2, 0)); p_quant(("lab", 0), "lab", 2); p_ayq((3, 0)); p_ayq((4, 0))
+        p_mix(("lab", 0)); p_ayq((0, 0)); p_ayq((1, 0)); p_mix(("lab", 1)); p_ayq((2, 0)); p_ayq((3, 0)); p_ayq((4, 0)); p_quant(("lab", 0), "lab", 2)
         p_amix((0, 0)); p_quant(("lab", 1), "lab", 2); p_amix((0, 1)); p_acq((0, 0)); p_amix((1, 0)); p_acq((0, 1))
         y_s(0, 0); y_s(0, 1)
         turn_a(1, both(range(3)))
@@ -474,27 +475,26 @@ def tile_cross_layer_transcoder_s8_kernel(
         y_s(0, 3)
         p_amix((1, 1)); p_acq((1, 0)); p_amix((2, 0)); p_acq((1, 1))
         c_group(1)
-        turn_a(1, [(G, h) for h in range(2) for G in (3, 4)], ((3, 0),))
+        turn_a(1, [(G, h) for h in range(2) for G in (3, 4)])
         p_amix((2, 1)); p_acq((2, 0)); p_ayq((0, 1), range(2)); p_acq((2, 1))
         c_group(2)
         for G in range(1, 3):
             p_ayq((G, 1), range(0, 2))
-        p_amix((3, 0))
-        for G, h in ((3, 0),):
-            p_a_out((G, 1), h, "V")
-        p_amix((3, 1))
+        p_amix((3, 0)); p_amix((3, 1))
         for G in range(3, 5):
             p_ayq((G, 1), range(0, 2))
         y_s(1, 0); y_s(1, 1)
         p_acq((3, 0)); p_ahalf((4, 0), 0); p_acq((3, 1))
         c_group(3)
         p_ahalf((4, 1), 0); p_acq((4, 0), 0, 256); p_ahalf((4, 0), 1); p_acq((4, 1), 0, 256)
-        p_ahalf((4, 1), 1); p_acq((4, 0), 256, 512); p_ayq((0, 1), range(2, 4)); p_acq((4, 1), 256, 512)
+        p_ahalf((4, 1), 1); p_acq((4, 0), 256, 512); p_ayq((0, 1), range(2, 3)); p_acq((4, 1), 256, 512)
         c_group(4)
         for G in range(1, 5):
-            p_ayq((G, 1), range(2, 4))
+            p_ayq((G, 1), range(2, 3))
+        for G in range(0, 5):
+            p_ayq((G, 1), range(3, 4))
         y_s(1, 2)
-        y_s(1, 3, "S", 0, 256); y_s(1, 3, "V", 256, 384); y_s(1, 3, "S", 384, 512)
+        y_s(1, 3, "S", 0, 256); y_s(1, 3, "V", 256, 512)
 
         made = set()
         queues = [scalar_p, vector_p, tensor_p]

@@ -16,19 +16,16 @@ ALU = mybir.AluOpType
 
 T, K, F1, F2, N, R = 1024, 1024, 1536, 1024, 512, 512
 P = 128
+W = 512
 FLOPS = 2 * (T * K * (F1 + F2) + T * (F1 + F2) * (N + R))
 GROUPS = 5
 HEAD_CUT = (336, 384)
-WARM = (2, 2)
-SH = 96
-VH = (0, 1)
 
 
 def tile_cross_layer_transcoder_s8_kernel(
     tc, x1, x2, e1, e2, d1_words, d1_scales, d2, labels_bytes, labels_scale, out_0, out_1, out_2
 ):
     nc = tc.nc
-    scalar_copy, vector_copy = nc.scalar.copy, nc.vector.tensor_copy
     with ExitStack() as ctx:
         pool = ctx.enter_context(tc.tile_pool(name="work", bufs=1))
         psum = ctx.enter_context(tc.psum_pool(name="psum", bufs=1))
@@ -38,29 +35,35 @@ def tile_cross_layer_transcoder_s8_kernel(
             return pool.tile(shape, dtype, name=tag, tag=tag, bufs=bufs, align_bytes=256)
 
         def bank():
-            return psum.tile([P, 512], F32, name="bank", tag="bank", bufs=8)
+            return psum.tile([P, W], F32, name="bank", tag="bank", bufs=8)
+
+        held = {}
+
+        def once(key, shape, dtype, tag, bufs):
+            if key not in held:
+                held[key] = tile(shape, dtype, tag, bufs)
+            return held[key]
 
         ident = tile([P, P], F32, "ident")
         make_identity(nc, ident[:])
-        d1_sc = tile([P, 3, 512], U8, "d1_sc")
+        d1_sc = tile([P, 3, N], U8, "d1_sc")
         nc.gpsimd.memset(d1_sc[:].rearrange("p g n -> p (g n)").bitcast(I32), 0)
 
-        x_raw, rows, lab_raw = {}, {}, {}
+        rows, lab_raw = {}, {}
 
-        def load_x(s, g, j, n):
-            t = tile([P, n, K], BF16, *(("x_t", 5) if n == 1 else ("x_raw", 4)))
-            nc.sync.dma_start(out=t[:], in_=(x1, x2)[s].rearrange("(g p j) k -> g p j k", p=P, j=4)[g][:, j : j + n, :])
-            for i in range(n):
-                x_raw[s, g, j + i] = t[:, i, :]
+        def x_raw(s, g, j, count=1):
+            return once(("x_raw", s, g, j // 2), [P, 2 * K], BF16, "x_raw", 4)[:, K * (j % 2) : K * (j % 2 + count)]
 
-        def load_rows(keys, src, half, col):
-            width = 512 * len(keys)
-            t = tile([P, 4, width], BF16, "rows", 4)
-            nc.sync.dma_start(
-                out=t[:], in_=src.rearrange("(h p j) c -> h p j c", p=P, j=4)[half][:, :, col : col + width]
-            )
-            for i, key in enumerate(keys):
-                rows[key, half] = t[:, :, 512 * i : 512 * (i + 1)]
+        def load_x(s, g, j, count):
+            src = (x1, x2)[s].rearrange("(g p j) k -> g p (j k)", p=P, j=4)[g]
+            nc.sync.dma_start(out=x_raw(s, g, j, count), in_=src[:, K * j : K * (j + count)])
+
+        def load_rows(names, src, half, col):
+            t = tile([P, 4, W * len(names)], BF16, "rows", 4)
+            src = src.rearrange("(h p j) c -> h p j c", p=P, j=4)[half]
+            nc.sync.dma_start(out=t[:], in_=src[:, :, col : col + W * len(names)])
+            for i, name in enumerate(names):
+                rows[name, half] = t[:, :, W * i : W * (i + 1)]
 
         load_x(0, 0, 0, 1)
         load_rows([0], e1, 0, 0)
@@ -68,11 +71,11 @@ def tile_cross_layer_transcoder_s8_kernel(
         load_rows([0], e1, 1, 0)
         load_x(0, 0, 2, 2)
         load_x(0, 1, 0, 2)
-        load_rows([1], e1, 0, 512)
+        load_rows([1], e1, 0, W)
         load_x(0, 1, 2, 2)
-        load_rows([1], e1, 1, 512)
-        load_rows([2], e1, 0, 1024)
-        load_rows([2], e1, 1, 1024)
+        load_rows([1], e1, 1, W)
+        load_rows([2], e1, 0, 2 * W)
+        load_rows([2], e1, 1, 2 * W)
         load_rows([3, 4], e2, 0, 0)
         load_x(1, 0, 0, 2)
         load_x(1, 0, 2, 2)
@@ -86,7 +89,7 @@ def tile_cross_layer_transcoder_s8_kernel(
         load_x(1, 1, 2, 2)
         load_rows(["d2"], d2, 0, 0)
         load_rows(["d2"], d2, 1, 0)
-        d1_w = tile([P, 3, 1024], U8, "d1_w")
+        d1_w = tile([P, 3, 2 * N], U8, "d1_w")
         nc.sync.dma_start(out=d1_w[:], in_=d1_words.rearrange("g p c -> p g c"))
         d1_si = d1_scales.bitcast(I32)
         d1_sv = d1_sc[:].rearrange("p g n -> p (g n)").bitcast(I32).rearrange("p (g n) -> p g n", g=3)
@@ -96,410 +99,354 @@ def tile_cross_layer_transcoder_s8_kernel(
                 in_=d1_si[:, 4 * quad : 4 * quad + 4, :].rearrange("g r n -> r g n"),
             )
 
-        x_c, x_s, x_b, x_t, x_w = {}, {}, {}, {}, {}
-        mixed, codes, scales = {}, {}, {}
-        a_raw, acc, a_b = {}, {}, {}
-        copies = {"S": scalar_copy, "V": vector_copy}
+        copies = {"S": nc.scalar.copy, "V": nc.vector.tensor_copy}
+        banks, x_sorted = {}, {}
+        programs = {"S": [], "V": [], "T": []}
+
+        def step(engine, makes, needs, function, *args):
+            programs[engine].append((makes, needs, function, args))
+
+        def quantise(key, tag, bufs, columns, values, lo, hi):
+            codes = once(("codes", key), [P, columns], U32, tag + "_c", bufs)
+            scales = once(("scales", key), [P, columns], U8, tag + "_s", bufs)
+            nc.vector.quantize_mx(out=codes[:, lo:hi].bitcast(E4M3X4), scales=scales[:, lo:hi], in_=values)
+
+        def operand(key, lo, hi):
+            return held["codes", key][:, lo:hi].bitcast(E4M3X4), held["scales", key][:, lo:hi]
+
+        def mx(out, stationary, moving, first, final):
+            nc.tensor.matmul_mx(
+                out=out,
+                lhsT=stationary[0],
+                lhsT_scale=stationary[1],
+                rhs=moving[0],
+                rhs_scale=moving[1],
+                start=first,
+                stop=final,
+            )
 
         def x_sort(x):
-            t = tile([P, 512], F32, "x_w", 2)
-            vector_copy(
-                out=t[:].rearrange("p (q u m) -> p q u m", q=2, u=2),
-                in_=x_raw[x].bitcast(F32).rearrange("p (q m u) -> p q u m", q=2, u=2),
-            )
-            x_w[x] = t
-
-        def x_turn(x):
-            x_b[x] = bank()
-            words = x_raw[x].bitcast(F32)
-            for q in range(2):
-                for u in range(2):
-                    i = 2 * q + u
-                    if x in x_w:
-                        src = x_w[x][:, i * P : (i + 1) * P]
-                    else:
-                        src = words[:, 256 * q + u : 256 * (q + 1) : 2]
-                    nc.tensor.transpose(x_b[x][:, i * P : (i + 1) * P], src, ident[:])
-
-        def x_out(x, eng):
-            x_t[x] = tile([P, 1024], BF16, "x_t", 5)
-            copies[eng](
-                out=x_t[x][:].bitcast(F32).rearrange("p (q t u) -> p q t u", q=2, u=2),
-                in_=x_b[x][:].rearrange("p (q u t) -> p q t u", q=2, u=2),
-            )
-
-        def x_quant(x):
-            x_c[x] = tile([P, 256], U32, "x_c", 16)
-            x_s[x] = tile([P, 256], U8, "x_s", 16)
-            nc.vector.quantize_mx(out=x_c[x][:].bitcast(E4M3X4), scales=x_s[x][:], in_=x_t[x][:])
-
-        def mix(key, eng, lo, hi):
-            if key not in mixed:
-                mixed[key] = tile([P, 512, 4], BF16, "mix", 4)
-            dst = mixed[key][:].rearrange("p (c i) j -> p c j i", i=2)
-            src = rows[key].rearrange("p j (c i) -> p c j i", i=2)
-            copies[eng](out=dst[:, lo // 2 : hi // 2], in_=src[:, lo // 2 : hi // 2])
-
-        def quant(key, tag, bufs):
-            codes[key] = tile([P, 512], U32, tag + "_c", bufs)
-            scales[key] = tile([P, 512], U8, tag + "_s", bufs)
-            nc.vector.quantize_mx(
-                out=codes[key][:].bitcast(E4M3X4), scales=scales[key][:], in_=mixed[key][:].rearrange("p c j -> p (c j)")
-            )
-
-        def widen(g, js):
-            if ("lab", g) not in rows:
-                wide = tile([P, 4, R], BF16, "rows", 4)
-                rows["lab", g] = wide[:]
-            t = rows["lab", g]
-            for j in js:
-                nc.vector.tensor_scalar(
-                    out=t[:, j, :],
-                    in0=lab_raw[g][:, j * R : (j + 1) * R].bitcast(E4M3),
-                    scalar1=lab_sc[:, g, j : j + 1],
-                    scalar2=None,
-                    op0=ALU.mult,
+            def run():
+                x_sorted[x] = tile([P, W], F32, "x_w", 2)
+                nc.vector.tensor_copy(
+                    out=x_sorted[x][:].rearrange("p (q u m) -> p q u m", q=2, u=2),
+                    in_=x_raw(*x).bitcast(F32).rearrange("p (q m u) -> p q u m", q=2, u=2),
                 )
 
-        def mx(out, lhs_c, lhs_s, rhs_c, rhs_s, first, final):
-            nc.tensor.matmul_mx(
-                out=out, lhsT=lhs_c, lhsT_scale=lhs_s, rhs=rhs_c, rhs_scale=rhs_s, start=first, stop=final
-            )
+            step("V", [("x_sorted", x)], [], run)
+
+        def x_turn(x, is_sorted=False):
+            def run():
+                banks[x] = bank()
+                words = x_raw(*x).bitcast(F32)
+                for q in range(2):
+                    for u in range(2):
+                        i = 2 * q + u
+                        src = x_sorted[x][:, i * P : (i + 1) * P] if is_sorted else words[:, 256 * q + u : 256 * (q + 1) : 2]
+                        nc.tensor.transpose(banks[x][:, i * P : (i + 1) * P], src, ident[:])
+
+            step("T", [("x_bank", x)], [("x_sorted", x)] if is_sorted else [], run)
+
+        def x_turned(s, g, j, count=1):
+            return once(("x_t", s, g, j // 2), [P, 2 * W], F32, "x_t", 3)[:, W * (j % 2) : W * (j % 2 + count)]
+
+        def x_out(x, engine="S"):
+            def run():
+                copies[engine](
+                    out=x_turned(*x).rearrange("p (q t u) -> p q t u", q=2, u=2),
+                    in_=banks[x][:].rearrange("p (q u t) -> p q t u", q=2, u=2),
+                )
+
+            step(engine, [("x_t", x)], [("x_bank", x)], run)
+
+        def x_quant(s, g, j, count):
+            def run():
+                lo = 256 * (j % 2)
+                values = x_turned(s, g, j, count).bitcast(BF16)
+                quantise(("x", s, g, j // 2), "x", 8, W, values, lo, lo + 256 * count)
+
+            xs = [(s, g, j + i) for i in range(count)]
+            step("V", [("x_q", x) for x in xs], [("x_t", x) for x in xs], run)
+
+        pairs = [((G, 0), (G, 1)) for G in range(3)] + [((3, q), (4, q)) for q in range(2)]
+        pairs = pairs + [((name, 0), (name, 1)) for name in ("d2", "lab")]
+        pairs = pairs + [(("c", G, 0), ("c", G, 1)) for G in range(GROUPS)]
+        place = {key: (pair, i) for pair in pairs for i, key in enumerate(pair)}
+        parts = {}
+
+        def mixed(key, count=1):
+            pair, i = place[key]
+            return once(("mixed", pair), [P, 8 * W], BF16, "mixed", 2)[:, 4 * W * i : 4 * W * (i + count)]
+
+        def mix(key, engine="V", lo=0, hi=W):
+            def run():
+                dst = mixed(key).rearrange("p (c i j) -> p c j i", i=2, j=4)
+                src = rows[key].rearrange("p j (c i) -> p c j i", i=2)
+                copies[engine](out=dst[:, lo // 2 : hi // 2], in_=src[:, lo // 2 : hi // 2])
+
+            parts.setdefault(key, []).append((lo, hi))
+            step(engine, [("mixed", key, lo)], [("wide", key[1], j) for j in range(4)] if key[0] == "lab" else [], run)
+
+        def quant(keys, lo=0, hi=W):
+            pair, i = place[keys[0]]
+            tag, bufs = ("a_c", 3) if keys[0][0] == "c" else ("w", 2) if keys[0][0] in ("d2", "lab") else ("e", 3)
+            end = hi + W * (len(keys) - 1)
+
+            def run():
+                values = mixed(keys[0], len(keys))[:, 4 * lo : 4 * end]
+                quantise(pair, tag, bufs, 2 * W, values, W * i + lo, W * i + end)
+
+            makes = [("q", key, b) for key in keys for b in range(lo // P, hi // P)]
+            needs = [("mixed", key, a) for key in keys for a, b in parts[key] if a < hi and lo < b]
+            step("V", makes, needs, run)
+
+        def quantised(key, lo=0, hi=W):
+            pair, i = place[key]
+            return operand(pair, W * i + lo, W * i + hi)
+
+        def whole(key):
+            return [("q", key, b) for b in range(4)]
+
+        def widen(g, js, engine="V"):
+            def run(j):
+                wide = once(("wide", g), [P, 4, R], BF16, "rows", 4)
+                rows["lab", g] = wide[:]
+                src = lab_raw[g][:, j * R : (j + 1) * R].bitcast(E4M3)
+                if engine == "S":
+                    nc.scalar.activation(out=wide[:, j, :], in_=src, func=ACT.Copy, scale=lab_sc[:, g, j : j + 1])
+                else:
+                    nc.vector.tensor_scalar(
+                        out=wide[:, j, :], in0=src, scalar1=lab_sc[:, g, j : j + 1], scalar2=None, op0=ALU.mult
+                    )
+
+            for j in js:
+                step(engine, [("wide", g, j)], [], run, j)
+
+        def features(unit):
+            return once(("a", unit), [P, 4, W], BF16, "a", 2 * GROUPS)
 
         def stage1(unit, j, q):
             G, g = unit
-            x = (0 if G < 3 else 1, g, j)
-            if q == 0:
-                acc[unit, j] = bank()
-            cols = slice(128 * q, 128 * (q + 1))
-            mx(acc[unit, j][:], x_c[x][:, cols].bitcast(E4M3X4), x_s[x][:, cols],
-               codes[G, q][:].bitcast(E4M3X4), scales[G, q][:], q == 0, q == 1)
+            s = G // 3
 
-        def relu(unit, j, eng):
-            if unit not in a_raw:
-                a_raw[unit] = tile([P, 4, 512], BF16, "a", 10)
-            dst = a_raw[unit][:, j, :].rearrange("p (u m e) -> p u m e", u=2, e=2)
-            src = acc[unit, j][:].rearrange("p (m u e) -> p u m e", u=2, e=2)
-            if eng == "S":
-                nc.scalar.activation(out=dst, in_=src, func=ACT.Relu)
-            else:
-                nc.vector.tensor_scalar(out=dst, in0=src, scalar1=0.0, scalar2=None, op0=ALU.max)
+            def run():
+                if q == 0:
+                    banks[unit, j] = bank()
+                lo = 256 * (j % 2) + P * q
+                mx(banks[unit, j][:], operand(("x", s, g, j // 2), lo, lo + P), quantised((G, q)), q == 0, q == 1)
+
+            step("T", [("s1", unit, j, q)], [("x_q", (s, g, j))] + whole((G, q)), run)
+
+        def relu(unit, j, engine="S"):
+            def run():
+                dst = features(unit)[:, j, :].rearrange("p (u m e) -> p u m e", u=2, e=2)
+                src = banks[unit, j][:].rearrange("p (m u e) -> p u m e", u=2, e=2)
+                if engine == "S":
+                    nc.scalar.activation(out=dst, in_=src, func=ACT.Relu)
+                else:
+                    nc.vector.tensor_scalar(out=dst, in0=src, scalar1=0.0, scalar2=None, op0=ALU.max)
+
+            step(engine, [("a", unit, j)], [("s1", unit, j, 1)], run)
 
         def a_turn(unit, h):
-            words = a_raw[unit][:].rearrange("p j f -> p (j f)").bitcast(F32)
-            a_b[unit, h] = bank()
-            for i in range(4):
-                col = 512 * h + 128 * i
-                nc.tensor.transpose(a_b[unit, h][:, i * P : (i + 1) * P], words[:, col : col + P], ident[:])
+            def run():
+                words = features(unit)[:].rearrange("p j f -> p (j f)").bitcast(F32)
+                banks["a", unit, h] = bank()
+                for i in range(4):
+                    col = W * h + P * i
+                    nc.tensor.transpose(banks["a", unit, h][:, i * P : (i + 1) * P], words[:, col : col + P], ident[:])
 
-        def a_out(unit, h, eng):
-            if ("ay", unit) not in mixed:
-                mixed["ay", unit] = tile([P, 1024], F32, "a_t", 5)
-            dst = mixed["ay", unit][:]
-            copies[eng](
-                out=dst[:, 512 * h : 512 * (h + 1)].rearrange("p (j t u) -> p j t u", j=2, u=2),
-                in_=a_b[unit, h][:].rearrange("p (j u t) -> p j t u", j=2, u=2),
-            )
+            step("T", [("a_bank", unit, h)], [("a", unit, 2 * h), ("a", unit, 2 * h + 1)], run)
 
-        def a_mix(unit, eng, quads):
-            if ("ac", unit) not in mixed:
-                mixed["ac", unit] = tile([P, 512, 4], BF16, "mix", 4)
-            copies[eng](
-                out=mixed["ac", unit][:].rearrange("p (m u e) j -> p u m j e", u=2, e=2)[:, :, quads],
-                in_=a_raw[unit][:].rearrange("p j (u m e) -> p u m j e", u=2, e=2)[:, :, quads],
-            )
+        def a_turned(g, h):
+            return once(("a_t", g, h), [P, GROUPS * W], F32, "a_t", 2)
 
-        def ac_quant(unit, cols):
-            key = ("ac", unit)
-            if key not in codes:
-                codes[key] = tile([P, 512], U32, "ac_c", 6)
-                scales[key] = tile([P, 512], U8, "ac_s", 6)
-            nc.vector.quantize_mx(
-                out=codes[key][:, cols].bitcast(E4M3X4),
-                scales=scales[key][:, cols],
-                in_=mixed[key][:, cols, :].rearrange("p c j -> p (c j)"),
-            )
+        def a_out(unit, h, engine="S"):
+            G, g = unit
 
-        def ay_quant(unit, cols):
-            key = ("ay", unit)
-            if key not in codes:
-                codes[key] = tile([P, 512], U32, "ay_c", 10)
-                scales[key] = tile([P, 512], U8, "ay_s", 10)
-            nc.vector.quantize_mx(
-                out=codes[key][:, cols].bitcast(E4M3X4),
-                scales=scales[key][:, cols],
-                in_=mixed[key][:, 2 * cols.start : 2 * cols.stop].bitcast(BF16),
-            )
+            def run():
+                copies[engine](
+                    out=a_turned(g, h)[:, W * G : W * (G + 1)].rearrange("p (j t u) -> p j t u", j=2, u=2),
+                    in_=banks["a", unit, h][:].rearrange("p (j u t) -> p j t u", j=2, u=2),
+                )
 
-        stored, staging = [], {}
+            step(engine, [("a_t", unit, h)], [("a_bank", unit, h)], run)
 
-        def store(key, dst, eng, width=512):
-            stored.append(dst)
-            n = len(stored)
-            if n % 2:
-                o = tile([P, 512], F32, "x_t", 5)[:]
-            else:
-                if n % 4 == 2:
-                    staging["pair"] = tile([P, 2, 512], F32, "x_raw", 4)
-                o = staging["pair"][:, n // 2 % 2, :]
-            copies[eng](out=o[:, :width], in_=acc[key][:, :width])
-            nc.sync.dma_start(out=dst, in_=o[:, :width])
+        def ay_quant(g, h, lo, hi):
+            def run():
+                values = a_turned(g, h)[:, W * lo : W * hi].bitcast(BF16)
+                quantise(("y", g, h), "a_y", 4, GROUPS * 256, values, 256 * lo, 256 * hi)
 
-        def c_block(G, b):
-            acc["c", G, b] = bank()
-            cols = slice(128 * b, 128 * (b + 1))
-            for g in range(2):
-                key = ("ac", (G, g))
-                mx(acc["c", G, b][:], codes[key][:, cols].bitcast(E4M3X4), scales[key][:, cols],
-                   codes["lab", g][:].bitcast(E4M3X4), scales["lab", g][:], g == 0, g == 1)
+            step("V", [("y_q", G, g, h) for G in range(lo, hi)], [("a_t", (G, g), h) for G in range(lo, hi)], run)
 
-        def c_out(G, b, eng):
-            dst = out_1[512 * G : 512 * (G + 1), :] if G < 3 else out_2[512 * (G - 3) : 512 * (G - 2), :]
-            store(("c", G, b), dst[128 * b : 128 * (b + 1), :], eng)
+        def a_mix(unit, engine="V", lo=0, hi=W):
+            key = ("c",) + unit
 
-        def y_tile(g, j, lo=0, hi=512):
-            acc["y", g, j, lo] = bank()
-            cols = slice(128 * j, 128 * (j + 1))
-            for G in range(GROUPS):
-                key = ("ay", (G, g))
-                if G < 3:
-                    rhs_c, rhs_s = d1_w[:, G, 2 * lo : 2 * hi].bitcast(E2M1X4), d1_sc[:, G, lo:hi]
-                else:
-                    rhs_c, rhs_s = codes["d2", G - 3][:, lo:hi].bitcast(E4M3X4), scales["d2", G - 3][:, lo:hi]
-                mx(acc["y", g, j, lo][:, : hi - lo], codes[key][:, cols].bitcast(E4M3X4), scales[key][:, cols], rhs_c, rhs_s,
-                   G == 0, G == GROUPS - 1)
+            def run():
+                quads = slice(lo // 4, hi // 4)
+                copies[engine](
+                    out=mixed(key).rearrange("p (m u e j) -> p u m j e", u=2, e=2, j=4)[:, :, quads],
+                    in_=features(unit)[:].rearrange("p j (u m e) -> p u m j e", u=2, e=2)[:, :, quads],
+                )
 
-        def y_out(g, j, eng, lo=0, hi=512):
-            store(("y", g, j, lo), out_0.rearrange("(g p j) n -> g j p n", p=P, j=4)[g][j][:, lo:hi], eng, hi - lo)
+            parts.setdefault(key, []).append((lo, hi))
+            step(engine, [("mixed", key, lo)], [("a", unit, j) for j in range(4)], run)
+
+        stored = []
+        staging = [("x_raw", 4, 2, 0), ("x_t", 3, 2, 8), ("rows", 4, 4, 14)]
+
+        def store(key, dst, engine, width):
+            def run():
+                n = len(stored)
+                stored.append(key)
+                tag, bufs, banks_held, first = [place for place in staging if place[3] <= n][-1]
+                group, i = divmod(n - first, banks_held)
+                staged = once(("staged", tag, group), [P, banks_held * W], F32, tag, bufs)[:, W * i : W * i + width]
+                copies[engine](out=staged, in_=banks[key][:, :width])
+                nc.sync.dma_start(out=dst, in_=staged)
+
+            step(engine, [("stored", key)], [key], run)
+
+        def c_block(G, b, engine="S"):
+            def run():
+                banks["c", G, b] = bank()
+                for g in range(2):
+                    lhs = quantised(("c", G, g), P * b, P * (b + 1))
+                    mx(banks["c", G, b][:], lhs, quantised(("lab", g)), g == 0, g == 1)
+
+            needs = [("q", ("c", G, g), b) for g in range(2)] + whole(("lab", 0)) + whole(("lab", 1))
+            step("T", [("c", G, b)], needs, run)
+            dst = out_1[W * G : W * (G + 1), :] if G < 3 else out_2[W * (G - 3) : W * (G - 2), :]
+            store(("c", G, b), dst[P * b : P * (b + 1), :], engine, R)
+
+        def y_tile(g, j, engine="S", lo=0, hi=N):
+            def run():
+                banks["y", g, j, lo] = bank()
+                for G in range(GROUPS):
+                    col = 256 * G + P * (j % 2)
+                    if G < 3:
+                        rhs = d1_w[:, G, 2 * lo : 2 * hi].bitcast(E2M1X4), d1_sc[:, G, lo:hi]
+                    else:
+                        rhs = quantised(("d2", G - 3), lo, hi)
+                    lhs = operand(("y", g, j // 2), col, col + P)
+                    mx(banks["y", g, j, lo][:, : hi - lo], lhs, rhs, G == 0, G == GROUPS - 1)
+
+            needs = [("y_q", G, g, j // 2) for G in range(GROUPS)] + whole(("d2", 0)) + whole(("d2", 1))
+            step("T", [("y", g, j, lo)], needs, run)
+            dst = out_0.rearrange("(g p j) n -> g j p n", p=P, j=4)[g][j][:, lo:hi]
+            store(("y", g, j, lo), dst, engine, hi - lo)
 
         def warm_up(count):
-            for i in range(count):
+            def run():
                 unread = bank()
-                first = x_raw[0, 0, 0]
-                nc.tensor.matmul(unread[:], lhsT=first[:, :P], rhs=first[:, :512], start=True, stop=True)
+                first = x_raw(0, 0, 0)
+                nc.tensor.matmul(unread[:], lhsT=first[:, :P], rhs=first[:, :W], start=True, stop=True)
 
-        tensor_p, scalar_p, vector_p = [], [], []
-        prog = {"S": scalar_p, "V": vector_p}
-        parts = {}
+            for i in range(count):
+                step("T", [], [], run)
 
-        def p_sort(x):
-            vector_p.append((("xw", x), [], x_sort, (x,)))
-
-        def p_turn_x(x, sort=False):
-            tensor_p.append((("xb", x), [("xw", x)] if sort else [], x_turn, (x,)))
-
-        def p_x_out(x, eng):
-            prog[eng].append((("xt", x), [("xb", x)], x_out, (x, eng)))
-
-        def p_xq(x):
-            vector_p.append((("xc", x), [("xt", x)], x_quant, (x,)))
-
-        def p_mix(key, eng="V", lo=0, hi=512):
-            parts.setdefault(key, []).append(("mix", key, lo))
-            prog[eng].append((("mix", key, lo), [("wide", key[1])] if key[0] == "lab" else [], mix, (key, eng, lo, hi)))
-
-        def p_quant(key, tag, bufs):
-            vector_p.append((("q", key), parts[key], quant, (key, tag, bufs)))
-
-        def p_widen(g, js):
-            vector_p.append((("wide", g) if 3 in js else ("wide", g, 0), [], widen, (g, js)))
-
-        def p_s1(unit, j, q):
-            tensor_p.append((("s1", unit, j, q), [("xc", (unit[0] // 3, unit[1], j)), ("q", (unit[0], q))], stage1, (unit, j, q)))
-
-        def p_relu(unit, j, eng):
-            prog[eng].append((("a", unit, j), [("s1", unit, j, 1)], relu, (unit, j, eng)))
-
-        def p_turn_a(unit, h):
-            tensor_p.append((("ab", unit, h), [("a", unit, 2 * h), ("a", unit, 2 * h + 1)], a_turn, (unit, h)))
-
-        def p_a_out(unit, h, eng):
-            parts.setdefault(("ay", unit), []).append(("at", unit, h))
-            prog[eng].append((("at", unit, h), [("ab", unit, h)], a_out, (unit, h, eng)))
-
-        def p_amix(unit, eng="V", lo=0, hi=P):
-            parts.setdefault(("ac", unit), []).append(("amix", unit, lo))
-            prog[eng].append((("amix", unit, lo), [("a", unit, j) for j in range(4)], a_mix, (unit, eng, slice(lo, hi))))
-
-        def p_ahalf(unit, e):
-            parts["ac", unit, e] = [("amix", unit, e)]
-            vector_p.append((("amix", unit, e), [("a", unit, j) for j in range(4)], a_mix, (unit, "V", slice(64 * e, 64 * (e + 1)))))
-
-        def p_acq(unit, lo=0, hi=512):
-            vector_p.append((("acq", unit, lo), parts["ac", unit] if hi - lo == 512 else parts["ac", unit, lo // 256], ac_quant, (unit, slice(lo, hi))))
-            for b in range(lo // P, hi // P):
-                parts["acb", unit, b] = ("acq", unit, lo)
-
-        def p_ayq(unit, js=range(4)):
-            needs = [("at", unit, h) for h in sorted({j // 2 for j in js})]
-            vector_p.append((("ayq", unit, js[0]), needs, ay_quant, (unit, slice(P * js[0], P * (js[-1] + 1)))))
+        def unit_banks(unit, js=range(4), on_vector=()):
             for j in js:
-                parts["acb", ("y", unit), j] = ("ayq", unit, js[0])
+                stage1(unit, j, 0)
+                stage1(unit, j, 1)
+                if j not in on_vector:
+                    relu(unit, j)
 
-        def p_c(G, b):
-            tensor_p.append((("c", G, b), [("acb", (G, g), b) for g in range(2)] + [("q", ("lab", g)) for g in range(2)], c_block, (G, b)))
+        def x_run(s, g, js, are_sorted=()):
+            for j in js:
+                x_turn((s, g, j), j in are_sorted)
+                x_out((s, g, j))
 
-        def p_c_out(G, b, eng):
-            prog[eng].append((("co", G, b), [("c", G, b)], c_out, (G, b, eng)))
+        def a_run(g, unit_halves):
+            for G, h in unit_halves:
+                a_turn((G, g), h)
+                a_out((G, g), h)
 
-        def p_y(g, j, lo=0, hi=512):
-            needs = [("acb", ("y", (G, g)), j) for G in range(GROUPS)] + [("q", ("d2", q)) for q in range(2)]
-            tensor_p.append((("y", g, j, lo), needs, y_tile, (g, j, lo, hi)))
+        def c_group(G):
+            for b in range(4):
+                c_block(G, b)
 
-        def p_y_out(g, j, eng, lo=0, hi=512):
-            prog[eng].append((("yo", g, j, lo), [("y", g, j, lo)], y_out, (g, j, eng, lo, hi)))
 
-        def p_warm(n):
-            tensor_p.append((("warm", len(tensor_p)), [], warm_up, (n,)))
-
-        def unit_s(unit, on_v=()):
-            for j in range(4):
-                p_s1(unit, j, 0)
-                p_s1(unit, j, 1)
-                if j not in on_v:
-                    p_relu(unit, j, "S")
-
-        def e_group(G, tag="e", bufs=6):
-            for q in range(2):
-                p_mix((G, q))
-            for q in range(2):
-                p_quant((G, q), tag, bufs)
-
-        def ac_group(G):
-            for g in range(2):
-                p_amix((G, g))
-            for g in range(2):
-                p_acq((G, g))
-
-        def c_group(G, bs=range(4), eng="S"):
-            for b in bs:
-                p_c(G, b)
-                if eng:
-                    p_c_out(G, b, eng)
-
-        def y_s(g, j, eng="S", lo=0, hi=512):
-            p_y(g, j, lo, hi)
-            if eng:
-                p_y_out(g, j, eng, lo, hi)
-
-        X = lambda s, g, js=range(4): [(s, g, j) for j in js]
-        U0 = (0, 0)
-        p_turn_x((0, 0, 0)); p_warm(WARM[0]); p_mix((0, 0), "V", 0, HEAD_CUT[0]); p_mix((0, 0), "S", HEAD_CUT[0], 512)
-        p_x_out((0, 0, 0), "S"); p_quant((0, 0), "e", 6)
-        p_turn_x((0, 0, 1)); p_warm(WARM[1]); p_xq((0, 0, 0))
-        p_x_out((0, 0, 1), "S")
-        p_mix((0, 1), "V", 0, HEAD_CUT[1]); p_mix((0, 1), "S", HEAD_CUT[1], 512)
-        p_xq((0, 0, 1)); p_quant((0, 1), "e", 6)
-        p_s1(U0, 0, 0)
+        x_turn((0, 0, 0)); warm_up(2)
+        mix((0, 0), "V", 0, HEAD_CUT[0]); mix((0, 0), "S", HEAD_CUT[0], W)
+        x_out((0, 0, 0)); quant([(0, 0)])
+        x_turn((0, 0, 1)); warm_up(2); x_quant(0, 0, 0, 1)
+        x_out((0, 0, 1))
+        mix((0, 1), "V", 0, HEAD_CUT[1]); mix((0, 1), "S", HEAD_CUT[1], W)
+        x_quant(0, 0, 1, 1); quant([(0, 1)])
+        stage1((0, 0), 0, 0)
+        x_run(0, 0, (2, 3))
+        stage1((0, 0), 1, 0); stage1((0, 0), 0, 1); stage1((0, 0), 1, 1)
+        x_sort((0, 1, 0)); x_sort((0, 1, 1)); x_quant(0, 0, 2, 1); x_quant(0, 0, 3, 1); mix((1, 0))
+        relu((0, 0), 0)
+        x_run(0, 1, (0, 1), (0, 1))
+        relu((0, 0), 1)
         for j in (2, 3):
-            p_turn_x((0, 0, j)); p_x_out((0, 0, j), "S")
-        p_s1(U0, 1, 0); p_s1(U0, 0, 1); p_s1(U0, 1, 1)
-        p_sort((0, 1, 0)); p_sort((0, 1, 1)); p_xq((0, 0, 2)); p_xq((0, 0, 3)); p_mix((1, 0))
-        p_relu(U0, 0, "S")
-        for x in X(0, 1, (0, 1)):
-            p_turn_x(x, True); p_x_out(x, "S")
-        p_relu(U0, 1, "S")
-        for j in (2, 3):
-            p_s1(U0, j, 0); p_s1(U0, j, 1)
-        p_relu(U0, 2, "S")
-        for x in X(0, 1, (2, 3)):
-            p_turn_x(x); p_x_out(x, "S")
-        p_relu(U0, 3, "S")
-        p_xq((0, 1, 0)); p_xq((0, 1, 1)); p_quant((1, 0), "e", 6); p_mix((1, 1)); p_xq((0, 1, 2)); p_xq((0, 1, 3)); p_quant((1, 1), "e", 6)
-        for j in (0, 1):
-            p_s1((0, 1), j, 0); p_s1((0, 1), j, 1); p_relu((0, 1), j, "S")
+            stage1((0, 0), j, 0); stage1((0, 0), j, 1)
+        relu((0, 0), 2)
+        x_run(0, 1, (2, 3))
+        relu((0, 0), 3)
+        x_quant(0, 1, 0, 1); x_quant(0, 1, 1, 1); quant([(1, 0)]); mix((1, 1)); x_quant(0, 1, 2, 1); x_quant(0, 1, 3, 1); quant([(1, 1)])
+        unit_banks((0, 1), (0, 1))
         for j in range(4):
-            p_s1((1, 0), j, 0)
-        for j in (2, 3):
-            p_s1((0, 1), j, 0); p_s1((0, 1), j, 1); p_relu((0, 1), j, "S")
+            stage1((1, 0), j, 0)
+        unit_banks((0, 1), (2, 3))
         for j in range(4):
-            p_s1((1, 0), j, 1); p_relu((1, 0), j, "S")
+            stage1((1, 0), j, 1); relu((1, 0), j)
 
-
-        def turn_x(xs, sort=(), on_v=()):
-            for x in xs:
-                p_turn_x(x, x[2] in sort)
-                if x[2] not in on_v:
-                    p_x_out(x, "S")
-
-        def turn_a(g, banks, on_v=()):
-            for G, h in banks:
-                p_turn_a((G, g), h)
-                if (G, h) not in on_v:
-                    p_a_out((G, g), h, "S")
-
-        def both(Gs):
-            return [(G, h) for G in Gs for h in range(2)]
-
-        SORT, XV, RV, AV = (0,), (), (3,), ()
-        p_mix((2, 0)); p_mix((2, 1)); p_quant((2, 0), "e", 6); p_quant((2, 1), "e", 6)
-        unit_s((1, 1))
-        unit_s((2, 0))
-        SA = ()
-        turn_x(X(1, 0), SA)
-        p_mix((3, 0))
-        for j in SA:
-            p_sort((1, 0, j))
-        p_mix((4, 0))
-        p_quant((3, 0), "e", 6); p_quant((4, 0), "e", 6)
-        p_mix((3, 1)); p_mix((4, 1)); p_quant((3, 1), "e", 6)
-        p_xq((1, 0, 0)); p_xq((1, 0, 1)); p_quant((4, 1), "e", 6); p_xq((1, 0, 2)); p_widen(0, (0,)); p_xq((1, 0, 3))
-        for j in SORT:
-            p_sort((1, 1, j))
-        p_widen(0, (1, 2, 3))
-        unit_s((2, 1))
-        unit_s((3, 0), on_v=RV)
-        turn_x(X(1, 1), SORT, XV)
-        unit_s((4, 0))
-        for j in RV:
-            p_relu((3, 0), j, "V")
-        p_mix(("d2", 0)); p_widen(1, range(4))
-
-        for j in XV:
-            p_x_out((1, 1, j), "V")
-        turn_a(0, both(range(5)), AV)
-        p_mix(("d2", 1))
-        for G, h in AV:
-            p_a_out((G, 0), h, "V")
-        p_quant(("d2", 0), "d2", 2)
-        for x in X(1, 1):
-            p_xq(x)
-        p_quant(("d2", 1), "d2", 2)
-        unit_s((3, 1)); unit_s((4, 1))
-        p_mix(("lab", 0)); p_ayq((0, 0)); p_ayq((1, 0)); p_mix(("lab", 1)); p_ayq((2, 0)); p_ayq((3, 0)); p_ayq((4, 0)); p_quant(("lab", 0), "lab", 2)
-        p_amix((0, 0)); p_quant(("lab", 1), "lab", 2); p_amix((0, 1)); p_acq((0, 0)); p_amix((1, 0)); p_acq((0, 1))
-        y_s(0, 0); y_s(0, 1)
-        turn_a(1, both(range(3)))
-        y_s(0, 2)
+        mix((2, 0)); mix((2, 1)); mix((3, 0)); quant([(2, 0), (2, 1)]); mix((4, 0)); quant([(3, 0)]); quant([(4, 0)])
+        mix((3, 1)); x_quant(1, 0, 0, 2); quant([(3, 1)]); x_quant(1, 0, 2, 2); mix((4, 1))
+        for j in (3,):
+            x_sort((1, 1, j))
+        widen(0, (0,)); quant([(4, 1)])
+        unit_banks((1, 1))
+        x_run(1, 0, range(4))
+        unit_banks((2, 0))
+        unit_banks((2, 1), on_vector=())
+        for j in ():
+            relu((2, 1), j, "V")
+        widen(0, (1, 2, 3))
+        unit_banks((3, 0), on_vector=(3,))
+        x_run(1, 1, range(4), (3,))
+        unit_banks((4, 0), on_vector=())
+        for j in (3,):
+            relu((3, 0), j, "V")
+        mix(("d2", 0)); widen(1, range(4))
+        for j in ():
+            relu((4, 0), j, "V")
+        mix(("d2", 1)); x_quant(1, 1, 0, 2); x_quant(1, 1, 2, 2); quant([("d2", 0), ("d2", 1)])
+        a_run(0, [(G, h) for h in range(2) for G in range(GROUPS)])
+        unit_banks((3, 1)); unit_banks((4, 1))
+        mix(("lab", 0)); mix(("lab", 1)); ay_quant(0, 0, 0, 4); ay_quant(0, 0, 4, 5)
+        a_mix((0, 0)); quant([("lab", 0), ("lab", 1)]); ay_quant(0, 1, 4, 5); a_mix((0, 1)); ay_quant(0, 1, 0, 4); quant([("c", 0, 0), ("c", 0, 1)])
+        y_tile(0, 0); y_tile(0, 1)
+        a_run(1, [(G, 0) for G in range(GROUPS)])
+        y_tile(0, 2)
         c_group(0)
-        y_s(0, 3)
-        p_amix((1, 1)); p_acq((1, 0)); p_amix((2, 0)); p_acq((1, 1))
+        y_tile(0, 3)
+        a_run(1, [(G, 1) for G in range(GROUPS)])
+        a_mix((1, 0)); a_mix((1, 1)); ay_quant(1, 0, 0, 4); quant([("c", 1, 0), ("c", 1, 1)]); ay_quant(1, 0, 4, 5)
         c_group(1)
-        turn_a(1, [(G, h) for h in range(2) for G in (3, 4)])
-        p_amix((2, 1)); p_acq((2, 0)); p_ayq((0, 1), range(2)); p_acq((2, 1))
+
+        a_mix((2, 0)); a_mix((2, 1), "V", 0, 512); quant([("c", 2, 0)]); quant([("c", 2, 1)])
+        y_tile(1, 0)
+
         c_group(2)
-        for G in range(1, 3):
-            p_ayq((G, 1), range(0, 2))
-        p_amix((3, 0)); p_amix((3, 1))
-        for G in range(3, 5):
-            p_ayq((G, 1), range(0, 2))
-        y_s(1, 0); y_s(1, 1)
-        p_acq((3, 0)); p_ahalf((4, 0), 0); p_acq((3, 1))
+
+        y_tile(1, 1)
+        a_mix((3, 0)); a_mix((3, 1)); quant([("c", 3, 0)]); quant([("c", 3, 1)])
+        a_mix((4, 1), "S", 448, W)
         c_group(3)
-        p_ahalf((4, 1), 0); p_acq((4, 0), 0, 256); p_ahalf((4, 0), 1); p_acq((4, 1), 0, 256)
-        p_ahalf((4, 1), 1); p_acq((4, 0), 256, 512); p_ayq((0, 1), range(2, 3)); p_acq((4, 1), 256, 512)
-        c_group(4)
-        for G in range(1, 5):
-            p_ayq((G, 1), range(2, 3))
-        for G in range(0, 5):
-            p_ayq((G, 1), range(3, 4))
-        y_s(1, 2)
-        y_s(1, 3, "S", 0, 256); y_s(1, 3, "V", 256, 512)
+        a_mix((4, 0), "V", 0, 256); a_mix((4, 1), "V", 0, 256); ay_quant(1, 1, 4, 5); quant([("c", 4, 0)], 0, 256); quant([("c", 4, 1)], 0, 256); ay_quant(1, 1, 0, 4)
+        a_mix((4, 1), "V", 256, 448); a_mix((4, 0), "V", 256, W); quant([("c", 4, 1)], 256, W); quant([("c", 4, 0)], 256, W)
+        c_block(4, 0); c_block(4, 1)
+        y_tile(1, 2)
+        c_block(4, 2); c_block(4, 3)
+        y_tile(1, 3, "S", 0, 256); y_tile(1, 3, "V", 256, N)
 
         made = set()
-        queues = [scalar_p, vector_p, tensor_p]
-        while any(queues):
-            ready = [q for q in queues if q and all(parts.get(n, n) in made if n[0] == "acb" else n in made for n in q[0][1])]
-            key, needs, fn, args = ready[0].pop(0)
-            fn(*args)
-            made.add(key)
+        while any(programs.values()):
+            ready = [queue for queue in programs.values() if queue and all(n in made for n in queue[0][1])]
+            makes, needs, function, args = ready[0].pop(0)
+            function(*args)
+            made = made | set(makes)

@@ -17,9 +17,9 @@ ALU = mybir.AluOpType
 T, K, F1, F2, N, R = 1024, 1024, 1536, 1024, 512, 512
 P = 128
 W = 512
+GROUPS = (F1 + F2) // W
+BANKS = 8
 FLOPS = 2 * (T * K * (F1 + F2) + T * (F1 + F2) * (N + R))
-GROUPS = 5
-HEAD_CUT = (336, 384)
 
 
 def tile_cross_layer_transcoder_s8_kernel(
@@ -31,84 +31,70 @@ def tile_cross_layer_transcoder_s8_kernel(
         psum = ctx.enter_context(tc.psum_pool(name="psum", bufs=1))
         ctx.enter_context(tc.manual_schedule())
 
-        def tile(shape, dtype, tag, bufs=1):
-            return pool.tile(shape, dtype, name=tag, tag=tag, bufs=bufs, align_bytes=256)
-
-        def bank():
-            return psum.tile([P, W], F32, name="bank", tag="bank", bufs=8)
-
         held = {}
 
-        def once(key, shape, dtype, tag, bufs):
+        def tile(key, shape, dtype, tag, bufs=1):
             if key not in held:
-                held[key] = tile(shape, dtype, tag, bufs)
+                held[key] = pool.tile(shape, dtype, name=tag, tag=tag, bufs=bufs, align_bytes=256)
             return held[key]
 
-        ident = tile([P, P], F32, "ident")
+        programs = {"S": [], "V": [], "T": []}
+        copies = {"S": nc.scalar.copy, "V": nc.vector.tensor_copy}
+
+        def step(engine, makes, needs, function, fills_new_bank=False):
+            programs[engine].append((makes, needs, function, fills_new_bank))
+
+        free_banks, banks = list(range(BANKS)), {}
+
+        def take_bank(key):
+            number = free_banks.pop(0)
+            banks[key] = number, psum.tile([P, W], F32, name="bank", tag="bank%d" % number, bufs=1)
+            return banks[key][1]
+
+        def emptied(key):
+            free_banks.append(banks[key][0])
+
+        ident = tile("ident", [P, P], F32, "ident")
         make_identity(nc, ident[:])
-        d1_sc = tile([P, 3, N], U8, "d1_sc")
+        d1_sc = tile("d1_sc", [P, 3, N], U8, "d1_sc")
         nc.gpsimd.memset(d1_sc[:].rearrange("p g n -> p (g n)").bitcast(I32), 0)
 
-        rows, lab_raw = {}, {}
+        rows = {}
 
         def x_raw(s, g, j, count=1):
-            return once(("x_raw", s, g, j // 2), [P, 2 * K], BF16, "x_raw", 4)[:, K * (j % 2) : K * (j % 2 + count)]
+            return tile(("x_raw", s, g, j // 2), [P, 2 * K], BF16, "x_raw", 4)[:, K * (j % 2) : K * (j % 2 + count)]
 
         def load_x(s, g, j, count):
             src = (x1, x2)[s].rearrange("(g p j) k -> g p (j k)", p=P, j=4)[g]
             nc.sync.dma_start(out=x_raw(s, g, j, count), in_=src[:, K * j : K * (j + count)])
 
-        def load_rows(names, src, half, col):
-            t = tile([P, 4, W * len(names)], BF16, "rows", 4)
-            src = src.rearrange("(h p j) c -> h p j c", p=P, j=4)[half]
-            nc.sync.dma_start(out=t[:], in_=src[:, :, col : col + W * len(names)])
+        def load_rows(names, src, q, col=0):
+            raw = tile(("rows", names[0], q), [P, 4, W * len(names)], BF16, "rows", 8)
+            src = src.rearrange("(q p j) c -> q p j c", p=P, j=4)[q]
+            nc.sync.dma_start(out=raw[:], in_=src[:, :, col : col + W * len(names)])
             for i, name in enumerate(names):
-                rows[name, half] = t[:, :, W * i : W * (i + 1)]
+                rows[name, q] = raw[:, :, W * i : W * (i + 1)]
 
-        load_x(0, 0, 0, 1)
-        load_rows([0], e1, 0, 0)
-        load_x(0, 0, 1, 1)
-        load_rows([0], e1, 1, 0)
-        load_x(0, 0, 2, 2)
-        load_x(0, 1, 0, 2)
-        load_rows([1], e1, 0, W)
-        load_x(0, 1, 2, 2)
-        load_rows([1], e1, 1, W)
-        load_rows([2], e1, 0, 2 * W)
-        load_rows([2], e1, 1, 2 * W)
-        load_rows([3, 4], e2, 0, 0)
-        load_x(1, 0, 0, 2)
-        load_x(1, 0, 2, 2)
-        load_rows([3, 4], e2, 1, 0)
-        lab_sc = tile([P, 2, 4], F32, "lab_sc")
-        nc.sync.dma_start(out=lab_sc[:], in_=labels_scale.rearrange("(g p j) o -> p g (j o)", p=P, j=4))
-        for g in range(2):
-            lab_raw[g] = tile([P, 4 * R], U8, "lab_raw", 2)
-            nc.sync.dma_start(out=lab_raw[g][:], in_=labels_bytes.rearrange("(g p j) r -> g p (j r)", p=P, j=4)[g])
-        load_x(1, 1, 0, 2)
-        load_x(1, 1, 2, 2)
-        load_rows(["d2"], d2, 0, 0)
-        load_rows(["d2"], d2, 1, 0)
-        d1_w = tile([P, 3, 2 * N], U8, "d1_w")
-        nc.sync.dma_start(out=d1_w[:], in_=d1_words.rearrange("g p c -> p g c"))
-        d1_si = d1_scales.bitcast(I32)
-        d1_sv = d1_sc[:].rearrange("p g n -> p (g n)").bitcast(I32).rearrange("p (g n) -> p g n", g=3)
-        for quad in range(4):
-            nc.sync.dma_start(
-                out=d1_sv[32 * quad : 32 * quad + 4, :, :],
-                in_=d1_si[:, 4 * quad : 4 * quad + 4, :].rearrange("g r n -> r g n"),
-            )
+        def load_labels():
+            scale = tile("lab_sc", [P, 2, 4], F32, "lab_sc")
+            nc.sync.dma_start(out=scale[:], in_=labels_scale.rearrange("(g p j) o -> p g (j o)", p=P, j=4))
+            for g in range(2):
+                raw = tile(("lab_raw", g), [P, 4 * R], U8, "lab_raw", 2)
+                nc.sync.dma_start(out=raw[:], in_=labels_bytes.rearrange("(g p j) r -> g p (j r)", p=P, j=4)[g])
 
-        copies = {"S": nc.scalar.copy, "V": nc.vector.tensor_copy}
-        banks, x_sorted = {}, {}
-        programs = {"S": [], "V": [], "T": []}
-
-        def step(engine, makes, needs, function, *args):
-            programs[engine].append((makes, needs, function, args))
+        def load_d1():
+            words = tile("d1_w", [P, 3, 2 * N], U8, "d1_w")
+            nc.sync.dma_start(out=words[:], in_=d1_words.rearrange("g p c -> p g c"))
+            src = d1_scales.bitcast(I32)
+            dst = d1_sc[:].rearrange("p g n -> p (g n)").bitcast(I32).rearrange("p (g n) -> p g n", g=3)
+            for Q in range(4):
+                nc.sync.dma_start(
+                    out=dst[32 * Q : 32 * Q + 4, :, :], in_=src[:, 4 * Q : 4 * Q + 4, :].rearrange("g r n -> r g n")
+                )
 
         def quantise(key, tag, bufs, columns, values, lo, hi):
-            codes = once(("codes", key), [P, columns], U32, tag + "_c", bufs)
-            scales = once(("scales", key), [P, columns], U8, tag + "_s", bufs)
+            codes = tile(("codes", key), [P, columns], U32, tag + "_c", bufs)
+            scales = tile(("scales", key), [P, columns], U8, tag + "_s", bufs)
             nc.vector.quantize_mx(out=codes[:, lo:hi].bitcast(E4M3X4), scales=scales[:, lo:hi], in_=values)
 
         def operand(key, lo, hi):
@@ -127,35 +113,35 @@ def tile_cross_layer_transcoder_s8_kernel(
 
         def x_sort(x):
             def run():
-                x_sorted[x] = tile([P, W], F32, "x_w", 2)
                 nc.vector.tensor_copy(
-                    out=x_sorted[x][:].rearrange("p (q u m) -> p q u m", q=2, u=2),
+                    out=tile(("x_w", x), [P, W], F32, "x_w", 2)[:].rearrange("p (q u m) -> p q u m", q=2, u=2),
                     in_=x_raw(*x).bitcast(F32).rearrange("p (q m u) -> p q u m", q=2, u=2),
                 )
 
             step("V", [("x_sorted", x)], [], run)
 
-        def x_turn(x, is_sorted=False):
+        def x_turn(x, is_sorted):
             def run():
-                banks[x] = bank()
+                bank = take_bank(x)
                 words = x_raw(*x).bitcast(F32)
                 for q in range(2):
                     for u in range(2):
-                        i = 2 * q + u
-                        src = x_sorted[x][:, i * P : (i + 1) * P] if is_sorted else words[:, 256 * q + u : 256 * (q + 1) : 2]
-                        nc.tensor.transpose(banks[x][:, i * P : (i + 1) * P], src, ident[:])
+                        col = P * (2 * q + u)
+                        src = held["x_w", x][:, col : col + P] if is_sorted else words[:, 256 * q + u : 256 * (q + 1) : 2]
+                        nc.tensor.transpose(bank[:, col : col + P], src, ident[:])
 
-            step("T", [("x_bank", x)], [("x_sorted", x)] if is_sorted else [], run)
+            step("T", [("x_bank", x)], [("x_sorted", x)] if is_sorted else [], run, True)
 
         def x_turned(s, g, j, count=1):
-            return once(("x_t", s, g, j // 2), [P, 2 * W], F32, "x_t", 3)[:, W * (j % 2) : W * (j % 2 + count)]
+            return tile(("x_t", s, g, j // 2), [P, 2 * W], F32, "x_t", 3)[:, W * (j % 2) : W * (j % 2 + count)]
 
         def x_out(x, engine="S"):
             def run():
                 copies[engine](
                     out=x_turned(*x).rearrange("p (q t u) -> p q t u", q=2, u=2),
-                    in_=banks[x][:].rearrange("p (q u t) -> p q t u", q=2, u=2),
+                    in_=banks[x][1][:].rearrange("p (q u t) -> p q t u", q=2, u=2),
                 )
+                emptied(x)
 
             step(engine, [("x_t", x)], [("x_bank", x)], run)
 
@@ -168,15 +154,14 @@ def tile_cross_layer_transcoder_s8_kernel(
             xs = [(s, g, j + i) for i in range(count)]
             step("V", [("x_q", x) for x in xs], [("x_t", x) for x in xs], run)
 
-        pairs = [((G, 0), (G, 1)) for G in range(3)] + [((3, q), (4, q)) for q in range(2)]
-        pairs = pairs + [((name, 0), (name, 1)) for name in ("d2", "lab")]
+        pairs = [((name, 0), (name, 1)) for name in list(range(GROUPS)) + ["d2", "lab"]]
         pairs = pairs + [(("c", G, 0), ("c", G, 1)) for G in range(GROUPS)]
         place = {key: (pair, i) for pair in pairs for i, key in enumerate(pair)}
         parts = {}
 
         def mixed(key, count=1):
             pair, i = place[key]
-            return once(("mixed", pair), [P, 8 * W], BF16, "mixed", 2)[:, 4 * W * i : 4 * W * (i + count)]
+            return tile(("mixed", pair), [P, 8 * W], BF16, "mixed", 2)[:, 4 * W * i : 4 * W * (i + count)]
 
         def mix(key, engine="V", lo=0, hi=W):
             def run():
@@ -207,59 +192,51 @@ def tile_cross_layer_transcoder_s8_kernel(
         def whole(key):
             return [("q", key, b) for b in range(4)]
 
-        def widen(g, js, engine="V"):
-            def run(j):
-                wide = once(("wide", g), [P, 4, R], BF16, "rows", 4)
+        def widen(g, j):
+            def run():
+                wide = tile(("wide", g), [P, 4, R], BF16, "rows", 8)
                 rows["lab", g] = wide[:]
-                src = lab_raw[g][:, j * R : (j + 1) * R].bitcast(E4M3)
-                if engine == "S":
-                    nc.scalar.activation(out=wide[:, j, :], in_=src, func=ACT.Copy, scale=lab_sc[:, g, j : j + 1])
-                else:
-                    nc.vector.tensor_scalar(
-                        out=wide[:, j, :], in0=src, scalar1=lab_sc[:, g, j : j + 1], scalar2=None, op0=ALU.mult
-                    )
+                src = held["lab_raw", g][:, j * R : (j + 1) * R].bitcast(E4M3)
+                scale = held["lab_sc"][:, g, j : j + 1]
+                nc.vector.tensor_scalar(out=wide[:, j, :], in0=src, scalar1=scale, scalar2=None, op0=ALU.mult)
 
-            for j in js:
-                step(engine, [("wide", g, j)], [], run, j)
+            step("V", [("wide", g, j)], [], run)
 
         def features(unit):
-            return once(("a", unit), [P, 4, W], BF16, "a", 2 * GROUPS)
+            return tile(("a", unit), [P, 4, W], BF16, "a", 2 * GROUPS)
 
         def stage1(unit, j, q):
             G, g = unit
             s = G // 3
 
             def run():
-                if q == 0:
-                    banks[unit, j] = bank()
+                bank = take_bank((unit, j)) if q == 0 else banks[unit, j][1]
                 lo = 256 * (j % 2) + P * q
-                mx(banks[unit, j][:], operand(("x", s, g, j // 2), lo, lo + P), quantised((G, q)), q == 0, q == 1)
+                mx(bank[:], operand(("x", s, g, j // 2), lo, lo + P), quantised((G, q)), q == 0, q == 1)
 
-            step("T", [("s1", unit, j, q)], [("x_q", (s, g, j))] + whole((G, q)), run)
+            step("T", [("s1", unit, j, q)], [("x_q", (s, g, j))] + whole((G, q)), run, q == 0)
 
-        def relu(unit, j, engine="S"):
+        def relu(unit, j):
             def run():
                 dst = features(unit)[:, j, :].rearrange("p (u m e) -> p u m e", u=2, e=2)
-                src = banks[unit, j][:].rearrange("p (m u e) -> p u m e", u=2, e=2)
-                if engine == "S":
-                    nc.scalar.activation(out=dst, in_=src, func=ACT.Relu)
-                else:
-                    nc.vector.tensor_scalar(out=dst, in0=src, scalar1=0.0, scalar2=None, op0=ALU.max)
+                src = banks[unit, j][1][:].rearrange("p (m u e) -> p u m e", u=2, e=2)
+                nc.scalar.activation(out=dst, in_=src, func=ACT.Relu)
+                emptied((unit, j))
 
-            step(engine, [("a", unit, j)], [("s1", unit, j, 1)], run)
+            step("S", [("a", unit, j)], [("s1", unit, j, 1)], run)
 
         def a_turn(unit, h):
             def run():
                 words = features(unit)[:].rearrange("p j f -> p (j f)").bitcast(F32)
-                banks["a", unit, h] = bank()
+                bank = take_bank(("a", unit, h))
                 for i in range(4):
                     col = W * h + P * i
-                    nc.tensor.transpose(banks["a", unit, h][:, i * P : (i + 1) * P], words[:, col : col + P], ident[:])
+                    nc.tensor.transpose(bank[:, i * P : (i + 1) * P], words[:, col : col + P], ident[:])
 
-            step("T", [("a_bank", unit, h)], [("a", unit, 2 * h), ("a", unit, 2 * h + 1)], run)
+            step("T", [("a_bank", unit, h)], [("a", unit, 2 * h), ("a", unit, 2 * h + 1)], run, True)
 
         def a_turned(g, h):
-            return once(("a_t", g, h), [P, GROUPS * W], F32, "a_t", 2)
+            return tile(("a_t", g, h), [P, GROUPS * W], F32, "a_t", 2)
 
         def a_out(unit, h, engine="S"):
             G, g = unit
@@ -267,12 +244,13 @@ def tile_cross_layer_transcoder_s8_kernel(
             def run():
                 copies[engine](
                     out=a_turned(g, h)[:, W * G : W * (G + 1)].rearrange("p (j t u) -> p j t u", j=2, u=2),
-                    in_=banks["a", unit, h][:].rearrange("p (j u t) -> p j t u", j=2, u=2),
+                    in_=banks["a", unit, h][1][:].rearrange("p (j u t) -> p j t u", j=2, u=2),
                 )
+                emptied(("a", unit, h))
 
             step(engine, [("a_t", unit, h)], [("a_bank", unit, h)], run)
 
-        def ay_quant(g, h, lo, hi):
+        def y_quant(g, h, lo, hi):
             def run():
                 values = a_turned(g, h)[:, W * lo : W * hi].bitcast(BF16)
                 quantise(("y", g, h), "a_y", 4, GROUPS * 256, values, 256 * lo, 256 * hi)
@@ -293,160 +271,158 @@ def tile_cross_layer_transcoder_s8_kernel(
             step(engine, [("mixed", key, lo)], [("a", unit, j) for j in range(4)], run)
 
         stored = []
-        staging = [("x_raw", 4, 2, 0), ("x_t", 3, 2, 8), ("rows", 4, 4, 14)]
+        staging = [("x_raw", 4, 2, 0), ("x_t", 3, 2, 8), ("rows", 8, 2, 14)]
 
         def store(key, dst, engine, width):
             def run():
-                n = len(stored)
+                tag, bufs, count, first = [place for place in staging if place[3] <= len(stored)][-1]
+                buffer, i = divmod(len(stored) - first, count)
                 stored.append(key)
-                tag, bufs, banks_held, first = [place for place in staging if place[3] <= n][-1]
-                group, i = divmod(n - first, banks_held)
-                staged = once(("staged", tag, group), [P, banks_held * W], F32, tag, bufs)[:, W * i : W * i + width]
-                copies[engine](out=staged, in_=banks[key][:, :width])
+                staged = tile(("staged", tag, buffer), [P, count * W], F32, tag, bufs)[:, W * i : W * i + width]
+                copies[engine](out=staged, in_=banks[key][1][:, :width])
+                emptied(key)
                 nc.sync.dma_start(out=dst, in_=staged)
 
             step(engine, [("stored", key)], [key], run)
 
-        def c_block(G, b, engine="S"):
+        def c_block(G, b, engine="S", lo=0, hi=R):
+            key = ("c", G, b, lo)
+
             def run():
-                banks["c", G, b] = bank()
+                bank = take_bank(key)
                 for g in range(2):
                     lhs = quantised(("c", G, g), P * b, P * (b + 1))
-                    mx(banks["c", G, b][:], lhs, quantised(("lab", g)), g == 0, g == 1)
+                    mx(bank[:, : hi - lo], lhs, quantised(("lab", g), lo, hi), g == 0, g == 1)
 
             needs = [("q", ("c", G, g), b) for g in range(2)] + whole(("lab", 0)) + whole(("lab", 1))
-            step("T", [("c", G, b)], needs, run)
+            step("T", [key], needs, run, True)
             dst = out_1[W * G : W * (G + 1), :] if G < 3 else out_2[W * (G - 3) : W * (G - 2), :]
-            store(("c", G, b), dst[P * b : P * (b + 1), :], engine, R)
+            store(key, dst[P * b : P * (b + 1), lo:hi], engine, hi - lo)
 
         def y_tile(g, j, engine="S", lo=0, hi=N):
+            key = ("y", g, j, lo)
+
             def run():
-                banks["y", g, j, lo] = bank()
+                bank = take_bank(key)
                 for G in range(GROUPS):
                     col = 256 * G + P * (j % 2)
                     if G < 3:
-                        rhs = d1_w[:, G, 2 * lo : 2 * hi].bitcast(E2M1X4), d1_sc[:, G, lo:hi]
+                        rhs = held["d1_w"][:, G, 2 * lo : 2 * hi].bitcast(E2M1X4), d1_sc[:, G, lo:hi]
                     else:
                         rhs = quantised(("d2", G - 3), lo, hi)
-                    lhs = operand(("y", g, j // 2), col, col + P)
-                    mx(banks["y", g, j, lo][:, : hi - lo], lhs, rhs, G == 0, G == GROUPS - 1)
+                    mx(bank[:, : hi - lo], operand(("y", g, j // 2), col, col + P), rhs, G == 0, G == GROUPS - 1)
 
             needs = [("y_q", G, g, j // 2) for G in range(GROUPS)] + whole(("d2", 0)) + whole(("d2", 1))
-            step("T", [("y", g, j, lo)], needs, run)
+            step("T", [key], needs, run, True)
             dst = out_0.rearrange("(g p j) n -> g j p n", p=P, j=4)[g][j][:, lo:hi]
-            store(("y", g, j, lo), dst, engine, hi - lo)
+            store(key, dst, engine, hi - lo)
 
         def warm_up(count):
             def run():
-                unread = bank()
                 first = x_raw(0, 0, 0)
-                nc.tensor.matmul(unread[:], lhsT=first[:, :P], rhs=first[:, :W], start=True, stop=True)
+                bank = take_bank("unread")
+                for i in range(count):
+                    nc.tensor.matmul(bank[:], lhsT=first[:, :P], rhs=first[:, :W], start=True, stop=True)
+                emptied("unread")
 
-            for i in range(count):
-                step("T", [], [], run)
+            step("T", [], [], run, True)
 
-        def unit_banks(unit, js=range(4), on_vector=()):
+        def unit_banks(unit, js=range(4)):
             for j in js:
                 stage1(unit, j, 0)
                 stage1(unit, j, 1)
-                if j not in on_vector:
-                    relu(unit, j)
+                relu(unit, j)
+
+        def first_passes(unit, js=range(4)):
+            for j in js:
+                stage1(unit, j, 0)
+
+        def second_passes(unit, js=range(4)):
+            for j in js:
+                stage1(unit, j, 1)
+                relu(unit, j)
 
         def x_run(s, g, js, are_sorted=()):
             for j in js:
                 x_turn((s, g, j), j in are_sorted)
                 x_out((s, g, j))
 
-        def a_run(g, unit_halves):
-            for G, h in unit_halves:
+        def a_run(g, halves):
+            for G, h in halves:
                 a_turn((G, g), h)
                 a_out((G, g), h)
 
-        def c_group(G):
-            for b in range(4):
+        def c_group(G, blocks=range(4)):
+            for b in blocks:
                 c_block(G, b)
 
-
-        x_turn((0, 0, 0)); warm_up(2)
-        mix((0, 0), "V", 0, HEAD_CUT[0]); mix((0, 0), "S", HEAD_CUT[0], W)
-        x_out((0, 0, 0)); quant([(0, 0)])
-        x_turn((0, 0, 1)); warm_up(2); x_quant(0, 0, 0, 1)
-        x_out((0, 0, 1))
-        mix((0, 1), "V", 0, HEAD_CUT[1]); mix((0, 1), "S", HEAD_CUT[1], W)
-        x_quant(0, 0, 1, 1); quant([(0, 1)])
-        stage1((0, 0), 0, 0)
-        x_run(0, 0, (2, 3))
-        stage1((0, 0), 1, 0); stage1((0, 0), 0, 1); stage1((0, 0), 1, 1)
-        x_sort((0, 1, 0)); x_sort((0, 1, 1)); x_quant(0, 0, 2, 1); x_quant(0, 0, 3, 1); mix((1, 0))
-        relu((0, 0), 0)
-        x_run(0, 1, (0, 1), (0, 1))
+        load_x(0, 0, 0, 1); load_rows([0], e1, 0); load_x(0, 0, 1, 1); load_rows([0], e1, 1); load_x(0, 0, 2, 2)
+        load_x(0, 1, 0, 2); load_rows([1], e1, 0, W); load_x(0, 1, 2, 2); load_rows([1], e1, 1, W)
+        load_rows([2], e1, 0, 2 * W); load_rows([2], e1, 1, 2 * W)
+        load_rows([3], e2, 0); load_x(1, 0, 0, 2); load_x(1, 0, 2, 2); load_rows([3], e2, 1); load_rows([4], e2, 0, W); load_rows([4], e2, 1, W)
+        load_x(1, 1, 0, 2); load_x(1, 1, 2, 2)
+        load_rows(["d2"], d2, 0); load_rows(["d2"], d2, 1); load_labels(); load_d1()
+        x_turn((0, 0, 0), False); warm_up(2)
+        mix((0, 0), "S", 336, W); x_out((0, 0, 0))
+        x_run(0, 0, [1]); warm_up(2)
+        mix((0, 1), "S", 384, W)
+        first_passes((0, 0), [0])
+        x_run(0, 0, [2, 3])
+        first_passes((0, 0), [1]); second_passes((0, 0), [0]); stage1((0, 0), 1, 1)
+        x_run(0, 1, [0, 1], [0, 1])
         relu((0, 0), 1)
-        for j in (2, 3):
-            stage1((0, 0), j, 0); stage1((0, 0), j, 1)
-        relu((0, 0), 2)
-        x_run(0, 1, (2, 3))
+        unit_banks((0, 0), [2]); stage1((0, 0), 3, 0); stage1((0, 0), 3, 1)
+        x_run(0, 1, [2, 3])
         relu((0, 0), 3)
-        x_quant(0, 1, 0, 1); x_quant(0, 1, 1, 1); quant([(1, 0)]); mix((1, 1)); x_quant(0, 1, 2, 1); x_quant(0, 1, 3, 1); quant([(1, 1)])
-        unit_banks((0, 1), (0, 1))
-        for j in range(4):
-            stage1((1, 0), j, 0)
-        unit_banks((0, 1), (2, 3))
-        for j in range(4):
-            stage1((1, 0), j, 1); relu((1, 0), j)
-
-        mix((2, 0)); mix((2, 1)); mix((3, 0)); quant([(2, 0), (2, 1)]); mix((4, 0)); quant([(3, 0)]); quant([(4, 0)])
-        mix((3, 1)); x_quant(1, 0, 0, 2); quant([(3, 1)]); x_quant(1, 0, 2, 2); mix((4, 1))
-        for j in (3,):
-            x_sort((1, 1, j))
-        widen(0, (0,)); quant([(4, 1)])
+        unit_banks((0, 1), [0, 1])
+        first_passes((1, 0))
+        mix((2, 0), "S", 384, W)
+        unit_banks((0, 1), [2, 3])
+        second_passes((1, 0))
         unit_banks((1, 1))
         x_run(1, 0, range(4))
-        unit_banks((2, 0))
-        unit_banks((2, 1), on_vector=())
-        for j in ():
-            relu((2, 1), j, "V")
-        widen(0, (1, 2, 3))
-        unit_banks((3, 0), on_vector=(3,))
-        x_run(1, 1, range(4), (3,))
-        unit_banks((4, 0), on_vector=())
-        for j in (3,):
-            relu((3, 0), j, "V")
-        mix(("d2", 0)); widen(1, range(4))
-        for j in ():
-            relu((4, 0), j, "V")
-        mix(("d2", 1)); x_quant(1, 1, 0, 2); x_quant(1, 1, 2, 2); quant([("d2", 0), ("d2", 1)])
+        unit_banks((2, 0)); unit_banks((2, 1)); unit_banks((3, 0))
+        x_run(1, 1, range(4))
+        unit_banks((4, 0))
         a_run(0, [(G, h) for h in range(2) for G in range(GROUPS)])
         unit_banks((3, 1)); unit_banks((4, 1))
-        mix(("lab", 0)); mix(("lab", 1)); ay_quant(0, 0, 0, 4); ay_quant(0, 0, 4, 5)
-        a_mix((0, 0)); quant([("lab", 0), ("lab", 1)]); ay_quant(0, 1, 4, 5); a_mix((0, 1)); ay_quant(0, 1, 0, 4); quant([("c", 0, 0), ("c", 0, 1)])
         y_tile(0, 0); y_tile(0, 1)
         a_run(1, [(G, 0) for G in range(GROUPS)])
-        y_tile(0, 2)
-        c_group(0)
+        y_tile(0, 2); c_group(0)
+        a_mix((2, 1), "S", 384, W)
         y_tile(0, 3)
         a_run(1, [(G, 1) for G in range(GROUPS)])
-        a_mix((1, 0)); a_mix((1, 1)); ay_quant(1, 0, 0, 4); quant([("c", 1, 0), ("c", 1, 1)]); ay_quant(1, 0, 4, 5)
-        c_group(1)
-
-        a_mix((2, 0)); a_mix((2, 1), "V", 0, 512); quant([("c", 2, 0)]); quant([("c", 2, 1)])
-        y_tile(1, 0)
-
-        c_group(2)
-
+        c_group(1); y_tile(1, 0); c_group(2)
+        a_mix((4, 1), "S", 384, W)
         y_tile(1, 1)
-        a_mix((3, 0)); a_mix((3, 1)); quant([("c", 3, 0)]); quant([("c", 3, 1)])
-        a_mix((4, 1), "S", 448, W)
-        c_group(3)
-        a_mix((4, 0), "V", 0, 256); a_mix((4, 1), "V", 0, 256); ay_quant(1, 1, 4, 5); quant([("c", 4, 0)], 0, 256); quant([("c", 4, 1)], 0, 256); ay_quant(1, 1, 0, 4)
-        a_mix((4, 1), "V", 256, 448); a_mix((4, 0), "V", 256, W); quant([("c", 4, 1)], 256, W); quant([("c", 4, 0)], 256, W)
-        c_block(4, 0); c_block(4, 1)
-        y_tile(1, 2)
-        c_block(4, 2); c_block(4, 3)
-        y_tile(1, 3, "S", 0, 256); y_tile(1, 3, "V", 256, N)
+        c_group(3); c_group(4, [0, 1]); y_tile(1, 2); c_group(4, [2, 3]); y_tile(1, 3, "S", 0, 256)
+        mix((0, 0), "V", 0, 336); quant([(0, 0)]); x_quant(0, 0, 0, 1); mix((0, 1), "V", 0, 384); x_quant(0, 0, 1, 1); quant([(0, 1)])
+        x_sort((0, 1, 0)); x_sort((0, 1, 1)); x_quant(0, 0, 2, 1); x_quant(0, 0, 3, 1); mix((1, 0))
+        x_quant(0, 1, 0, 1); x_quant(0, 1, 1, 1); quant([(1, 0)]); mix((1, 1)); x_quant(0, 1, 2, 1); x_quant(0, 1, 3, 1); quant([(1, 1)])
+        mix((2, 0), "V", 0, 384); mix((2, 1)); mix((3, 0)); quant([(2, 0), (2, 1)]); mix((3, 1)); mix((4, 0), "V", 0, 128); quant([(3, 0), (3, 1)])
+        mix((4, 0), "V", 128, W); x_quant(1, 0, 0, 2); x_quant(1, 0, 2, 2); mix((4, 1)); mix(("d2", 0)); quant([(4, 0), (4, 1)]); mix(("d2", 1))
+        for j in range(4):
+            widen(0, j)
+        quant([("d2", 0), ("d2", 1)])
+        for j in range(4):
+            widen(1, j)
+        x_quant(1, 1, 0, 2); mix(("lab", 0)); x_quant(1, 1, 2, 2); mix(("lab", 1))
+        a_mix((0, 0)); y_quant(0, 0, 0, 4); y_quant(0, 0, 4, 5); quant([("lab", 0), ("lab", 1)]); a_mix((0, 1)); y_quant(0, 1, 0, 4); y_quant(0, 1, 4, 5)
+        quant([("c", 0, 0), ("c", 0, 1)]); a_mix((1, 0)); a_mix((1, 1)); a_mix((2, 0)); quant([("c", 1, 0), ("c", 1, 1)])
+        a_mix((2, 1), "V", 0, 384); y_quant(1, 0, 0, 4); y_quant(1, 0, 4, 5); a_mix((3, 0))
+        quant([("c", 2, 0), ("c", 2, 1)]); a_mix((3, 1)); a_mix((4, 0), "V", 0, 256); quant([("c", 3, 0), ("c", 3, 1)])
+        a_mix((4, 1), "V", 0, 256); y_quant(1, 1, 0, 4); quant([("c", 4, 0)], 0, 256); quant([("c", 4, 1)], 0, 256); y_quant(1, 1, 4, 5)
+        a_mix((4, 0), "V", 256, W); a_mix((4, 1), "V", 256, 384); quant([("c", 4, 0)], 256, W); quant([("c", 4, 1)], 256, W)
+        y_tile(1, 3, "V", 256, N)
+
 
         made = set()
         while any(programs.values()):
-            ready = [queue for queue in programs.values() if queue and all(n in made for n in queue[0][1])]
-            makes, needs, function, args = ready[0].pop(0)
-            function(*args)
+            ready = [
+                queue
+                for queue in programs.values()
+                if queue and all(n in made for n in queue[0][1]) and (free_banks or not queue[0][3])
+            ]
+            makes, needs, function, fills_new_bank = ready[0].pop(0)
+            function()
             made = made | set(makes)

@@ -69,11 +69,18 @@ def tile_cross_layer_transcoder_s8_kernel(
             nc.sync.dma_start(out=x_raw(s, g, j, count), in_=src[:, K * j : K * (j + count)])
 
         def load_rows(names, src, q, col=0):
-            raw = tile(("rows", names[0], q), [P, 4, W * len(names)], BF16, "rows", 8)
+            raw = tile(("rows", names[0], q), [P, 4, W * len(names)], BF16, "rows", 4)
             src = src.rearrange("(q p j) c -> q p j c", p=P, j=4)[q]
             nc.sync.dma_start(out=raw[:], in_=src[:, :, col : col + W * len(names)])
             for i, name in enumerate(names):
                 rows[name, q] = raw[:, :, W * i : W * (i + 1)]
+
+        def load_d2(q):
+            raw = tile(("rows", "d2", q), [P, 4, W], BF16, "rows", 4)
+            src = d2.rearrange("(q b t i) n -> q t b i n", b=16, t=4, i=8)[q]
+            for t in range(4):
+                nc.sync.dma_start(out=raw[:, t, :], in_=src[t])
+            rows["d2", q] = raw[:]
 
         def load_labels():
             scale = tile("lab_sc", [P, 2, 4], F32, "lab_sc")
@@ -149,32 +156,68 @@ def tile_cross_layer_transcoder_s8_kernel(
             def run():
                 lo = 256 * (j % 2)
                 values = x_turned(s, g, j, count).bitcast(BF16)
-                quantise(("x", s, g, j // 2), "x", 8, W, values, lo, lo + 256 * count)
+                quantise(("x", s, g, j // 2), "x", 4, W, values, lo, lo + 256 * count)
 
             xs = [(s, g, j + i) for i in range(count)]
             step("V", [("x_q", x) for x in xs], [("x_t", x) for x in xs], run)
 
+        def x2_turn(g, u, q):
+            def run():
+                bank = take_bank(("x2", g, u, q))
+                for e in range(2):
+                    words = x_raw(1, g, 2 * u + e).bitcast(F32)
+                    for v in range(2):
+                        col = P * (2 * e + v)
+                        nc.tensor.transpose(bank[:, col : col + P], words[:, 256 * q + v : 256 * (q + 1) : 2], ident[:])
+
+            step("T", [("x2_bank", g, u, q)], [], run, True)
+
+        def x2_turned(g, q):
+            return tile(("x2_t", g, q), [P, 2 * W], F32, "x_t", 3)
+
+        def x2_out(g, u, q):
+            def run():
+                nc.scalar.copy(
+                    out=x2_turned(g, q)[:, W * u : W * (u + 1)].rearrange("p (c i) -> p c i", i=4),
+                    in_=banks["x2", g, u, q][1][:].rearrange("p (i c) -> p c i", i=4),
+                )
+                emptied(("x2", g, u, q))
+
+            step("S", [("x2_t", g, u, q)], [("x2_bank", g, u, q)], run)
+
+        def x2_quant(g, q):
+            def run():
+                quantise(("x2", g), "x2", 2, 2 * W, x2_turned(g, q)[:].bitcast(BF16), W * q, W * (q + 1))
+
+            step("V", [("x2_q", g, q)], [("x2_t", g, u, q) for u in range(2)], run)
+
         pairs = [((name, 0), (name, 1)) for name in list(range(GROUPS)) + ["d2", "lab"]]
-        pairs = pairs + [(("c", G, 0), ("c", G, 1)) for G in range(GROUPS)]
+        pairs = pairs + [(("c", G, 0), ("c", G, 1)) for G in range(3)]
         place = {key: (pair, i) for pair in pairs for i, key in enumerate(pair)}
         parts = {}
 
         def mixed(key, count=1):
             pair, i = place[key]
-            return tile(("mixed", pair), [P, 8 * W], BF16, "mixed", 2)[:, 4 * W * i : 4 * W * (i + count)]
+            return tile(("mixed", pair), [P, 8 * W], BF16, "mixed", 3)[:, 4 * W * i : 4 * W * (i + count)]
 
         def mix(key, engine="V", lo=0, hi=W):
             def run():
-                dst = mixed(key).rearrange("p (c i j) -> p c j i", i=2, j=4)
-                src = rows[key].rearrange("p j (c i) -> p c j i", i=2)
-                copies[engine](out=dst[:, lo // 2 : hi // 2], in_=src[:, lo // 2 : hi // 2])
+                if key[0] in (3, 4):
+                    dst = mixed(key).rearrange("p (t b h i j) -> p t b h j i", t=4, h=4, i=2, j=4)
+                    src = rows[key].rearrange("p j (b t h i) -> p t b h j i", t=4, h=4, i=2)
+                    for t in range(lo // P, hi // P):
+                        copies[engine](out=dst[:, t], in_=src[:, t])
+                else:
+                    dst = mixed(key).rearrange("p (c i j) -> p c j i", i=2, j=4)
+                    src = rows[key].rearrange("p j (c i) -> p c j i", i=2)
+                    copies[engine](out=dst[:, lo // 2 : hi // 2], in_=src[:, lo // 2 : hi // 2])
 
             parts.setdefault(key, []).append((lo, hi))
             step(engine, [("mixed", key, lo)], [("wide", key[1], j) for j in range(4)] if key[0] == "lab" else [], run)
 
         def quant(keys, lo=0, hi=W):
             pair, i = place[keys[0]]
-            tag, bufs = ("a_c", 3) if keys[0][0] == "c" else ("w", 2) if keys[0][0] in ("d2", "lab") else ("e", 3)
+            tag, bufs = ("w", 2) if keys[0][0] in ("d2", "lab") else ("e", 3)
             end = hi + W * (len(keys) - 1)
 
             def run():
@@ -194,7 +237,7 @@ def tile_cross_layer_transcoder_s8_kernel(
 
         def widen(g, j):
             def run():
-                wide = tile(("wide", g), [P, 4, R], BF16, "rows", 8)
+                wide = tile(("wide", g), [P, 4, R], BF16, "rows", 4)
                 rows["lab", g] = wide[:]
                 src = held["lab_raw", g][:, j * R : (j + 1) * R].bitcast(E4M3)
                 scale = held["lab_sc"][:, g, j : j + 1]
@@ -207,23 +250,32 @@ def tile_cross_layer_transcoder_s8_kernel(
 
         def stage1(unit, j, q):
             G, g = unit
-            s = G // 3
 
             def run():
                 bank = take_bank((unit, j)) if q == 0 else banks[unit, j][1]
-                lo = 256 * (j % 2) + P * q
-                mx(bank[:], operand(("x", s, g, j // 2), lo, lo + P), quantised((G, q)), q == 0, q == 1)
+                if G < 3:
+                    lo = 256 * (j % 2) + P * q
+                    mx(bank[:], operand(("x", 0, g, j // 2), lo, lo + P), quantised((G, q)), q == 0, q == 1)
+                else:
+                    moving = operand(("x2", g), W * q, W * (q + 1))
+                    mx(bank[:], quantised((G, q), P * j, P * (j + 1)), moving, q == 0, q == 1)
 
-            step("T", [("s1", unit, j, q)], [("x_q", (s, g, j))] + whole((G, q)), run, q == 0)
+            needs = [("x_q", (0, g, j))] + whole((G, q)) if G < 3 else [("x2_q", g, q), ("q", (G, q), j)]
+            step("T", [("s1", unit, j, q)], needs, run, q == 0)
 
-        def relu(unit, j):
+        def relu(unit, j, engine="S"):
             def run():
-                dst = features(unit)[:, j, :].rearrange("p (u m e) -> p u m e", u=2, e=2)
-                src = banks[unit, j][1][:].rearrange("p (m u e) -> p u m e", u=2, e=2)
-                nc.scalar.activation(out=dst, in_=src, func=ACT.Relu)
+                dst, src = features(unit)[:, j, :], banks[unit, j][1][:]
+                if unit[0] < 3:
+                    dst = dst.rearrange("p (u m e) -> p u m e", u=2, e=2)
+                    src = src.rearrange("p (m u e) -> p u m e", u=2, e=2)
+                if engine == "S":
+                    nc.scalar.activation(out=dst, in_=src, func=ACT.Relu)
+                else:
+                    nc.vector.tensor_scalar(out=dst, in0=src, scalar1=0.0, scalar2=None, op0=ALU.max)
                 emptied((unit, j))
 
-            step("S", [("a", unit, j)], [("s1", unit, j, 1)], run)
+            step(engine, [("a", unit, j)], [("s1", unit, j, 1)], run)
 
         def a_turn(unit, h):
             def run():
@@ -243,19 +295,63 @@ def tile_cross_layer_transcoder_s8_kernel(
 
             def run():
                 copies[engine](
-                    out=a_turned(g, h)[:, W * G : W * (G + 1)].rearrange("p (j t u) -> p j t u", j=2, u=2),
-                    in_=banks["a", unit, h][1][:].rearrange("p (j u t) -> p j t u", j=2, u=2),
+                    out=a_turned(g, h)[:, W * G : W * (G + 1)].rearrange("p (c i) -> p c i", i=4),
+                    in_=banks["a", unit, h][1][:].rearrange("p (i c) -> p c i", i=4),
                 )
                 emptied(("a", unit, h))
 
-            step(engine, [("a_t", unit, h)], [("a_bank", unit, h)], run)
+            step(engine, [("a_t", unit, h, i) for i in range(2)], [("a_bank", unit, h)], run)
 
         def y_quant(g, h, lo, hi):
             def run():
-                values = a_turned(g, h)[:, W * lo : W * hi].bitcast(BF16)
-                quantise(("y", g, h), "a_y", 4, GROUPS * 256, values, 256 * lo, 256 * hi)
+                values = a_turned(g, h)[:, 256 * lo : 256 * hi].bitcast(BF16)
+                quantise(("y", g, h), "a_y", 4, GROUPS * 256, values, P * lo, P * hi)
 
-            step("V", [("y_q", G, g, h) for G in range(lo, hi)], [("a_t", (G, g), h) for G in range(lo, hi)], run)
+            pieces = [divmod(n, 2) for n in range(lo, hi)]
+            step("V", [("y_q", G, g, h, i) for G, i in pieces], [("a_t", (G, g), h, i) for G, i in pieces], run)
+
+        def y_mix(unit, h, engine="V", lo=0, hi=256):
+            G, g = unit
+
+            def run():
+                dst = a_turned(g, h)[:, W * G : W * (G + 1)].bitcast(BF16)[:, 4 * lo : 4 * hi]
+                src = features(unit)[:, :, 256 * h + lo : 256 * h + hi]
+                copies[engine](
+                    out=dst.rearrange("p (c e t) -> p c t e", e=2, t=4), in_=src.rearrange("p t (c e) -> p c t e", e=2)
+                )
+
+            step(engine, [("a_t", unit, h, i) for i in range(lo // P, hi // P)], [("a", unit, t) for t in range(4)], run)
+
+        def c_turn(G, t):
+            def run():
+                bank = take_bank(("c_bank", G, t))
+                for g in range(2):
+                    words = features((G, g))[:, t, :].bitcast(F32)
+                    for u in range(2):
+                        col = P * (2 * g + u)
+                        nc.tensor.transpose(bank[:, col : col + P], words[:, P * u : P * (u + 1)], ident[:])
+
+            step("T", [("c_bank", G, t)], [("a", (G, g), t) for g in range(2)], run, True)
+
+        def c_turned(G):
+            return tile(("c_t", G), [P, 4 * W], F32, "mixed", 3)
+
+        def c_out(G, t):
+            def run():
+                nc.scalar.copy(
+                    out=c_turned(G)[:, W * t : W * (t + 1)].rearrange("p (g m u) -> p g m u", g=2, u=2),
+                    in_=banks["c_bank", G, t][1][:].rearrange("p (g u m) -> p g m u", g=2, u=2),
+                )
+                emptied(("c_bank", G, t))
+
+            step("S", [("c_t", G, t)], [("c_bank", G, t)], run)
+
+        def c_quant(G, lo, hi):
+            def run():
+                values = c_turned(G)[:, W * lo : W * hi].bitcast(BF16)
+                quantise(("c", G), "e", 3, 2 * W, values, 256 * lo, 256 * hi)
+
+            step("V", [("c_q", G, t) for t in range(lo, hi)], [("c_t", G, t) for t in range(lo, hi)], run)
 
         def a_mix(unit, engine="V", lo=0, hi=W):
             key = ("c",) + unit
@@ -271,7 +367,7 @@ def tile_cross_layer_transcoder_s8_kernel(
             step(engine, [("mixed", key, lo)], [("a", unit, j) for j in range(4)], run)
 
         stored = []
-        staging = [("x_raw", 4, 2, 0), ("x_t", 3, 2, 8), ("rows", 8, 2, 14)]
+        staging = [("x_raw", 4, 2, 0), ("x_t", 3, 2, 8), ("rows", 4, 4, 14)]
 
         def store(key, dst, engine, width):
             def run():
@@ -285,26 +381,32 @@ def tile_cross_layer_transcoder_s8_kernel(
 
             step(engine, [("stored", key)], [key], run)
 
-        def c_block(G, b, engine="S", lo=0, hi=R):
-            key = ("c", G, b, lo)
+        def c_block(G, b):
+            key = ("c", G, b)
 
             def run():
                 bank = take_bank(key)
                 for g in range(2):
-                    lhs = quantised(("c", G, g), P * b, P * (b + 1))
-                    mx(bank[:, : hi - lo], lhs, quantised(("lab", g), lo, hi), g == 0, g == 1)
+                    col = 256 * b + P * g
+                    lhs = quantised(("c", G, g), P * b, P * (b + 1)) if G < 3 else operand(("c", G), col, col + P)
+                    mx(bank[:], lhs, quantised(("lab", g)), g == 0, g == 1)
 
-            needs = [("q", ("c", G, g), b) for g in range(2)] + whole(("lab", 0)) + whole(("lab", 1))
-            step("T", [key], needs, run, True)
-            dst = out_1[W * G : W * (G + 1), :] if G < 3 else out_2[W * (G - 3) : W * (G - 2), :]
-            store(key, dst[P * b : P * (b + 1), lo:hi], engine, hi - lo)
+            needs = [("q", ("c", G, g), b) for g in range(2)] if G < 3 else [("c_q", G, b)]
+            step("T", [key], needs + whole(("lab", 0)) + whole(("lab", 1)), run, True)
+
+        def c_store(G, b):
+            if G < 3:
+                dst = out_1[W * G + P * b : W * G + P * (b + 1), :]
+            else:
+                dst = out_2.rearrange("(G b t i) r -> G t b i r", b=16, t=4, i=8)[G - 3][b]
+            store(("c", G, b), dst, "S", R)
 
         def y_tile(g, j, engine="S", lo=0, hi=N):
             key = ("y", g, j, lo)
 
-            def run():
-                bank = take_bank(key)
-                for G in range(GROUPS):
+            def one_pass(G):
+                def run():
+                    bank = take_bank(key) if G == 0 else banks[key][1]
                     col = 256 * G + P * (j % 2)
                     if G < 3:
                         rhs = held["d1_w"][:, G, 2 * lo : 2 * hi].bitcast(E2M1X4), d1_sc[:, G, lo:hi]
@@ -312,9 +414,12 @@ def tile_cross_layer_transcoder_s8_kernel(
                         rhs = quantised(("d2", G - 3), lo, hi)
                     mx(bank[:, : hi - lo], operand(("y", g, j // 2), col, col + P), rhs, G == 0, G == GROUPS - 1)
 
-            needs = [("y_q", G, g, j // 2) for G in range(GROUPS)] + whole(("d2", 0)) + whole(("d2", 1))
-            step("T", [key], needs, run, True)
-            dst = out_0.rearrange("(g p j) n -> g j p n", p=P, j=4)[g][j][:, lo:hi]
+                needs = [("y_q", G, g, j // 2, j % 2)] + whole(("d2", 0)) + whole(("d2", 1))
+                step("T", [key] if G == GROUPS - 1 else [], needs, run, G == 0)
+
+            for G in range(GROUPS):
+                one_pass(G)
+            dst = out_0.rearrange("(g h c u e) n -> g u h c e n", g=2, h=2, u=2, e=2)[g][j // 2][j % 2][:, :, lo:hi]
             store(key, dst, engine, hi - lo)
 
         def warm_up(count):
@@ -327,11 +432,12 @@ def tile_cross_layer_transcoder_s8_kernel(
 
             step("T", [], [], run, True)
 
-        def unit_banks(unit, js=range(4)):
+        def unit_banks(unit, js=range(4), on_vector=()):
             for j in js:
                 stage1(unit, j, 0)
                 stage1(unit, j, 1)
-                relu(unit, j)
+                if j not in on_vector:
+                    relu(unit, j)
 
         def first_passes(unit, js=range(4)):
             for j in js:
@@ -352,16 +458,28 @@ def tile_cross_layer_transcoder_s8_kernel(
                 a_turn((G, g), h)
                 a_out((G, g), h)
 
+        def x2_run(g):
+            for q in range(2):
+                for u in range(2):
+                    x2_turn(g, u, q)
+                    x2_out(g, u, q)
+
+        def c_run(G):
+            for t in range(4):
+                c_turn(G, t)
+                c_out(G, t)
+
         def c_group(G, blocks=range(4)):
             for b in blocks:
                 c_block(G, b)
+                c_store(G, b)
 
         load_x(0, 0, 0, 1); load_rows([0], e1, 0); load_x(0, 0, 1, 1); load_rows([0], e1, 1); load_x(0, 0, 2, 2)
         load_x(0, 1, 0, 2); load_rows([1], e1, 0, W); load_x(0, 1, 2, 2); load_rows([1], e1, 1, W)
         load_rows([2], e1, 0, 2 * W); load_rows([2], e1, 1, 2 * W)
-        load_rows([3], e2, 0); load_x(1, 0, 0, 2); load_x(1, 0, 2, 2); load_rows([3], e2, 1); load_rows([4], e2, 0, W); load_rows([4], e2, 1, W)
+        load_rows([3, 4], e2, 0); load_x(1, 0, 0, 2); load_x(1, 0, 2, 2); load_rows([3, 4], e2, 1); load_labels()
         load_x(1, 1, 0, 2); load_x(1, 1, 2, 2)
-        load_rows(["d2"], d2, 0); load_rows(["d2"], d2, 1); load_labels(); load_d1()
+        load_d2(0); load_d2(1); load_d1()
         x_turn((0, 0, 0), False); warm_up(2)
         mix((0, 0), "S", 336, W); x_out((0, 0, 0))
         x_run(0, 0, [1]); warm_up(2)
@@ -376,43 +494,40 @@ def tile_cross_layer_transcoder_s8_kernel(
         relu((0, 0), 3)
         unit_banks((0, 1), [0, 1])
         first_passes((1, 0))
-        mix((2, 0), "S", 384, W)
         unit_banks((0, 1), [2, 3])
         second_passes((1, 0))
         unit_banks((1, 1))
-        x_run(1, 0, range(4))
-        unit_banks((2, 0)); unit_banks((2, 1)); unit_banks((3, 0))
-        x_run(1, 1, range(4))
+        x2_run(0)
+        unit_banks((2, 0)); unit_banks((2, 1)); unit_banks((3, 0), on_vector=[3])
+        x2_run(1)
         unit_banks((4, 0))
-        a_run(0, [(G, h) for h in range(2) for G in range(GROUPS)])
+        a_run(0, [(G, h) for h in range(2) for G in range(3)])
         unit_banks((3, 1)); unit_banks((4, 1))
         y_tile(0, 0); y_tile(0, 1)
-        a_run(1, [(G, 0) for G in range(GROUPS)])
-        y_tile(0, 2); c_group(0)
-        a_mix((2, 1), "S", 384, W)
-        y_tile(0, 3)
-        a_run(1, [(G, 1) for G in range(GROUPS)])
-        c_group(1); y_tile(1, 0); c_group(2)
-        a_mix((4, 1), "S", 384, W)
-        y_tile(1, 1)
-        c_group(3); c_group(4, [0, 1]); y_tile(1, 2); c_group(4, [2, 3]); y_tile(1, 3, "S", 0, 256)
+        c_run(3); c_run(4)
+        y_tile(0, 2); y_tile(0, 3)
+        c_group(3); c_group(4)
+        a_run(1, [(G, h) for h in range(2) for G in range(3)])
+        c_group(0); y_tile(1, 0); c_group(1); y_tile(1, 1); c_group(2); y_tile(1, 2); y_tile(1, 3, "S", 0, 256)
         mix((0, 0), "V", 0, 336); quant([(0, 0)]); x_quant(0, 0, 0, 1); mix((0, 1), "V", 0, 384); x_quant(0, 0, 1, 1); quant([(0, 1)])
         x_sort((0, 1, 0)); x_sort((0, 1, 1)); x_quant(0, 0, 2, 1); x_quant(0, 0, 3, 1); mix((1, 0))
         x_quant(0, 1, 0, 1); x_quant(0, 1, 1, 1); quant([(1, 0)]); mix((1, 1)); x_quant(0, 1, 2, 1); x_quant(0, 1, 3, 1); quant([(1, 1)])
-        mix((2, 0), "V", 0, 384); mix((2, 1)); mix((3, 0)); quant([(2, 0), (2, 1)]); mix((3, 1)); mix((4, 0), "V", 0, 128); quant([(3, 0), (3, 1)])
-        mix((4, 0), "V", 128, W); x_quant(1, 0, 0, 2); x_quant(1, 0, 2, 2); mix((4, 1)); mix(("d2", 0)); quant([(4, 0), (4, 1)]); mix(("d2", 1))
-        for j in range(4):
+        mix((2, 0)); mix((2, 1)); mix((3, 0)); quant([(2, 0), (2, 1)]); mix((4, 0)); quant([(3, 0)]); quant([(4, 0)])
+        mix((3, 1)); x2_quant(0, 0); quant([(3, 1)], 0, 256); x2_quant(0, 1); quant([(3, 1)], 256, W); mix((4, 1)); widen(0, 0); quant([(4, 1)])
+        for j in range(1, 4):
             widen(0, j)
-        quant([("d2", 0), ("d2", 1)])
+        relu((3, 0), 3, "V")
+        mix(("d2", 0))
         for j in range(4):
             widen(1, j)
-        x_quant(1, 1, 0, 2); mix(("lab", 0)); x_quant(1, 1, 2, 2); mix(("lab", 1))
-        a_mix((0, 0)); y_quant(0, 0, 0, 4); y_quant(0, 0, 4, 5); quant([("lab", 0), ("lab", 1)]); a_mix((0, 1)); y_quant(0, 1, 0, 4); y_quant(0, 1, 4, 5)
-        quant([("c", 0, 0), ("c", 0, 1)]); a_mix((1, 0)); a_mix((1, 1)); a_mix((2, 0)); quant([("c", 1, 0), ("c", 1, 1)])
-        a_mix((2, 1), "V", 0, 384); y_quant(1, 0, 0, 4); y_quant(1, 0, 4, 5); a_mix((3, 0))
-        quant([("c", 2, 0), ("c", 2, 1)]); a_mix((3, 1)); a_mix((4, 0), "V", 0, 256); quant([("c", 3, 0), ("c", 3, 1)])
-        a_mix((4, 1), "V", 0, 256); y_quant(1, 1, 0, 4); quant([("c", 4, 0)], 0, 256); quant([("c", 4, 1)], 0, 256); y_quant(1, 1, 4, 5)
-        a_mix((4, 0), "V", 256, W); a_mix((4, 1), "V", 256, 384); quant([("c", 4, 0)], 256, W); quant([("c", 4, 1)], 256, W)
+        mix(("d2", 1)); x2_quant(1, 0); x2_quant(1, 1)
+        y_mix((3, 0), 0); y_mix((4, 0), 0); quant([("d2", 0), ("d2", 1)]); y_quant(0, 0, 0, 8); y_quant(0, 0, 8, 10); mix(("lab", 0))
+        y_mix((3, 0), 1); y_mix((4, 0), 1); mix(("lab", 1)); y_quant(0, 1, 0, 8); y_quant(0, 1, 8, 10)
+        quant([("lab", 0), ("lab", 1)]); y_mix((3, 1), 0); c_quant(3, 0, 2); y_mix((4, 1), 0); c_quant(3, 2, 4); c_quant(4, 0, 2); a_mix((0, 0)); c_quant(4, 2, 4); a_mix((0, 1)); a_mix((1, 0), "V", 0, 128)
+        quant([("c", 0, 0), ("c", 0, 1)]); a_mix((1, 0), "V", 128, W); a_mix((1, 1)); y_quant(1, 0, 0, 4); y_quant(1, 0, 4, 8); y_quant(1, 0, 8, 10); quant([("c", 1, 0), ("c", 1, 1)]); a_mix((2, 0), "V", 0, 256)
+        a_mix((2, 1), "V", 0, 256); quant([("c", 2, 0)], 0, 256); a_mix((2, 0), "V", 256, W); quant([("c", 2, 1)], 0, 256); a_mix((2, 1), "V", 256, W); quant([("c", 2, 0)], 256, W)
+        y_quant(1, 1, 0, 4); quant([("c", 2, 1)], 256, W); y_quant(1, 1, 4, 6); y_mix((3, 1), 1); y_mix((4, 1), 1, "V", 0, P); y_quant(1, 1, 6, 8)
+        y_mix((4, 1), 1, "V", P, 256); y_quant(1, 1, 8, 9); y_quant(1, 1, 9, 10)
         y_tile(1, 3, "V", 256, N)
 
 

@@ -77,7 +77,7 @@ def tile_cross_layer_transcoder_s8_kernel(
 
         def load_d2(q):
             raw = tile(("rows", "d2", q), [P, 4, W], BF16, "rows", 4)
-            src = d2.rearrange("(q b t i) n -> q t b i n", b=16, t=4, i=8)[q]
+            src = d2.rearrange("(q n t i) c -> q t n i c", n=64, t=4, i=2)[q]
             for t in range(4):
                 nc.sync.dma_start(out=raw[:, t, :], in_=src[t])
             rows["d2", q] = raw[:]
@@ -203,14 +203,12 @@ def tile_cross_layer_transcoder_s8_kernel(
         def mix(key, engine="V", lo=0, hi=W):
             def run():
                 if key[0] in (3, 4):
-                    dst = mixed(key).rearrange("p (t b h i j) -> p t b h j i", t=4, h=4, i=2, j=4)
-                    src = rows[key].rearrange("p j (b t h i) -> p t b h j i", t=4, h=4, i=2)
-                    for t in range(lo // P, hi // P):
-                        copies[engine](out=dst[:, t], in_=src[:, t])
+                    dst = mixed(key).rearrange("p (t n i j) -> p n t j i", t=4, i=2, j=4)
+                    src = rows[key].rearrange("p j (n t i) -> p n t j i", t=4, i=2)
                 else:
-                    dst = mixed(key).rearrange("p (c i j) -> p c j i", i=2, j=4)
-                    src = rows[key].rearrange("p j (c i) -> p c j i", i=2)
-                    copies[engine](out=dst[:, lo // 2 : hi // 2], in_=src[:, lo // 2 : hi // 2])
+                    dst = mixed(key).rearrange("p (c i j) -> p c j i", i=2, j=4)[:, lo // 2 : hi // 2]
+                    src = rows[key].rearrange("p j (c i) -> p c j i", i=2)[:, lo // 2 : hi // 2]
+                copies[engine](out=dst, in_=src)
 
             parts.setdefault(key, []).append((lo, hi))
             step(engine, [("mixed", key, lo)], [("wide", key[1], j) for j in range(4)] if key[0] == "lab" else [], run)
@@ -334,7 +332,7 @@ def tile_cross_layer_transcoder_s8_kernel(
             step("T", [("c_bank", G, t)], [("a", (G, g), t) for g in range(2)], run, True)
 
         def c_turned(G):
-            return tile(("c_t", G), [P, 4 * W], F32, "mixed", 3)
+            return tile(("c_t", G), [P, 4 * W], F32, "rows", 4)
 
         def c_out(G, t):
             def run():
@@ -398,26 +396,26 @@ def tile_cross_layer_transcoder_s8_kernel(
             if G < 3:
                 dst = out_1[W * G + P * b : W * G + P * (b + 1), :]
             else:
-                dst = out_2.rearrange("(G b t i) r -> G t b i r", b=16, t=4, i=8)[G - 3][b]
+                dst = out_2.rearrange("(G n t i) r -> G t n i r", n=64, t=4, i=2)[G - 3][b]
             store(("c", G, b), dst, "S", R)
 
-        def y_tile(g, j, engine="S", lo=0, hi=N):
+        def y_tile(g, j, engine="S", lo=0, hi=N, order=range(GROUPS)):
             key = ("y", g, j, lo)
 
             def one_pass(G):
                 def run():
-                    bank = take_bank(key) if G == 0 else banks[key][1]
+                    bank = take_bank(key) if G == order[0] else banks[key][1]
                     col = 256 * G + P * (j % 2)
                     if G < 3:
                         rhs = held["d1_w"][:, G, 2 * lo : 2 * hi].bitcast(E2M1X4), d1_sc[:, G, lo:hi]
                     else:
                         rhs = quantised(("d2", G - 3), lo, hi)
-                    mx(bank[:, : hi - lo], operand(("y", g, j // 2), col, col + P), rhs, G == 0, G == GROUPS - 1)
+                    mx(bank[:, : hi - lo], operand(("y", g, j // 2), col, col + P), rhs, G == order[0], G == order[-1])
 
                 needs = [("y_q", G, g, j // 2, j % 2)] + whole(("d2", 0)) + whole(("d2", 1))
-                step("T", [key] if G == GROUPS - 1 else [], needs, run, G == 0)
+                step("T", [key] if G == order[-1] else [], needs, run, G == order[0])
 
-            for G in range(GROUPS):
+            for G in order:
                 one_pass(G)
             dst = out_0.rearrange("(g h c u e) n -> g u h c e n", g=2, h=2, u=2, e=2)[g][j // 2][j % 2][:, :, lo:hi]
             store(key, dst, engine, hi - lo)
@@ -498,7 +496,7 @@ def tile_cross_layer_transcoder_s8_kernel(
         second_passes((1, 0))
         unit_banks((1, 1))
         x2_run(0)
-        unit_banks((2, 0)); unit_banks((2, 1)); unit_banks((3, 0), on_vector=[3])
+        unit_banks((2, 0)); unit_banks((2, 1)); first_passes((3, 0), [0, 1]); second_passes((3, 0), [0, 1]); unit_banks((3, 0), [2, 3], on_vector=[3])
         x2_run(1)
         unit_banks((4, 0))
         a_run(0, [(G, h) for h in range(2) for G in range(3)])
@@ -508,26 +506,27 @@ def tile_cross_layer_transcoder_s8_kernel(
         y_tile(0, 2); y_tile(0, 3)
         c_group(3); c_group(4)
         a_run(1, [(G, h) for h in range(2) for G in range(3)])
-        c_group(0); y_tile(1, 0); c_group(1); y_tile(1, 1); c_group(2); y_tile(1, 2); y_tile(1, 3, "S", 0, 256)
+        c_group(0); y_tile(1, 0, order=(3, 4, 0, 1, 2)); c_group(1); y_tile(1, 1); c_group(2); y_tile(1, 2); y_tile(1, 3, "S", 0, 256)
         mix((0, 0), "V", 0, 336); quant([(0, 0)]); x_quant(0, 0, 0, 1); mix((0, 1), "V", 0, 384); x_quant(0, 0, 1, 1); quant([(0, 1)])
         x_sort((0, 1, 0)); x_sort((0, 1, 1)); x_quant(0, 0, 2, 1); x_quant(0, 0, 3, 1); mix((1, 0))
         x_quant(0, 1, 0, 1); x_quant(0, 1, 1, 1); quant([(1, 0)]); mix((1, 1)); x_quant(0, 1, 2, 1); x_quant(0, 1, 3, 1); quant([(1, 1)])
         mix((2, 0)); mix((2, 1)); mix((3, 0)); quant([(2, 0), (2, 1)]); mix((4, 0)); quant([(3, 0)]); quant([(4, 0)])
-        mix((3, 1)); x2_quant(0, 0); quant([(3, 1)], 0, 256); x2_quant(0, 1); quant([(3, 1)], 256, W); mix((4, 1)); widen(0, 0); quant([(4, 1)])
+        mix((3, 1)); x2_quant(0, 0); x2_quant(0, 1); quant([(3, 1)]); mix((4, 1)); widen(0, 0); quant([(4, 1)])
         for j in range(1, 4):
             widen(0, j)
         relu((3, 0), 3, "V")
         mix(("d2", 0))
         for j in range(4):
             widen(1, j)
-        mix(("d2", 1)); x2_quant(1, 0); x2_quant(1, 1)
+        x2_quant(1, 0); mix(("d2", 1)); x2_quant(1, 1)
         y_mix((3, 0), 0); y_mix((4, 0), 0); quant([("d2", 0), ("d2", 1)]); y_quant(0, 0, 0, 8); y_quant(0, 0, 8, 10); mix(("lab", 0))
         y_mix((3, 0), 1); y_mix((4, 0), 1); mix(("lab", 1)); y_quant(0, 1, 0, 8); y_quant(0, 1, 8, 10)
-        quant([("lab", 0), ("lab", 1)]); y_mix((3, 1), 0); c_quant(3, 0, 2); y_mix((4, 1), 0); c_quant(3, 2, 4); c_quant(4, 0, 2); a_mix((0, 0)); c_quant(4, 2, 4); a_mix((0, 1)); a_mix((1, 0), "V", 0, 128)
-        quant([("c", 0, 0), ("c", 0, 1)]); a_mix((1, 0), "V", 128, W); a_mix((1, 1)); y_quant(1, 0, 0, 4); y_quant(1, 0, 4, 8); y_quant(1, 0, 8, 10); quant([("c", 1, 0), ("c", 1, 1)]); a_mix((2, 0), "V", 0, 256)
-        a_mix((2, 1), "V", 0, 256); quant([("c", 2, 0)], 0, 256); a_mix((2, 0), "V", 256, W); quant([("c", 2, 1)], 0, 256); a_mix((2, 1), "V", 256, W); quant([("c", 2, 0)], 256, W)
-        y_quant(1, 1, 0, 4); quant([("c", 2, 1)], 256, W); y_quant(1, 1, 4, 6); y_mix((3, 1), 1); y_mix((4, 1), 1, "V", 0, P); y_quant(1, 1, 6, 8)
-        y_mix((4, 1), 1, "V", P, 256); y_quant(1, 1, 8, 9); y_quant(1, 1, 9, 10)
+        quant([("lab", 0), ("lab", 1)]); y_mix((3, 1), 0); y_mix((4, 1), 0); c_quant(3, 0, 4); a_mix((0, 0)); c_quant(4, 0, 4); a_mix((0, 1)); y_quant(1, 0, 6, 10)
+        quant([("c", 0, 0), ("c", 0, 1)]); a_mix((1, 0)); a_mix((1, 1)); y_quant(1, 0, 0, 4); y_quant(1, 0, 4, 6); quant([("c", 1, 0), ("c", 1, 1)])
+        a_mix((2, 0), "V", 0, 256)
+        a_mix((2, 1), "V", 0, 256); quant([("c", 2, 0)], 0, 256); a_mix((2, 0), "V", 256, W); quant([("c", 2, 1)], 0, 256); a_mix((2, 1), "V", 256, 512); quant([("c", 2, 0)], 256, W)
+        y_quant(1, 1, 0, 4); quant([("c", 2, 1)], 256, W); y_quant(1, 1, 4, 6); y_mix((3, 1), 1); y_mix((4, 1), 1, "V", 0, P); y_quant(1, 1, 6, 8); y_quant(1, 1, 8, 9)
+        y_mix((4, 1), 1, "V", P, 256); y_quant(1, 1, 9, 10)
         y_tile(1, 3, "V", 256, N)
 
 

from contextlib import ExitStack

import concourse.mybir as mybir
from concourse.masks import make_identity

F32 = mybir.dt.float32
BF16 = mybir.dt.bfloat16
U32 = mybir.dt.uint32
I32 = mybir.dt.int32
U8 = mybir.dt.uint8
E4M3 = mybir.dt.float8_e4m3fn
E4M3X4 = mybir.dt.float8_e4m3fn_x4
E2M1X4 = mybir.dt.float4_e2m1fn_x4
ACT = mybir.ActivationFunctionType
ALU = mybir.AluOpType

T, K, F1, F2, N, R = 1024, 1024, 1536, 1024, 512, 512
P = 128
W = 512
GROUPS = (F1 + F2) // W
BANKS = 8
FLOPS = 2 * (T * K * (F1 + F2) + T * (F1 + F2) * (N + R))


def tile_cross_layer_transcoder_s8_kernel(
    tc, x1, x2, e1, e2, d1_words, d1_scales, d2, labels_bytes, labels_scale, out_0, out_1, out_2
):
    nc = tc.nc
    with ExitStack() as ctx:
        pool = ctx.enter_context(tc.tile_pool(name="work", bufs=1))
        psum = ctx.enter_context(tc.psum_pool(name="psum", bufs=1))
        ctx.enter_context(tc.manual_schedule())

        held = {}

        def tile(key, shape, dtype, tag, bufs=1):
            if key not in held:
                held[key] = pool.tile(shape, dtype, name=tag, tag=tag, bufs=bufs, align_bytes=256)
            return held[key]

        programs = {"S": [], "V": [], "T": []}
        copies = {"S": nc.scalar.copy, "V": nc.vector.tensor_copy}

        def step(engine, makes, needs, function, fills_new_bank=False):
            programs[engine].append((makes, needs, function, fills_new_bank))

        free_banks, banks = list(range(BANKS)), {}

        def take_bank(key):
            number = free_banks.pop(0)
            banks[key] = number, psum.tile([P, W], F32, name="bank", tag="bank%d" % number, bufs=1)
            return banks[key][1]

        def emptied(key):
            free_banks.append(banks[key][0])

        ident = tile("ident", [P, P], F32, "ident")
        make_identity(nc, ident[:])
        d1_sc = tile("d1_sc", [P, 3, N], U8, "d1_sc")
        nc.gpsimd.memset(d1_sc[:].rearrange("p g n -> p (g n)").bitcast(I32), 0)

        rows = {}

        def x_raw(s, g, j, count=1):
            return tile(("x_raw", s, g, j // 2), [P, 2 * K], BF16, "x_raw", 4)[:, K * (j % 2) : K * (j % 2 + count)]

        def load_x(s, g, j, count):
            src = (x1, x2)[s].rearrange("(g p j) k -> g p (j k)", p=P, j=4)[g]
            nc.sync.dma_start(out=x_raw(s, g, j, count), in_=src[:, K * j : K * (j + count)])

        def load_rows(names, src, q, col=0):
            raw = tile(("rows", names[0], q), [P, 4, W * len(names)], BF16, "rows", 4)
            src = src.rearrange("(q p j) c -> q p j c", p=P, j=4)[q]
            nc.sync.dma_start(out=raw[:], in_=src[:, :, col : col + W * len(names)])
            for i, name in enumerate(names):
                rows[name, q] = raw[:, :, W * i : W * (i + 1)]

        def load_d2(q):
            raw = tile(("rows", "d2", q), [P, 4, W], BF16, "rows", 4)
            src = d2.rearrange("(q n t i) c -> q t n i c", n=64, t=4, i=2)[q]
            for t in range(4):
                nc.sync.dma_start(out=raw[:, t, :], in_=src[t])
            rows["d2", q] = raw[:]

        def load_labels():
            scale = tile("lab_sc", [P, 2, 4], F32, "lab_sc")
            nc.sync.dma_start(out=scale[:], in_=labels_scale.rearrange("(g p j) o -> p g (j o)", p=P, j=4))
            for g in range(2):
                raw = tile(("lab_raw", g), [P, 4 * R], U8, "lab_raw", 2)
                nc.sync.dma_start(out=raw[:], in_=labels_bytes.rearrange("(g p j) r -> g p (j r)", p=P, j=4)[g])

        def load_d1():
            words = tile("d1_w", [P, 3, 2 * N], U8, "d1_w")
            nc.sync.dma_start(out=words[:], in_=d1_words.rearrange("g p c -> p g c"))
            src = d1_scales.bitcast(I32)
            dst = d1_sc[:].rearrange("p g n -> p (g n)").bitcast(I32).rearrange("p (g n) -> p g n", g=3)
            for Q in range(4):
                nc.sync.dma_start(
                    out=dst[32 * Q : 32 * Q + 4, :, :], in_=src[:, 4 * Q : 4 * Q + 4, :].rearrange("g r n -> r g n")
                )

        def quantise(key, tag, bufs, columns, values, lo, hi):
            codes = tile(("codes", key), [P, columns], U32, tag + "_c", bufs)
            scales = tile(("scales", key), [P, columns], U8, tag + "_s", bufs)
            nc.vector.quantize_mx(out=codes[:, lo:hi].bitcast(E4M3X4), scales=scales[:, lo:hi], in_=values)

        def operand(key, lo, hi):
            return held["codes", key][:, lo:hi].bitcast(E4M3X4), held["scales", key][:, lo:hi]

        def mx(out, stationary, moving, first, final):
            nc.tensor.matmul_mx(
                out=out,
                lhsT=stationary[0],
                lhsT_scale=stationary[1],
                rhs=moving[0],
                rhs_scale=moving[1],
                start=first,
                stop=final,
            )

        def x_sort(x):
            def run():
                nc.vector.tensor_copy(
                    out=tile(("x_w", x), [P, W], F32, "x_w", 2)[:].rearrange("p (q u m) -> p q u m", q=2, u=2),
                    in_=x_raw(*x).bitcast(F32).rearrange("p (q m u) -> p q u m", q=2, u=2),
                )

            step("V", [("x_sorted", x)], [], run)

        def x_turn(x, is_sorted):
            def run():
                bank = take_bank(x)
                words = x_raw(*x).bitcast(F32)
                for q in range(2):
                    for u in range(2):
                        col = P * (2 * q + u)
                        src = held["x_w", x][:, col : col + P] if is_sorted else words[:, 256 * q + u : 256 * (q + 1) : 2]
                        nc.tensor.transpose(bank[:, col : col + P], src, ident[:])

            step("T", [("x_bank", x)], [("x_sorted", x)] if is_sorted else [], run, True)

        def x_turned(s, g, j, count=1):
            return tile(("x_t", s, g, j // 2), [P, 2 * W], F32, "x_t", 3)[:, W * (j % 2) : W * (j % 2 + count)]

        def x_out(x, engine="S"):
            def run():
                copies[engine](
                    out=x_turned(*x).rearrange("p (q t u) -> p q t u", q=2, u=2),
                    in_=banks[x][1][:].rearrange("p (q u t) -> p q t u", q=2, u=2),
                )
                emptied(x)

            step(engine, [("x_t", x)], [("x_bank", x)], run)

        def x_quant(s, g, j, count):
            def run():
                lo = 256 * (j % 2)
                values = x_turned(s, g, j, count).bitcast(BF16)
                quantise(("x", s, g, j // 2), "x", 4, W, values, lo, lo + 256 * count)

            xs = [(s, g, j + i) for i in range(count)]
            step("V", [("x_q", x) for x in xs], [("x_t", x) for x in xs], run)

        def x2_turn(g, u, q):
            def run():
                bank = take_bank(("x2", g, u, q))
                for e in range(2):
                    words = x_raw(1, g, 2 * u + e).bitcast(F32)
                    for v in range(2):
                        col = P * (2 * e + v)
                        nc.tensor.transpose(bank[:, col : col + P], words[:, 256 * q + v : 256 * (q + 1) : 2], ident[:])

            step("T", [("x2_bank", g, u, q)], [], run, True)

        def x2_turned(g, q):
            return tile(("x2_t", g, q), [P, 2 * W], F32, "x_t", 3)

        def x2_out(g, u, q):
            def run():
                nc.scalar.copy(
                    out=x2_turned(g, q)[:, W * u : W * (u + 1)].rearrange("p (c i) -> p c i", i=4),
                    in_=banks["x2", g, u, q][1][:].rearrange("p (i c) -> p c i", i=4),
                )
                emptied(("x2", g, u, q))

            step("S", [("x2_t", g, u, q)], [("x2_bank", g, u, q)], run)

        def x2_quant(g, q):
            def run():
                quantise(("x2", g), "x2", 2, 2 * W, x2_turned(g, q)[:].bitcast(BF16), W * q, W * (q + 1))

            step("V", [("x2_q", g, q)], [("x2_t", g, u, q) for u in range(2)], run)

        pairs = [((name, 0), (name, 1)) for name in list(range(GROUPS)) + ["d2", "lab"]]
        pairs = pairs + [(("c", G, 0), ("c", G, 1)) for G in range(3)]
        place = {key: (pair, i) for pair in pairs for i, key in enumerate(pair)}
        parts = {}

        def mixed(key, count=1):
            pair, i = place[key]
            return tile(("mixed", pair), [P, 8 * W], BF16, "mixed", 3)[:, 4 * W * i : 4 * W * (i + count)]

        def mix(key, engine="V", lo=0, hi=W):
            def run():
                if key[0] in (3, 4):
                    dst = mixed(key).rearrange("p (t n i j) -> p n t j i", t=4, i=2, j=4)
                    src = rows[key].rearrange("p j (n t i) -> p n t j i", t=4, i=2)
                else:
                    dst = mixed(key).rearrange("p (c i j) -> p c j i", i=2, j=4)[:, lo // 2 : hi // 2]
                    src = rows[key].rearrange("p j (c i) -> p c j i", i=2)[:, lo // 2 : hi // 2]
                copies[engine](out=dst, in_=src)

            parts.setdefault(key, []).append((lo, hi))
            step(engine, [("mixed", key, lo)], [("wide", key[1], j) for j in range(4)] if key[0] == "lab" else [], run)

        def quant(keys, lo=0, hi=W):
            pair, i = place[keys[0]]
            tag, bufs = ("w", 2) if keys[0][0] in ("d2", "lab") else ("e", 3)
            end = hi + W * (len(keys) - 1)

            def run():
                values = mixed(keys[0], len(keys))[:, 4 * lo : 4 * end]
                quantise(pair, tag, bufs, 2 * W, values, W * i + lo, W * i + end)

            makes = [("q", key, b) for key in keys for b in range(lo // P, hi // P)]
            needs = [("mixed", key, a) for key in keys for a, b in parts[key] if a < hi and lo < b]
            step("V", makes, needs, run)

        def quantised(key, lo=0, hi=W):
            pair, i = place[key]
            return operand(pair, W * i + lo, W * i + hi)

        def whole(key):
            return [("q", key, b) for b in range(4)]

        def widen(g, j):
            def run():
                wide = tile(("wide", g), [P, 4, R], BF16, "rows", 4)
                rows["lab", g] = wide[:]
                src = held["lab_raw", g][:, j * R : (j + 1) * R].bitcast(E4M3)
                scale = held["lab_sc"][:, g, j : j + 1]
                nc.vector.tensor_scalar(out=wide[:, j, :], in0=src, scalar1=scale, scalar2=None, op0=ALU.mult)

            step("V", [("wide", g, j)], [], run)

        def features(unit):
            return tile(("a", unit), [P, 4, W], BF16, "a", 2 * GROUPS)

        def stage1(unit, j, q):
            G, g = unit

            def run():
                bank = take_bank((unit, j)) if q == 0 else banks[unit, j][1]
                if G < 3:
                    lo = 256 * (j % 2) + P * q
                    mx(bank[:], operand(("x", 0, g, j // 2), lo, lo + P), quantised((G, q)), q == 0, q == 1)
                else:
                    moving = operand(("x2", g), W * q, W * (q + 1))
                    mx(bank[:], quantised((G, q), P * j, P * (j + 1)), moving, q == 0, q == 1)

            needs = [("x_q", (0, g, j))] + whole((G, q)) if G < 3 else [("x2_q", g, q), ("q", (G, q), j)]
            step("T", [("s1", unit, j, q)], needs, run, q == 0)

        def relu(unit, j, engine="S"):
            def run():
                dst, src = features(unit)[:, j, :], banks[unit, j][1][:]
                if unit[0] < 3:
                    dst = dst.rearrange("p (u m e) -> p u m e", u=2, e=2)
                    src = src.rearrange("p (m u e) -> p u m e", u=2, e=2)
                if engine == "S":
                    nc.scalar.activation(out=dst, in_=src, func=ACT.Relu)
                else:
                    nc.vector.tensor_scalar(out=dst, in0=src, scalar1=0.0, scalar2=None, op0=ALU.max)
                emptied((unit, j))

            step(engine, [("a", unit, j)], [("s1", unit, j, 1)], run)

        def a_turn(unit, h):
            def run():
                words = features(unit)[:].rearrange("p j f -> p (j f)").bitcast(F32)
                bank = take_bank(("a", unit, h))
                for i in range(4):
                    col = W * h + P * i
                    nc.tensor.transpose(bank[:, i * P : (i + 1) * P], words[:, col : col + P], ident[:])

            step("T", [("a_bank", unit, h)], [("a", unit, 2 * h), ("a", unit, 2 * h + 1)], run, True)

        def a_turned(g, h):
            return tile(("a_t", g, h), [P, GROUPS * W], F32, "a_t", 2)

        def a_out(unit, h, engine="S"):
            G, g = unit

            def run():
                copies[engine](
                    out=a_turned(g, h)[:, W * G : W * (G + 1)].rearrange("p (c i) -> p c i", i=4),
                    in_=banks["a", unit, h][1][:].rearrange("p (i c) -> p c i", i=4),
                )
                emptied(("a", unit, h))

            step(engine, [("a_t", unit, h, i) for i in range(2)], [("a_bank", unit, h)], run)

        def y_quant(g, h, lo, hi):
            def run():
                values = a_turned(g, h)[:, 256 * lo : 256 * hi].bitcast(BF16)
                quantise(("y", g, h), "a_y", 4, GROUPS * 256, values, P * lo, P * hi)

            pieces = [divmod(n, 2) for n in range(lo, hi)]
            step("V", [("y_q", G, g, h, i) for G, i in pieces], [("a_t", (G, g), h, i) for G, i in pieces], run)

        def y_mix(unit, h, engine="V", lo=0, hi=256):
            G, g = unit

            def run():
                dst = a_turned(g, h)[:, W * G : W * (G + 1)].bitcast(BF16)[:, 4 * lo : 4 * hi]
                src = features(unit)[:, :, 256 * h + lo : 256 * h + hi]
                copies[engine](
                    out=dst.rearrange("p (c e t) -> p c t e", e=2, t=4), in_=src.rearrange("p t (c e) -> p c t e", e=2)
                )

            step(engine, [("a_t", unit, h, i) for i in range(lo // P, hi // P)], [("a", unit, t) for t in range(4)], run)

        def c_turn(G, t):
            def run():
                bank = take_bank(("c_bank", G, t))
                for g in range(2):
                    words = features((G, g))[:, t, :].bitcast(F32)
                    for u in range(2):
                        col = P * (2 * g + u)
                        nc.tensor.transpose(bank[:, col : col + P], words[:, P * u : P * (u + 1)], ident[:])

            step("T", [("c_bank", G, t)], [("a", (G, g), t) for g in range(2)], run, True)

        def c_turned(G):
            return tile(("c_t", G), [P, 4 * W], F32, "rows", 4)

        def c_out(G, t):
            def run():
                nc.scalar.copy(
                    out=c_turned(G)[:, W * t : W * (t + 1)].rearrange("p (g m u) -> p g m u", g=2, u=2),
                    in_=banks["c_bank", G, t][1][:].rearrange("p (g u m) -> p g m u", g=2, u=2),
                )
                emptied(("c_bank", G, t))

            step("S", [("c_t", G, t)], [("c_bank", G, t)], run)

        def c_quant(G, lo, hi):
            def run():
                values = c_turned(G)[:, W * lo : W * hi].bitcast(BF16)
                quantise(("c", G), "e", 3, 2 * W, values, 256 * lo, 256 * hi)

            step("V", [("c_q", G, t) for t in range(lo, hi)], [("c_t", G, t) for t in range(lo, hi)], run)

        def a_mix(unit, engine="V", lo=0, hi=W):
            key = ("c",) + unit

            def run():
                quads = slice(lo // 4, hi // 4)
                copies[engine](
                    out=mixed(key).rearrange("p (m u e j) -> p u m j e", u=2, e=2, j=4)[:, :, quads],
                    in_=features(unit)[:].rearrange("p j (u m e) -> p u m j e", u=2, e=2)[:, :, quads],
                )

            parts.setdefault(key, []).append((lo, hi))
            step(engine, [("mixed", key, lo)], [("a", unit, j) for j in range(4)], run)

        stored = []
        staging = [("x_raw", 4, 2, 0), ("x_t", 3, 2, 8), ("rows", 4, 4, 14)]

        def store(key, dst, engine, width):
            def run():
                tag, bufs, count, first = [place for place in staging if place[3] <= len(stored)][-1]
                buffer, i = divmod(len(stored) - first, count)
                stored.append(key)
                staged = tile(("staged", tag, buffer), [P, count * W], F32, tag, bufs)[:, W * i : W * i + width]
                copies[engine](out=staged, in_=banks[key][1][:, :width])
                emptied(key)
                nc.sync.dma_start(out=dst, in_=staged)

            step(engine, [("stored", key)], [key], run)

        def c_block(G, b):
            key = ("c", G, b)

            def run():
                bank = take_bank(key)
                for g in range(2):
                    col = 256 * b + P * g
                    lhs = quantised(("c", G, g), P * b, P * (b + 1)) if G < 3 else operand(("c", G), col, col + P)
                    mx(bank[:], lhs, quantised(("lab", g)), g == 0, g == 1)

            needs = [("q", ("c", G, g), b) for g in range(2)] if G < 3 else [("c_q", G, b)]
            step("T", [key], needs + whole(("lab", 0)) + whole(("lab", 1)), run, True)

        def c_store(G, b):
            if G < 3:
                dst = out_1[W * G + P * b : W * G + P * (b + 1), :]
            else:
                dst = out_2.rearrange("(G n t i) r -> G t n i r", n=64, t=4, i=2)[G - 3][b]
            store(("c", G, b), dst, "S", R)

        def y_tile(g, j, engine="S", lo=0, hi=N, order=range(GROUPS)):
            key = ("y", g, j, lo)

            def one_pass(G):
                def run():
                    bank = take_bank(key) if G == order[0] else banks[key][1]
                    col = 256 * G + P * (j % 2)
                    if G < 3:
                        rhs = held["d1_w"][:, G, 2 * lo : 2 * hi].bitcast(E2M1X4), d1_sc[:, G, lo:hi]
                    else:
                        rhs = quantised(("d2", G - 3), lo, hi)
                    mx(bank[:, : hi - lo], operand(("y", g, j // 2), col, col + P), rhs, G == order[0], G == order[-1])

                needs = [("y_q", G, g, j // 2, j % 2)] + whole(("d2", 0)) + whole(("d2", 1))
                step("T", [key] if G == order[-1] else [], needs, run, G == order[0])

            for G in order:
                one_pass(G)
            dst = out_0.rearrange("(g h c u e) n -> g u h c e n", g=2, h=2, u=2, e=2)[g][j // 2][j % 2][:, :, lo:hi]
            store(key, dst, engine, hi - lo)

        def warm_up(count):
            def run():
                first = x_raw(0, 0, 0)
                bank = take_bank("unread")
                for i in range(count):
                    nc.tensor.matmul(bank[:], lhsT=first[:, :P], rhs=first[:, :W], start=True, stop=True)
                emptied("unread")

            step("T", [], [], run, True)

        def unit_banks(unit, js=range(4), on_vector=()):
            for j in js:
                stage1(unit, j, 0)
                stage1(unit, j, 1)
                if j not in on_vector:
                    relu(unit, j)

        def first_passes(unit, js=range(4)):
            for j in js:
                stage1(unit, j, 0)

        def second_passes(unit, js=range(4)):
            for j in js:
                stage1(unit, j, 1)
                relu(unit, j)

        def x_run(s, g, js, are_sorted=()):
            for j in js:
                x_turn((s, g, j), j in are_sorted)
                x_out((s, g, j))

        def a_run(g, halves):
            for G, h in halves:
                a_turn((G, g), h)
                a_out((G, g), h)

        def x2_run(g):
            for q in range(2):
                for u in range(2):
                    x2_turn(g, u, q)
                    x2_out(g, u, q)

        def c_run(G):
            for t in range(4):
                c_turn(G, t)
                c_out(G, t)

        def c_group(G, blocks=range(4)):
            for b in blocks:
                c_block(G, b)
                c_store(G, b)

        load_x(0, 0, 0, 1); load_rows([0], e1, 0); load_x(0, 0, 1, 1); load_rows([0], e1, 1); load_x(0, 0, 2, 2)
        load_x(0, 1, 0, 2); load_rows([1], e1, 0, W); load_x(0, 1, 2, 2); load_rows([1], e1, 1, W)
        load_rows([2], e1, 0, 2 * W); load_rows([2], e1, 1, 2 * W)
        load_rows([3, 4], e2, 0); load_x(1, 0, 0, 2); load_x(1, 0, 2, 2); load_rows([3, 4], e2, 1); load_labels()
        load_x(1, 1, 0, 2); load_x(1, 1, 2, 2)
        load_d2(0); load_d2(1); load_d1()
        x_turn((0, 0, 0), False); warm_up(2)
        mix((0, 0), "S", 336, W); x_out((0, 0, 0))
        x_run(0, 0, [1]); warm_up(2)
        mix((0, 1), "S", 384, W)
        first_passes((0, 0), [0])
        x_run(0, 0, [2, 3])
        first_passes((0, 0), [1]); second_passes((0, 0), [0]); stage1((0, 0), 1, 1)
        x_run(0, 1, [0, 1], [0, 1])
        relu((0, 0), 1)
        unit_banks((0, 0), [2]); stage1((0, 0), 3, 0); stage1((0, 0), 3, 1)
        x_run(0, 1, [2, 3])
        relu((0, 0), 3)
        unit_banks((0, 1), [0, 1])
        first_passes((1, 0))
        unit_banks((0, 1), [2, 3])
        second_passes((1, 0))
        unit_banks((1, 1))
        x2_run(0)
        unit_banks((2, 0)); unit_banks((2, 1)); first_passes((3, 0), [0, 1]); second_passes((3, 0), [0, 1]); unit_banks((3, 0), [2, 3], on_vector=[3])
        x2_run(1)
        unit_banks((4, 0))
        a_run(0, [(G, h) for h in range(2) for G in range(3)])
        unit_banks((3, 1)); unit_banks((4, 1))
        y_tile(0, 0); y_tile(0, 1)
        c_run(3); c_run(4)
        y_tile(0, 2); y_tile(0, 3)
        c_group(3); c_group(4)
        a_run(1, [(G, h) for h in range(2) for G in range(3)])
        c_group(0); y_tile(1, 0, order=(3, 4, 0, 1, 2)); c_group(1); y_tile(1, 1); c_group(2); y_tile(1, 2); y_tile(1, 3, "S", 0, 256)
        mix((0, 0), "V", 0, 336); quant([(0, 0)]); x_quant(0, 0, 0, 1); mix((0, 1), "V", 0, 384); x_quant(0, 0, 1, 1); quant([(0, 1)])
        x_sort((0, 1, 0)); x_sort((0, 1, 1)); x_quant(0, 0, 2, 1); x_quant(0, 0, 3, 1); mix((1, 0))
        x_quant(0, 1, 0, 1); x_quant(0, 1, 1, 1); quant([(1, 0)]); mix((1, 1)); x_quant(0, 1, 2, 1); x_quant(0, 1, 3, 1); quant([(1, 1)])
        mix((2, 0)); mix((2, 1)); mix((3, 0)); quant([(2, 0), (2, 1)]); mix((4, 0)); quant([(3, 0)]); quant([(4, 0)])
        mix((3, 1)); x2_quant(0, 0); x2_quant(0, 1); quant([(3, 1)]); mix((4, 1)); widen(0, 0); quant([(4, 1)])
        for j in range(1, 4):
            widen(0, j)
        relu((3, 0), 3, "V")
        mix(("d2", 0))
        for j in range(4):
            widen(1, j)
        x2_quant(1, 0); mix(("d2", 1)); x2_quant(1, 1)
        y_mix((3, 0), 0); y_mix((4, 0), 0); quant([("d2", 0), ("d2", 1)]); y_quant(0, 0, 0, 8); y_quant(0, 0, 8, 10); mix(("lab", 0))
        y_mix((3, 0), 1); y_mix((4, 0), 1); mix(("lab", 1)); y_quant(0, 1, 0, 8); y_quant(0, 1, 8, 10)
        quant([("lab", 0), ("lab", 1)]); y_mix((3, 1), 0); y_mix((4, 1), 0); c_quant(3, 0, 4); a_mix((0, 0)); c_quant(4, 0, 4); a_mix((0, 1)); y_quant(1, 0, 6, 10)
        quant([("c", 0, 0), ("c", 0, 1)]); a_mix((1, 0)); a_mix((1, 1)); y_quant(1, 0, 0, 4); y_quant(1, 0, 4, 6); quant([("c", 1, 0), ("c", 1, 1)])
        a_mix((2, 0), "V", 0, 256)
        a_mix((2, 1), "V", 0, 256); quant([("c", 2, 0)], 0, 256); a_mix((2, 0), "V", 256, W); quant([("c", 2, 1)], 0, 256); a_mix((2, 1), "V", 256, 512); quant([("c", 2, 0)], 256, W)
        y_quant(1, 1, 0, 4); quant([("c", 2, 1)], 256, W); y_quant(1, 1, 4, 6); y_mix((3, 1), 1); y_mix((4, 1), 1, "V", 0, P); y_quant(1, 1, 6, 8); y_quant(1, 1, 8, 9)
        y_mix((4, 1), 1, "V", P, 256); y_quant(1, 1, 9, 10)
        y_tile(1, 3, "V", 256, N)


        made = set()
        while any(programs.values()):
            ready = [
                queue
                for queue in programs.values()
                if queue and all(n in made for n in queue[0][1]) and (free_banks or not queue[0][3])
            ]
            makes, needs, function, fills_new_bank = ready[0].pop(0)
            function()
            made = made | set(makes)
